import numpy as np, ml_dtypes
CORES = [51,54,179,182]
N = 4
BF = ml_dtypes.bfloat16
W, C, TS, S = 2048, 256, 5, 1
B = W // C
SHAPES = np.array([[0, 15, 1, 2, 3, 4, 5, 6, 7, 8, 9, 10, 11, 12, 13, 14], [0, 1, 2, 15, 3, 14, 4, 13, 5, 12, 6, 11, 7, 10, 8, 9], [14, 15, 0, 13, 1, 12, 2, 11, 3, 10, 4, 9, 5, 8, 6, 7],
                   [1, 14, 0, 15, 2, 3, 4, 5, 6, 7, 8, 9, 10, 11, 12, 13], [7, 8, 0, 15, 1, 14, 2, 13, 3, 12, 4, 11, 5, 10, 6, 9], [3, 11, 0, 8, 1, 9, 2, 10, 4, 12, 5, 13, 6, 14, 7, 15],
                   [0, 2, 1, 3, 4, 15, 5, 14, 6, 13, 7, 12, 8, 11, 9, 10]])
def place(a, b, n):
    return ((a * b >> 5) + 37 * a + 11 * b + (n & 63)) & (W - 1)
def mate(o):
    p = np.zeros_like(o); np.put_along_axis(p, o, o[..., np.array([0, 1, 3, 2, 5, 4, 7, 6, 9, 8, 11, 10, 13, 12, 15, 14])], -1)
    return np.ascontiguousarray(np.moveaxis(p, -1, -2))
def loose(p):
    m = p == np.arange(16).reshape(1, 1, 16, 1)
    return np.argmax(m, axis=2), 15 - np.argmax(m[:, :, ::-1], axis=2)
def look(x, l, p, fr, z, a):
    lf = np.take_along_axis(l, fr[:, :, None, :], 2); lp = np.take_along_axis(l, p, 2); n = a[:, :, None, None]
    xk = np.take_along_axis(x, place(l, lp, n).reshape(N, 8, 1, 16 * C), 3).reshape(N, 8, 16, 16, C)
    yk = np.take_along_axis(x, place(lf, l, n).reshape(N, 8, 1, 16 * C), 3).reshape(N, 8, 16, 16, C)
    dx = np.sum(np.abs(xk - z[:, :, :, None, :]), axis=2); dy = np.sum(np.abs(yk - z[:, :, :, None, :]), axis=2)
    return xk, yk, dx, dx - dy
def parts(rng):
    x = rng.integers(0, 64, (N, 8, 16, W)); l = rng.integers(0, 4096, (N, 8, 16, C)); z = rng.integers(0, 64, (N, 8, 16, C))
    p = mate(np.argsort(rng.random((N, 8, C, 16)), axis=-1)); t = rng.integers(60, 241, (N, 8, TS))
    return x, l, p, z, t
def pack(x, l, p, z, t):
    return {"xt": np.ascontiguousarray(x.reshape(N, 128, W)).astype(np.float32).astype(BF), "nm": np.ascontiguousarray(l.reshape(N, 128, C)).astype(np.int32),
            "pr": np.ascontiguousarray(p.reshape(N, 128, C)).astype(np.int32), "z0": np.ascontiguousarray(z.reshape(N, 128, C)).astype(np.float32).astype(BF),
            "th": np.ascontiguousarray(np.repeat(t, 16, axis=1)).astype(np.int32)}
def plant(rng, x, l, p, z, used, q, g, i, zz, v, w, odd, last):
    c = rng.integers(0, 4096, (512, 16)); pp = p[q, g, :, i]; bd = np.flatnonzero(pp != np.arange(16)); fr = int(np.flatnonzero(pp == np.arange(16))[0])
    hx = place(c[:, bd], c[:, pp[bd]], 0); hy = place(c[:, fr:fr + 1], c[:, bd], 0); h = np.concatenate([hx, hy], axis=1); k = np.sort(h, axis=1)
    fit = np.all(k[:, 1:] != k[:, :-1], axis=1) & ~np.any(used[h], axis=1); j = int(np.argmax(fit))
    assert fit[j], "no fitting names"
    ax = np.zeros((16, len(bd)), np.int64) + np.reshape(v, (-1, 1)); ax[15, :-1] = odd; ax[15, -1] = last
    xx = x[q, g]; xx[:, hx[j]] = ax; xx[:, hy[j]] = w
    l[q, g, :, i] = c[j]; z[q, g, :, i] = zz; used[h[j]] = True
def setup_inputs(rng):
    return pack(*parts(rng))
def setup_inputs_spread(rng):
    x, l, p, z, t = parts(rng)
    x = (rng.random((N, 8, 16, W)) * np.exp2(rng.integers(0, 7, (N, 8, 1, W)))).astype(np.int64); x = np.where(rng.random((N, 8, 1, W)) < 0.5, 63 - x, x)
    l = np.where(rng.random((N, 8, 1, C)) < 0.5, np.exp2(12 * rng.random((N, 8, 16, C))).astype(np.int64) - 1, l); l = np.minimum(l, 4095)
    z = np.where(rng.random((N, 8, 1, C)) < 0.7, np.minimum(np.exp2(6 * rng.random((N, 8, 16, C))).astype(np.int64) - 1, 63), z)
    t = np.where(rng.random((N, 8, TS)) < 0.4, rng.integers(-1008, 1009, (N, 8, TS)), rng.integers(0, 300, (N, 8, TS)))
    return pack(x, l, p, z, t)
def setup_inputs_ends(rng):
    x, l, p, z, t = parts(rng)
    x = 63 * np.where(rng.random((N, 8, 1, W)) < 0.75, rng.integers(0, 2, (N, 8, 1, W)), rng.integers(0, 2, (N, 8, 16, W)))
    l = np.where(rng.random((N, 8, 16, C)) < 0.75, 4095 * rng.integers(0, 2, (N, 8, 16, C)), l)
    z = 63 * np.where(rng.random((N, 8, 1, C)) < 0.6, rng.integers(0, 2, (N, 8, 1, C)), rng.integers(0, 2, (N, 8, 16, C)))
    sh = rng.integers(0, 6, (N, 8, C)); sh[:, :, np.array([0, C // 2, C - 1])] = 1
    sh[:, :, np.array([1, 2, C - 3])] = 6; sh[1::2, :, C // 2] = 6; p = mate(SHAPES[sh])
    t = 2016 * rng.integers(0, 2, (N, 8, TS)) - 1008; t[:, 0] = 1008; t[:, 1] = -1008
    t[:, 2] = rng.choice(np.array([1007, 0, -1007, 500]), (N, TS)); t[:, 5] = rng.choice(np.array([1007, 0, -1007, 500]), (N, TS))
    t[:, 2, 0] = 1007; t[:, 5, 0] = 1007; t[:, 7, 0] = 1007
    for q in range(N):
        for g in range(8):
            used = np.zeros(W, bool); m = int(rng.integers(9, 16))
            plant(rng, x, l, p, z, used, q, g, C - 1, 63, 0, 63, 1, 0)
            plant(rng, x, l, p, z, used, q, g, C - 2, 0, 0, 63, 0, 0)
            plant(rng, x, l, p, z, used, q, g, 0, 63, 63, 0, 62, 63)
            plant(rng, x, l, p, z, used, q, g, C // 2, 63, 0, 63, 0, 0)
            plant(rng, x, l, p, z, used, q, g, 1, 63, 0, 0, 0, 1)
            plant(rng, x, l, p, z, used, q, g, C - 3, 63, 63, 0, 63, 62)
            plant(rng, x, l, p, z, used, q, g, 2, 63, np.where(np.arange(16) < m, 0, 63), 0, 62, 63)
    return pack(x, l, p, z, t)
def setup_inputs_corners(rng):
    x, l, p, z, t = parts(rng); p = mate(SHAPES[rng.integers(0, 6, (N, 8, C))])
    l[:, 0] = rng.integers(0, 4096, (N, 1, C)); t[:, 0] = rng.integers(-1, 1, (N, TS))
    for q in range(N): l[q, 1] = (0, 4095, 1, 2048, 4094, 77, 1023, 64)[(q + int(rng.integers(0, 8))) % 8]
    l[:, 2] = 4095 * rng.integers(0, 2, (N, 16, C))
    x[:, 3] = rng.integers(0, 64, (N, 16, 1)); t[:, 3] = rng.integers(-1, 1, (N, TS))
    z[:, 4] = 63 * rng.integers(0, 2, (N, 1, C))
    t[:, 7] = 2016 * rng.integers(0, 2, (N, TS)) - 1008
    fr, e = loose(p); s = look(x, l, p, fr, z, np.zeros((N, 8), np.int64))[3]
    best = np.max(np.where(p != np.arange(16).reshape(1, 1, 16, 1), s, -1008), axis=2)
    t[:, 5, 0] = best[:, 5, 0]; t[:, 6, 0] = np.maximum(best[:, 6, C - 1] - 1, -1008)
    return pack(x, l, p, z, t)
def setup_inputs_crowd(rng):
    x, l, p, z, t = parts(rng); x = rng.integers(1, 63, (N, 8, 16, W)); z = rng.integers(1, 63, (N, 8, 16, C))
    l[:, 4] = rng.integers(0, 4096, (N, 1, 1)); l[:, 6] = rng.integers(0, 4096, (N, 1, 1))
    t[:] = 1008; t[:, 1, 0] = 1007; t[:, 5, 0] = 1007
    for g in (2, 3, 6, 7): t[:, g] = -1008
    for q in range(N):
        for g, i in ((1, C - 1), (5, 0)): plant(rng, x, l, p, z, np.zeros(W, bool), q, g, i, 63, 0, 63, 0, 0)
        for g, i in ((3, 0), (7, C - 1)): plant(rng, x, l, p, z, np.zeros(W, bool), q, g, i, 0, 0, 63, 0, 0)
    return pack(x, l, p, z, t)
def check_inputs(d):
    bad = []
    for k, lo, hi in (("xt", 0, 63), ("nm", 0, 4095), ("pr", 0, 15), ("z0", 0, 63), ("th", -1008, 1008)):
        v = np.asarray(d[k]).astype(np.float64)
        if not (np.min(v) >= lo and np.max(v) <= hi): bad.append("range of " + k)
        elif np.any(v != np.floor(v)): bad.append("whole numbers in " + k)
    p = np.clip(np.asarray(d["pr"]).astype(np.int64), 0, 15).reshape(N, 8, 16, C); row = np.arange(16).reshape(1, 1, 16, 1)
    if np.any(np.take_along_axis(p, p, 2) != row): bad.append("pairs in pr")
    if np.any(np.sum(p == row, axis=2) != 2): bad.append("two free rows in pr")
    t = np.asarray(d["th"]).reshape(N, 8, 16, TS)
    if np.any(t != t[:, :, :1]): bad.append("rows of a group alike in th")
    return bad
def reference(xt, nm, pr, z0, th):
    x = xt.astype(np.float32).astype(np.int64).reshape(N, 8, 16, W); l = nm.astype(np.int64).reshape(N, 8, 16, C); p = pr.astype(np.int64).reshape(N, 8, 16, C)
    z = z0.astype(np.float32).astype(np.int64).reshape(N, 8, 16, C); tt = th.astype(np.int64).reshape(N, 8, 16, TS)[:, :, 0]
    row = np.arange(16).reshape(1, 1, 16, 1); fr, e = loose(p); a = np.zeros((N, 8), np.int64); ct = np.zeros((TS, N, 8), np.int64)
    for t in range(TS):
        at = (np.arange(N) + S * t) % N; xa = x[at]
        xk, yk, dx, s = look(xa, l, p, fr, z, a[at]); bonded = p != row
        top = np.where(bonded, s, -9999); k1 = np.argmax(top, axis=2); k2 = np.argmin(np.where(bonded, dx, 9999), axis=2)
        esc = np.max(top, axis=2) <= tt[at][:, :, t:t + 1]
        k = np.where(esc, k2, k1); kk = k[:, :, None, :]; q = np.take_along_axis(p, kk, 2); es = esc[:, :, None, :]
        px = np.take_along_axis(xk, k[:, :, None, None, :], 3)[:, :, :, 0]; py = np.take_along_axis(yk, k[:, :, None, None, :], 3)[:, :, :, 0]
        z = np.where(es, np.abs(z - px), (z + py) >> 1)
        ff = fr[:, :, None, :]; m = np.where(es, e[:, :, None, :], kk)
        p = np.where(row == ff, m, np.where(row == m, ff, p)); p = np.where(row == q, q, p); p = np.where(es & (row == kk), kk, p)
        q = q[:, :, 0]; fr = np.where(esc, k, q); e = np.where(esc, q, e)
        col = (B * np.arange(C) + (np.sum(z, axis=2) & (B - 1)))[:, :, None, :]
        new = (np.take_along_axis(xa, col, 3) + z) >> 1
        np.put_along_axis(xa, np.ascontiguousarray(np.broadcast_to(col, (N, 8, 16, C))), new, 3); x[at] = xa
        ct[t, at] = np.sum(esc, axis=2); a = a + ct[t]
    return {"yx": x.reshape(N, 128, W).astype(np.float32).astype(BF), "ye": np.ascontiguousarray(np.repeat(np.moveaxis(ct, 0, -1), 16, axis=1)).astype(np.float32),
            "yp": p.reshape(N, 128, C).astype(np.float32), "yf": fr.astype(np.float32), "yz": z.reshape(N, 128, C).astype(np.float32).astype(BF)}

@@ -1,0 +1,635 @@
+from concourse.mybir import dt, AluOpType as A, AxisListType, ActivationFunctionType as F
+
+N, TS = 4, 5
+VPEN = 0.0
+WAKE, SHIP = 70.0, 4200.0
+SCRATCH = {
+    "X": ("sbuf", [128, 2112], "bfloat16"), "NM": ("sbuf", [128, 256], "int32"), "PR": ("sbuf", [128, 256], "int32"),
+    "TH": ("sbuf", [128, 5], "int32"), "LL": ("sbuf", [128, 4, 2, 128], "float32"), "NQH": ("sbuf", [128, 256], "float16"),
+    "PT": ("sbuf", [128, 256], "bfloat16"), "MA": ("sbuf", [128, 512], "float32"), "MB": ("sbuf", [128, 2048], "bfloat16"),
+    "FMG": ("sbuf", [128, 256], "bfloat16"), "KC": ("sbuf", [128, 16], "float32"),
+    "OO": ("sbuf", [128, 3, 2, 128], "float32"), "A1": ("sbuf", [128, 3, 2, 128], "float32"),
+    "B1": ("sbuf", [128, 3, 2, 128], "float32"), "SXY": ("sbuf", [128, 3, 2, 2, 128], "float32"),
+    "ONE": ("sbuf", [128, 128], "float32"), "If": ("sbuf", [128, 128], "float32"), "BOa": ("sbuf", [128, 128], "float32"),
+    "BO": ("sbuf", [128, 128], "float32"), "PX": ("sbuf", [128, 2, 64], "float32"), "PM": ("sbuf", [128, 4, 4, 2, 16], "float16"),
+    "II": ("sbuf", [128, 256], "bfloat16"), "nI": ("sbuf", [128, 128], "bfloat16"), "PN": ("sbuf", [128, 128], "bfloat16"),
+    "Ih": ("sbuf", [128, 128], "float16"), "BOb": ("sbuf", [128, 128], "bfloat16"), "BOh": ("sbuf", [128, 128], "float16"),
+    "SEL": ("sbuf", [128, 2048], "float16"), "RX": ("sbuf", [128, 16], "bfloat16"), "KD": ("sbuf", [128, 256], "bfloat16"),
+    "KDF": ("sbuf", [128, 256], "bfloat16"), "C2": ("sbuf", [128, 256], "bfloat16"), "OB": ("sbuf", [128, 128], "bfloat16"),
+    "O5": ("sbuf", [128, 128], "float16"), "THD": ("sbuf", [128, 640], "float16"), "D0": ("sbuf", [128, 256], "float32"),
+    "RLi": ("sbuf", [128, 24], "int32"), "RL": ("sbuf", [128, 24], "uint16"), "PI": ("sbuf", [128, 32], "int32"),
+    "RM": ("sbuf", [128, 2], "uint16"), "DJ": ("sbuf", [128, 128], "int32"), "DD": ("sbuf", [128, 128], "float32"),
+    "M8": ("sbuf", [128, 128], "bfloat16"), "M1": ("sbuf", [128, 128], "bfloat16"), "JI": ("sbuf", [128, 8], "int32"),
+    "JC": ("sbuf", [128, 8], "bfloat16"), "J8": ("sbuf", [128, 8], "bfloat16"), "KR": ("sbuf", [128, 384], "bfloat16"),
+    "CM": ("sbuf", [128, 128], "bfloat16"), "COL": ("sbuf", [128, 16], "float32"), "PI2": ("sbuf", [128, 16], "int32"),
+    "ZL": ("sbuf", [128, 1280], "bfloat16"), "ZN": ("sbuf", [128, 1280], "bfloat16"),
+    "HL": ("sbuf", [128, 10, 2, 128], "float16"), "HN": ("sbuf", [128, 10, 2, 128], "float16"),
+    "PK": ("sbuf", [128, 5120], "bfloat16"), "PS": ("sbuf", [128, 5120], "bfloat16"),
+    "RI": ("sbuf", [128, 1600], "int32"), "RS": ("sbuf", [128, 1600], "int32"),
+    "OFF": ("sbuf", [128, 512], "uint16"), "WW": ("sbuf", [128, 8192], "bfloat16"), "AY": ("sbuf", [128, 4096], "bfloat16"),
+    "XR": ("sbuf", [128, 4096], "bfloat16"), "SC": ("sbuf", [128, 512], "float32"), "SE": ("sbuf", [128, 16], "int32"),
+    "TM": ("sbuf", [128, 64], "float32"), "KQ": ("sbuf", [128, 16], "int32"), "GMx": ("sbuf", [128, 512], "bfloat16"),
+    "LS": ("sbuf", [128, 16], "uint16"), "LC": ("sbuf", [128, 16], "uint16"), "AW": ("sbuf", [128, 256], "bfloat16"),
+    "SZ": ("sbuf", [128, 256], "float32"), "HZ": ("sbuf", [128, 256], "int32"), "UI": ("sbuf", [128, 32], "int32"),
+    "SX2": ("sbuf", [128, 256], "float32"), "HX2": ("sbuf", [128, 256], "int32"), "ES": ("sbuf", [128, 320], "bfloat16"),
+    "M3": ("sbuf", [128, 48], "int32"), "DF": ("sbuf", [128, 128], "float32"),
+    "UO": ("sbuf", [128, 128], "float32"), "MaL": ("sbuf", [128, 128], "float32"), "R1": ("sbuf", [128, 128], "float32"),
+    "QI2": ("sbuf", [128, 256], "float32"), "LPi": ("sbuf", [128, 256], "int32"), "Pi": ("sbuf", [128, 256], "int32"),
+    "QQ": ("sbuf", [128, 256], "int32"), "HB": ("sbuf", [128, 256], "int32"), "HF": ("sbuf", [128, 256], "float16"),
+    "MSK": ("sbuf", [128, 512], "bfloat16"), "PRD": ("sbuf", [128, 512], "float16"), "T1": ("sbuf", [128, 256], "float32"),
+    "AT": ("sbuf", [128, 8], "float32"), "NC": ("sbuf", [128, 8], "float32"), "AI": ("sbuf", [128, 8], "int32"),
+    "YE": ("sbuf", [128, 5], "float32"), "YP": ("sbuf", [128, 256], "float32"), "YF": ("sbuf", [128, 256], "float32"),
+    "FA": ("sbuf", [128, 32], "bfloat16"), "P2": ("sbuf", [128, 256], "float32"),
+    "SB": ("psum", [128, 2048], "float32"), "KP": ("psum", [128, 512], "float32"), "HR": ("psum", [128, 2, 128], "float32"),
+    "ST": ("psum", [128, 512], "float32"), "TL": ("psum", [128, 512], "float32"),
+}
+PSUM = ("SB", "KP", "ST", "TL", "HR")
+KINDS = ("z", "h", "p", "r")
+SEMAPHORES = ["v", "p", "s", "gq", "sent", "dm0", "dm1", "dm2", "dm3", "dx0", "out"] + \
+    ["a%s%d%d" % (k, t, h) for t in range(1, TS) for h in range(2) for k in KINDS] + ["l%d" % t for t in range(1, N)]
+
+
+def rank_program(g, core, T, topo):
+    rank = T.rank_of(core)
+    if rank is None:
+        return
+    sem = T.sem
+    Q = {"v": g.vector, "p": g.tensor, "s": g.scalar, "gq": g, "sy": g.sync}
+    cnt, know, hist, free, late = {}, {q: {} for q in Q}, {}, {q: 0.0 for q in Q}, [False]
+
+    def needs(q, rd, wr):
+        out = []
+        for regs, w in ((rd, False), (wr, True)):
+            for (b, lo, hi) in regs:
+                for e in hist.get(b, ()):
+                    if e[1] < hi and lo < e[2] and (w or e[3]) and not (e[0] == q and (q == "p" or not e[3])):
+                        out.append(e)
+        return out
+
+    def start(d):
+        return max([free[d[0]]] + [e[7] + WAKE for e in needs(d[0], d[2], d[3])])
+
+    def acc(q, rd, wr):
+        for e in sorted(needs(q, rd, wr), key=lambda e: -e[5]):
+            if know[q].get(e[4], 0) < e[5]:
+                Q[q].wait_ge(sem[e[4]], e[5])
+                for s, n in list(e[6].items()) + [(e[4], e[5])]:
+                    know[q][s] = max(know[q].get(s, 0), n)
+
+    def note(q, rd, wr, s, n, snap, fin):
+        for regs, w in ((rd, False), (wr, True)):
+            for (b, lo, hi) in regs:
+                old = [e for e in hist.get(b, []) if not (lo <= e[1] and e[2] <= hi and (w or (e[0] == q and not e[3])))]
+                hist[b] = old + [(q, lo, hi, w, s, n, snap, fin)]
+
+    def do(d):
+        q, fn, rd, wr, s, inc, dur, lat, post = d
+        t0 = start(d)
+        acc(q, rd, wr)
+        free[q] = t0 + dur
+        if s is None:
+            fn(Q[q])
+        else:
+            cnt[s] = cnt.get(s, 0) + inc
+            fn(Q[q]).then_inc(sem[s], inc)
+            note(q, rd, wr, s, cnt[s], dict(know[q]), t0 + dur + lat)
+        if post:
+            post(t0 + dur)
+
+    def give(d):
+        if late[0]:
+            return d
+        do(d)
+
+    def ps(b, lo, hi):
+        return (b, lo // 512, (hi + 511) // 512) if b in PSUM else (b, lo, hi)
+
+    def c(b, lo=0, hi=None, st=1):
+        hi = T[b].shape[1] if hi is None else hi
+        return (T[b][:, lo:hi:st], ps(b, lo, hi))
+
+    def ind(w, o):
+        return (w[0].indirect(o[0]), w[1], o[1])
+
+    def size(x):
+        n = 1
+        for k in list(x[0].shape)[1:]:
+            n *= int(k)
+        return n
+
+    def op(q, fn, out, *ins, dur=300.0):
+        rs = [r for x in ins for r in x[1:]]
+        return give((q, fn, [r for r in rs if r[0] not in PSUM], [out[1]] + [r for r in rs if r[0] in PSUM] + list(out[2:]), q, 1, dur, 0.0, None))
+
+    def span(n, f):
+        return max(64, f * n) + 60.0
+
+    def tt(out, a, b, o):
+        n = size(b)
+        d = 60 + 1.56 * n if len(a) > 2 else span(n, 1 if a[1][0] in PSUM or b[1][0] in PSUM else 2)
+        return op("v", lambda e: e.tensor_tensor(out[0], a[0], b[0], o), out, a, b, dur=d)
+
+    def ts(out, a, s1, s2, o0, o1=None):
+        x = [s for s in (s1, s2) if isinstance(s, tuple)]
+        f1, f2 = [s[0] if isinstance(s, tuple) else s for s in (s1, s2)]
+        d = span(size(out), 1)
+        if o1 is None:
+            return op("v", lambda e: e.tensor_scalar(out[0], a[0], f1, None, o0), out, a, *x, dur=d)
+        return op("v", lambda e: e.tensor_scalar(out[0], a[0], f1, f2, o0, o1), out, a, *x, dur=d)
+
+    def cp(out, a):
+        d = 60 + 3.8 * size(a) if len(out) > 2 else (60 + 1.56 * size(out) if len(a) > 2 else span(size(out), 1))
+        return op("v", lambda e: e.tensor_copy(out[0], a[0]), out, a, dur=d)
+
+    def ms(out, k):
+        return op("v", lambda e: e.memset(out[0], k), out)
+
+    def scan(out, d):
+        return op("v", lambda e: e.tensor_tensor_scan(out[0], T.D0[:, :], d[0], 0.0, A.add, A.max), out, c("D0"), d, dur=320.0)
+
+    def act(out, a, f, bias=0.0, scale=1.0):
+        x = [s for s in (bias, scale) if isinstance(s, tuple)]
+        bb, sc = [s[0] if isinstance(s, tuple) else s for s in (bias, scale)]
+        return op("s", lambda e: e.activation(out[0], a[0], f, bias=bb, scale=sc), out, a, *x, dur=60 + (1.56 if len(a) > 2 else 1) * size(out))
+
+    def mm(out, l, r, first, last):
+        d = max(64, size(r)) * (2.4 if l[1][0] in ("BO", "If") else 0.6)
+        return op("p", lambda e: e.matmul(out[0], l[0], r[0], first, last), out, l, r, dur=d)
+
+    def dma(q, out, in_, s, rd, wr):
+        return give((q, lambda e: e.dma_start(out, in_), rd, wr, s, 16, 60.0, 2200.0, None))
+
+    sent = [0]
+    nxt, prv = T.cores[(rank + 1) % N], T.cores[(rank - 1) % N]
+
+    def send(dst, src, s, outap, in_, lreg):
+        rid, pid = topo.addr(dst, core)
+        en = topo.engines(core, dst)[:8]
+        sent[0] += len(en)
+        return give(("gq", lambda e: e.remote_dma(outap, in_[0], sem[s], sem.sent, pid, rid, sum(1 << x for x in en)), [in_[1]], [], None, 0, 1000.0, 0.0,
+                     lambda t: note("rem", [], [lreg], s, len(topo.engines(src, core)[:8]), {}, t + SHIP - 1000)))
+
+    dma("sy", T.NM[:, :], T.nm[:, :], "dm0", [], [("NM", 0, 256)])
+    dma("sy", T.PR[:, :], T.pr[:, :], "dm1", [], [("PR", 0, 256)])
+    dma("sy", T.ZL[:, 0:256], T.z0[:, :], "dm2", [], [("ZL", 0, 256)])
+    dma("sy", T.TH[:, :], T.th[:, :], "dm3", [], [("TH", 0, 5)])
+    dma("s", T.X[:, 0:2048], T.xt[:, :], "dx0", [], [("X", 0, 2048)])
+    ms(c("ONE"), 1.0)
+
+    def gi(out, pat, base, cm, flag=False):
+        if flag:
+            op("gq", lambda e: e.iota(out[0], pat, base, cm, allow_small_or_imprecise_dtypes=True), out)
+        else:
+            op("gq", lambda e: e.iota(out[0], pat, base, cm), out)
+
+    def gs(out, a, pat, cmp_, base, cm):
+        op("gq", lambda e: e.affine_select(out[0], a[0], pat, cmp_, 0.0, base, cm), out, a)
+
+    gi(c("PI"), [[0, 32]], 0, 1)
+    gi(c("DJ"), [[-1, 128]], 128, 1)
+    gs(c("BOa"), c("ONE"), [[-16, 8], [0, 16]], A.is_ge, 0, 1)
+    gs(c("BO"), c("BOa"), [[16, 8], [0, 16]], A.is_ge, 15, -1)
+    gs(c("If"), c("ONE"), [[-1, 128]], A.is_equal, 0, 1)
+    L3 = lambda b, s: (T[b][:, s], (b, s * 256, s * 256 + 256))
+    Lh = lambda b, s, h: (T[b][:, s, h, :], (b, s * 256 + h * 128, s * 256 + h * 128 + 128))
+    half = lambda b, h, n=128: c(b, h * n, h * n + n)
+    col = lambda j: c("COL", j, j + 1)
+    for h in range(2):
+        cp(Lh("LL", 0, h), half("NM", h))
+    ts(c("PI2"), c("PI", 0, 16), 15, None, A.bitwise_and)
+    u0 = c("PI2", 0, 1)
+    ts(c("DJ"), c("DJ"), 15, None, A.bitwise_and)
+    ts(c("DD"), c("DJ"), 0, None, A.is_equal)
+    cp(c("BOh"), c("BO"))
+    ts(c("NQH"), c("NM"), -2048, None, A.add)
+    ts(c("PT"), c("PR"), -1, 15, A.mult, A.add)
+    gi(c("KR"), [[0, 24], [-1, 16]], 15, 0, True)
+    gi(c("RLi"), [[1, 24]], 0, 0)
+    gi(c("JI"), [[16, 8]], 0, 0)
+    for x4 in range(2):
+        gs((T.PX[:, x4, :], ("PX", x4 * 64, x4 * 64 + 64)), c("ONE", 0, 64), [[-32, 4], [-1, 16]], A.is_equal, -16 * x4, 1)
+    for t in range(1, N):
+        send(T.cores[(rank + t) % N], T.cores[(rank - t) % N], "l%d" % t, T.LL[:, t, :, :], L3("LL", 0), ("LL", t * 256, t * 256 + 256))
+    sset = lambda t: 0 if t % N == 0 else 1 + t % 2
+    ms(c("KC", 0, 1), 1.0)
+    late[0] = True
+    Ib, IND = c("II", 0, 128), c("BOb", 0, 128, 16)
+
+    def statics(t):
+        if t == 3:
+            yield ("need", ("state", 1, 1))
+        if t:
+            yield ("need", ("sel", t - 1, 0))
+        yield ("need", "col")
+        s, ll = sset(t), L3("LL", t % N)
+        yield act(L3("OO", s), ll, F.Identity, bias=col(5), scale=16.0)
+        yield act(L3("A1", s), ll, F.Copy, bias=352.0)
+        yield act(L3("B1", s), ll, F.Copy, bias=1184.0)
+        for j, (w, k) in enumerate(((3232, 352), (2400, 1184))):
+            yield act((T.SXY[:, s, :, j, :], ("SXY", s * 512, s * 512 + 512)), ll, F.Copy, bias=float(w * k - 2 ** 23 - 13024 * 32), scale=float(w))
+        yield ("done", ("statics", t))
+
+    def rows_out():
+        for k in range(16):
+            b = 512 * (k % 4)
+            yield ts(c("SEL", k * 128, k * 128 + 128), c("BOh"), c("DD", k, k + 1), None, A.mult)
+            if k > 3:
+                yield ("need", ("kept", k - 4))
+            yield mm(c("SB", b, b + 256), c("SEL", k * 128, k * 128 + 128), c("NQH"), True, True)
+            yield ("done", ("row", k))
+
+    def some_masks():
+        for k in range(1, 16, 2):
+            a = c("MA", 256 * (k // 2 % 2), 256 * (k // 2 % 2) + 256)
+            yield ts(c("KC", k, k + 1), u0, 0, k - 15, A.mult, A.add)
+            yield act(a, c("PT"), F.Abs, bias=c("KC", k, k + 1))
+            yield act(c("MB", 256 * (k // 2), 256 * (k // 2) + 256), a, F.Relu, bias=c("KC", 0, 1), scale=-1.0)
+            yield ("done", ("mask", k))
+
+    def names():
+        yield cp(c("Ih"), c("If"))
+        for k in range(16):
+            b = 512 * (k % 4)
+            r = c("PRD", 256 * (k % 2), 256 * (k % 2) + 256)
+            if k % 2:
+                m = c("MB", 256 * (k // 2), 256 * (k // 2) + 256)
+                yield ("need", ("mask", k))
+            else:
+                m = c("MSK", 256 * (k // 2 % 2), 256 * (k // 2 % 2) + 256)
+                yield ts(m, c("PT"), 15 - k, None, A.is_equal)
+            yield ("need", ("row", k))
+            if k:
+                yield last
+            yield tt(r, m, c("SB", b, b + 256), A.mult)
+            yield ("done", ("kept", k))
+            last = mm(c("ST", 0, 256), c("Ih"), r, k == 0, k == 15)
+        yield last
+        yield cp(c("LPi"), c("ST", 0, 256))
+        yield ("done", "names")
+
+    def consts():
+        yield ts(col(0), u0, 1, 0, A.mult, A.add)
+        yield ts(col(1), u0, -1, 15, A.mult, A.add)
+        yield ts(col(5), u0, -1, 15 - 32768, A.mult, A.add)
+        yield ("done", "col")
+        yield ts(c("FMG"), c("PT"), col(1), None, A.is_equal)
+        for q in range(2):
+            yield act(c("II", q * 128, q * 128 + 128), c("If"), F.Copy)
+        yield ts(col(3), u0, -1, 16, A.mult, A.add)
+        yield ts(col(4), u0, 1, 1, A.mult, A.add)
+        for q in range(2):
+            yield act(c("KDF", q * 128, q * 128 + 128), c("If"), F.Copy, scale=col(3 + q))
+        yield ms(c("D0"), 0.0)
+        yield ms(c("D0", 0, 256, 16), -1e9)
+        yield cp(c("RL"), c("RLi"))
+        yield act(c("BOb"), c("BO"), F.Copy)
+        yield ms(c("CM"), -128.0)
+        yield ms(c("M3"), 0)
+        yield ms(c("NC"), 0.0)
+        yield ms(c("AT"), 0.0)
+        yield ms((T.PM[:, :, :, :, :], ("PM", 0, 512)), 0.0)
+        for i in range(4):
+            yield cp((T.PM[:, i, :, i % 2, :], ("PM", i * 128, i * 128 + 128)), (T.PX[:, i // 2, :], ("PX", 64 * (i // 2), 64 * (i // 2) + 64)))
+        yield act(c("nI"), c("If"), F.Copy, scale=-1.0)
+        yield ms(c("COL", 15, 16), 128.0)
+        yield ("done", "consts")
+        yield cp(c("X", 2048, 2112), c("X", 0, 64))
+        yield ("done", ("table", -1, 0))
+        yield ("done", ("table", -1, 1))
+        yield ("need", ("H", 0, 0))
+        for h in range(2):
+            yield cp(c("PK", h * 512 + 384, h * 512 + 512), half("PT", h))
+        yield act(c("PN"), c("If"), F.Copy, scale=-2.0 ** 25)
+        yield ts(c("RX", 0, 8), IND, -512, None, A.mult)
+        yield ts(c("RX", 8, 16), IND, 512, None, A.mult)
+        yield ts(col(2), u0, -16, 240, A.mult, A.add)
+        for q in range(2):
+            yield act(c("KD", q * 128, q * 128 + 128), c("If"), F.Copy, scale=col(2))
+            yield ms(c("C2", q * 128, q * 128 + 128), (2.0 ** 20, 256.0)[q])
+        yield ms(c("OB"), 1.0)
+        yield ms(c("O5"), 512.0)
+        yield ts(c("COL", 8, 13), c("TH"), -1, -1, A.mult, A.add)
+        for t in range(TS):
+            yield ts(c("THD", t * 128, t * 128 + 128), c("Ih"), col(8 + t), None, A.mult)
+        yield ("done", ("scan", -1, 1))
+        yield ts(c("PI2", 2, 4), c("PI", 0, 2), 7, None, A.bitwise_and)
+        yield cp(c("RM"), c("PI2", 2, 4))
+        yield act(c("M8"), c("DD"), F.Copy, scale=-8.0)
+        yield act(c("M1"), c("DD"), F.Copy)
+        yield ts(c("JC"), c("JI"), col(0), None, A.add)
+        yield ts(c("J8"), c("JC"), 8, None, A.mult)
+        yield ("done", "rest")
+
+    def masks(rows, P, i):
+        return tt(c(P, i * 512, i * 512 + 384), ind(rows, c("RL")), c("KR"), A.is_equal)
+
+    def new_f(h, s, P, i):
+        yield mm(c("ST", 128, 256), c(P, i * 512 + 128, i * 512 + 256), Ib, True, True)
+        yield tt(c("MaL"), c("ST", 128, 256), Lh("LL", s[0], h), A.mult)
+        yield [mm(c("ST", 384, 512), c("BO"), c("MaL"), True, False), mm(c("ST", 384, 512), c("BOb"), c("CM"), False, True)]
+        yield tt(c("ST", 128, 256), c("ST", 384, 512), Lh("B1", s[1], h), A.mult)
+
+    def names_to_H(h, s, H, i):
+        yield tt(c("ST", 0, 128), Lh("A1", s[1], h), half("LPi", h), A.mult)
+        q = s[1] * 512 + h * 256
+        yield tt(c("QQ"), c("ST", 0, 256), (T.SXY[:, s[1], h, :, :], ("SXY", s[1] * 512, s[1] * 512 + 512)), A.add)
+        yield ts(c("HB"), c("QQ"), 65535, 5, A.bitwise_and, A.logical_shift_right)
+        yield cp(c("HF"), c("HB"))
+        yield op("v", lambda e: e.transpose(T[H][:, i, :, :], T.HF[:, :]), (None, (H, i * 256, i * 256 + 256)), c("HF"), dur=190.0)
+
+    def first_state(h):
+        if h:
+            yield ("need", ("state", -1, 0))
+        else:
+            for k in ("consts", "names", ("statics", 0)):
+                yield ("need", k)
+        yield mm(c("ST", 0, 256), half("FMG", h), c("KDF"), True, True)
+        sc, r = h * 256, h * 160
+        yield ts(c("T1", 0, 128), half("LPi", h), 16, None, A.mult)
+        yield tt(c("RI", r, r + 128), c("T1", 0, 128), half("PT", h), A.add)
+        yield scan(c("SC", sc, sc + 256), c("ST", 0, 256))
+        yield ts(c("M3", h * 24 + 8, h * 24 + 16), c("SC", sc + 15, sc + 128, 16), -1, None, A.add)
+        yield ts(c("M3", h * 24 + 16, h * 24 + 24), c("SC", sc + 143, sc + 256, 16), -1, 16, A.mult, A.add)
+        yield masks(c("M3", h * 24, h * 24 + 24), "PK", h)
+        for x in new_f(h, (0, 0), "PK", h):
+            yield x
+        for x in names_to_H(h, (0, 0), "HL", h):
+            yield x
+        yield ("done", ("H", 0, h))
+        for e in (128, 152):
+            yield cp(c("RI", r + e, r + e + 8), c("M3", h * 24 + 16, h * 24 + 24))
+        for k in ("p", "r", "z"):
+            yield ("done", (k, 0, h))
+        yield ("done", ("state", -1, h))
+
+    def lists(t, h):
+        i = t * 2 + h
+        yield ("need", ("H", t, h))
+        yield ("need", ("scan", t - 1, 1))
+        if h:
+            yield ("need", ("L", t, 0))
+        for ib in range(4):
+            p = []
+            for x4 in range(2):
+                for g2 in range(2):
+                    w = ib * 32 + g2 * 16
+                    p.append(mm((T.HR[:, :, 2 * ib + x4:128:8], ("HR", 0, 1)), (T.PM[:, 2 * x4 + g2], ("PM", 0, 512)),
+                                (T.HL[:, i, :, w:w + 16], ("HL", i * 256, i * 256 + 256)), g2 == 0, g2 == 1))
+            yield p
+        yield ("need", ("nc", t))
+        if h == 0:
+            yield ("need", ("g", t - 1, 0))
+        yield ts(c("OFF", h * 256, h * 256 + 256), (T.HR[:, :, :], ("HR", 0, 1)), c("NC", t, t + 1), None, A.add)
+        yield ("done", ("L", t, h))
+
+    XW = c("X", 0, 2112)
+
+    def raw(h, j):
+        return c("WW", h * 4096 + 512 * j, h * 4096 + 512 * j + 512) if j < 4 else c("XR", h * 2048 + 512 * (j - 4), h * 2048 + 512 * (j - 4) + 512)
+
+    def gathers(t, h):
+        yield ("need", ("L", t, h))
+        yield ("need", ("table", t - 1, 0))
+        yield ("need", ("table", t - 1, 1))
+        if h:
+            yield ("need", ("g", t, 0))
+        for j in range(8):
+            o = h * 256 + (128 + 32 * j if j < 4 else 32 * (j - 4))
+            w = ind(XW, c("OFF", o, o + 32))
+            a = act(raw(h, j), w, F.Copy, bias=-128.0 if j < 4 else 0.0)
+            if j < 4:
+                yield a
+            else:
+                yield ("alt", a, cp(raw(h, j), w))
+            yield ("done", ("g", t, h, j))
+        yield ("done", ("g", t, h))
+
+    def minus_z(t, h):
+        i = t * 2 + h
+        yield ("need", ("z", t, h))
+        for j in range(8):
+            b, J = 512 * (j % 4), i * 8 + j - 4
+            yield ("need", ("g", t, h, j))
+            if J >= 0:
+                yield ("need", ("abs", J))
+            yield [mm(c("SB", b, b + 512), Ib, raw(h, j), True, False)] + \
+                [mm(c("SB", b + 128 * r, b + 128 * r + 128), c("nI"), c("ZL", i * 128, i * 128 + 128), False, r == 3) for r in range(4)]
+            yield ("done", ("d", t, h, j))
+
+    def absval(t, h):
+        for j in range(8):
+            yield ("need", ("d", t, h, j))
+            b, w = 512 * (j % 4), h * 4096 + 2048 + 512 * (j - 4)
+            if j < 4:
+                yield act(c("AY", h * 2048 + 512 * j, h * 2048 + 512 * j + 512), c("SB", b, b + 512), F.Abs, bias=c("COL", 15, 16))
+            else:
+                yield act(c("WW", w, w + 512), c("SB", b, b + 512), F.Abs)
+            yield ("done", ("abs", (t * 2 + h) * 8 + j))
+
+    def sums(t, h):
+        i = (t * 2 + h) * 512
+        yield ("need", ("scan", t - 1 + h, 1 - h))
+        yield ("need", ("p", t, h))
+        kp = c("KP", 0, 256)
+        yield [mm(kp, Ib, c("C2"), True, False), mm(kp, c("OB"), c("KD"), False, False),
+               mm(c("KP", 128, 256), c("O5"), c("THD", t * 128, t * 128 + 128), False, False)]
+        yield [mm(kp, c("PK", i + 384, i + 512), c("II"), False, False)] + \
+            [mm(c("KP", q * 128, q * 128 + 128), c("PN"), c("PK", i + j, i + j + 128), False, False) for q in range(2) for j in (128, 256)]
+        for j in range(8):
+            yield ("need", ("abs", (t * 2 + h) * 8 + j))
+            p = []
+            for k in range(4 * (j % 4), 4 * (j % 4) + 4):
+                if j < 4:
+                    p.append(mm(c("KP", 128 + k, 256, 16), c("AY", h * 2048 + k * 128, h * 2048 + k * 128 + 128), c("RX", 0, 8), False, False))
+                else:
+                    w = h * 4096 + 2048 + k * 128
+                    p.append(mm(c("KP", k, 256, 16), c("WW", w, w + 128), c("RX"), False, k == 15))
+            yield p
+        yield ("done", ("sums", t, h))
+
+    def choose(t, h):
+        sc, e, i = h * 256, (t * 2 + h) * 32, t * 2 + h
+        yield ("need", ("sums", t, h))
+        yield scan(c("SC", sc, sc + 256), c("KP", 0, 256))
+        yield ("done", ("scan", t, h))
+        yield ("need", "rest")
+        mS, mD = c("SC", sc + 143, sc + 256, 16), c("SC", sc + 15, sc + 128, 16)
+        m, a, sel = c("TM", h * 16, h * 16 + 8), c("TM", 32 + h * 16, 40 + h * 16), c("SE", h * 8, h * 8 + 8)
+        yield ts(m, mS, 0, 2 ** 21, A.is_ge, A.mult)
+        yield tt(a, m, mS, A.add)
+        yield tt(sel, a, mD, A.max)
+        yield ts(half("KQ", h, 8), sel, 0x1F0, None, A.bitwise_and)
+        yield tt(half("GMx", h), ind(half("KQ", h, 8), c("RL", 0, 8)), c("M8"), A.mult)
+        yield [mm(c("TL", 0, 8), Ib, c("JC"), True, False), mm(c("TL", 0, 8), half("GMx", h), IND, False, True)]
+        yield ts(c("ES", e, e + 32), ind(sel, c("RM")), 2 ** 21, None, A.is_lt)
+        yield ("done", ("sel", t, h))
+        yield ts(half("LS", h, 8), c("TL", 0, 8), 3968, None, A.add)
+        yield act(half("AW", h), ind(half("WW", h, 4096), half("LS", h, 8)), F.Abs)
+        z, zn = c("ZL", i * 128, i * 128 + 128), c("ZN", i * 128, i * 128 + 128)
+        yield tt(half("SZ", h), ind(half("WW", h, 4096), half("LS", h, 8)), z, A.add)
+        yield ts(half("HZ", h), half("SZ", h), 0.5, 63.75, A.mult, A.add)
+        yield tt(zn, half("HZ", h), half("AW", h), A.min)
+        if t + 1 < TS:
+            n = (i + 2) * 128
+            yield send(nxt, prv, "az%d%d" % (t + 1, h), T.ZL[:, n:n + 128], zn, ("ZL", n, n + 128))
+            yield ("done", ("z", t + 1, h))
+        yield mm(c("TL", 8, 16), zn, IND, True, True)
+        yield cp(c("UI", h * 16, h * 16 + 8), c("TL", 8, 16))
+        yield ts(c("UI", h * 16 + 8, h * 16 + 16), c("UI", h * 16, h * 16 + 8), 7, None, A.bitwise_and)
+        yield tt(half("GMx", 2 + h), ind(c("UI", h * 16 + 8, h * 16 + 16), c("RL", 0, 8)), c("M1"), A.mult)
+        yield [mm(c("TL", 16, 24), Ib, c("J8"), True, False), mm(c("TL", 16, 24), half("GMx", 2 + h), IND, False, True)]
+        yield cp(half("LC", h, 8), c("TL", 16, 24))
+        xw = c("X", 1024 * h, 1024 * h + 1024)
+        yield tt(half("SX2", h), ind(xw, half("LC", h, 8)), zn, A.add)
+        yield ts(half("HX2", h), half("SX2", h), 0.5, -0.25, A.mult, A.add)
+        yield ("need", ("g", t, 1))
+        yield cp(ind(xw, half("LC", h, 8)), half("HX2", h))
+        if h == 0 and t + 1 < TS:
+            yield cp(c("X", 2048, 2112), c("X", 0, 64))
+        yield ("done", ("table", t, h))
+
+    def count(t):
+        yield ("need", ("sel", t, 0))
+        yield ("need", ("sel", t, 1))
+        yield [mm(c("TL", 24, 32), c("OB"), c("ES", j * 32, j * 32 + 8), j == 0, j == 2 * t + 1) for j in range(2 * t + 2)]
+        yield tt(c("DF", 96, 104), c("TL", 24, 32), c("BO", 0, 128, 16), A.mult)
+        yield op("v", lambda e: e.tensor_reduce(T.AT[:, t + 1:t + 2], T.DF[:, 96:104], AxisListType.X, A.add), c("AT", t + 1, t + 2), c("DF", 96, 104), dur=130.0)
+        if t + 1 < TS:
+            yield ts(c("AI", t, t + 1), c("AT", t + 1, t + 2), 1 / 64, -63 / 128, A.mult, A.add)
+            yield ts(c("NC", t + 1, t + 2), c("AI", t, t + 1), -64, c("AT", t + 1, t + 2), A.mult, A.add)
+            yield ("done", ("nc", t + 1))
+        else:
+            yield tt(c("YE"), c("AT", 1, 6), c("AT", 0, 5), A.subtract)
+            yield out(T.ye[:, :], c("YE"))
+
+    def state(t, h):
+        i, s, d = t * 2 + h, (t % N, sset(t)), 48 * h
+        sel, e, b, j = c("SE", h * 8, h * 8 + 8), i * 32, i * 160 + 128, i * 512
+        yield ("need", ("sel", t, h))
+        yield ("need", ("r", t, h))
+        yield ts(c("RI", b + 8, b + 16), sel, 4, 15, A.logical_shift_right, A.bitwise_and)
+        yield ts(c("RI", b + 16, b + 24), sel, 15, None, A.bitwise_and)
+        yield tt(c("DF", d, d + 24), c("RI", b, b + 24), c("RI", b + 8, b + 32), A.subtract)
+        yield tt(c("DF", d + 24, d + 48), c("DF", d, d + 24), c("ES", e, e + 24), A.mult)
+        yield tt(c("RS", b + 8, b + 32), c("RI", b + 8, b + 32), c("DF", d + 24, d + 48), A.add)
+        yield masks(c("RS", b + 8, b + 32), "PS", i)
+        yield ("need", ("statics", t % N))
+        Qo, Qn, R = c("RI", i * 160, i * 160 + 128), c("RS", i * 160, i * 160 + 128), half("QI2", h)
+        yield tt(R, Qo, Lh("OO", s[1], h), A.add)
+        yield ("need", ("state", t - 1 + h, 1 - h))
+        yield [mm(c("ST", 0, 128), c("PS", j, j + 128), Ib, True, False), mm(c("ST", 0, 128), c("PK", j + 128, j + 256), Ib, False, True)]
+        yield tt(c("UO"), c("ST", 0, 128), Lh("OO", s[1], h), A.mult)
+        yield mm(c("ST", 256, 384), c("BO"), c("UO"), True, True)
+        if t + 1 < TS:
+            for x in new_f(h, s, "PS", i):
+                yield x
+        yield tt(c("R1"), c("ST", 256, 384), R, A.subtract)
+        yield tt(c("ST", 256, 384), c("ST", 0, 128), c("R1"), A.mult)
+        yield tt(Qn, c("ST", 256, 384), Qo, A.add)
+        if t + 1 == TS:
+            yield ts(half("Pi", h), Qn, 15, None, A.bitwise_and)
+            yield ("done", ("state", t, h))
+            return
+        yield ts(half("LPi", h), Qn, 4, None, A.arith_shift_right)
+        for x in names_to_H(h, s, "HN", i):
+            yield x
+        n = i + 2
+
+        def ship(k, outap, inap, reg, lreg):
+            return send(nxt, prv, "a%s%d%d" % (k, t + 1, h), outap, (inap, reg), lreg)
+        yield ship("h", T.HL[:, n, :, :], T.HN[:, i, :, :], ("HN", i * 256, i * 256 + 256), ("HL", n * 256, n * 256 + 256))
+        yield ("done", ("H", t + 1, h))
+        yield ts(half("Pi", h), Qn, 15, None, A.bitwise_and)
+        yield cp(c("PS", j + 384, j + 512), half("Pi", h))
+        yield ship("p", T.PK[:, n * 512 + 128:n * 512 + 512], T.PS[:, j + 128:j + 512], ("PS", j + 128, j + 512), ("PK", n * 512 + 128, n * 512 + 512))
+        yield ("done", ("p", t + 1, h))
+        yield cp(c("RS", b, b + 8), c("RS", b + 24, b + 32))
+        yield ship("r", T.RI[:, n * 160:n * 160 + 160], T.RS[:, i * 160:i * 160 + 160], ("RS", i * 160, i * 160 + 160), ("RI", n * 160, n * 160 + 160))
+        yield ("done", ("r", t + 1, h))
+        yield ("done", ("state", t, h))
+
+    def out(dst, src, q="sy"):
+        return give((q, lambda e: e.dma_start(dst, src[0]), [src[1]], [], "out", 16, 60.0, 2200.0, None))
+
+    def finish(h):
+        i = 2 * (TS - 1) + h
+        j = i * 512
+        yield ("need", ("state", TS - 1, h))
+        if h:
+            yield ("need", ("finish", 0))
+        yield cp(half("FA", h, 8), c("RS", i * 160 + 144, i * 160 + 152))
+        o = (T.ST[0:8, 384:512], ("ST", 0, 1))
+        yield [mm(c("ST", 128, 256), c("PS", j + 128, j + 256), Ib, True, False), mm(c("ST", 128, 256), c("PS", j + 256, j + 384), Ib, False, True),
+               mm(o, half("FA", h, 8), Ib, True, True)]
+        p = c("P2", 128 * h, 128 * h + 128)
+        yield ts(p, half("Pi", h), -1, col(1), A.mult, A.add)
+        yield tt(c("T1", 128 * h, 128 * h + 128), c("ST", 128, 256), p, A.mult)
+        y = (T.YF[0:8, h * 128:h * 128 + 128], ("YF", h * 128, h * 128 + 128))
+        yield ts(y, o, -1, 15, A.mult, A.add)
+        yield ("done", ("finish", h))
+        yield out(T.yf[:, h * 128:h * 128 + 128], y)
+        yield tt(p, c("T1", 128 * h, 128 * h + 128), half("Pi", h), A.add)
+        yield ts(half("YP", h), p, -1, 15, A.mult, A.add)
+        yield out(T.yp[:, h * 128:h * 128 + 128], half("YP", h))
+
+    def last():
+        yield ("need", ("table", TS - 1, 0))
+        yield ("need", ("table", TS - 1, 1))
+        yield out(T.yx[:, :], c("X", 0, 2048))
+        yield out(T.yz[:, :], c("ZN", 8 * 128, 10 * 128), "s")
+
+    th = [(0, some_masks()), (0, rows_out()), (0, names()), (2, consts()), (3, first_state(0)), (4, first_state(1)), (0, last())]
+    for t in range(TS):
+        for h in range(2):
+            th += [(0, lists(t, h)), (0, choose(t, h)), (3 - h, state(t, h)), (5, gathers(t, h)), (4, minus_z(t, h)), (4, absval(t, h)), (4, sums(t, h))]
+        th.append((1, count(t)))
+        if t < N:
+            th.append((6, statics(t)))
+    for h in range(2):
+        th.append((3, finish(h)))
+    ev, live, blocked = {("nc", 0), ("g", -1, 0)}, [], {}
+
+    def pull(rec):
+        for x in rec[1]:
+            if isinstance(x, tuple) and x[0] == "done":
+                ev.add(x[1])
+                for r in blocked.pop(x[1], ()):
+                    pull(r)
+            elif isinstance(x, tuple) and x[0] == "need":
+                if x[1] not in ev:
+                    blocked.setdefault(x[1], []).append(rec)
+                    return
+            else:
+                rec[2] = x
+                live.append(rec)
+                return
+
+    def when(x):
+        if isinstance(x, list):
+            return start(x[0]), x
+        if x[0] == "alt":
+            a, v = start(x[1]), start(x[2])
+            return (v, [x[2]]) if v + x[2][6] + VPEN < a + x[1][6] else (a, [x[1]])
+        return start(x), [x]
+
+    for n, (p, gen) in enumerate(th):
+        pull([p * 1000 + n, gen, None])
+    while live:
+        best = None
+        for rec in live:
+            s, calls = when(rec[2])
+            if best is None or (s, rec[0]) < (best[0], best[1][0]):
+                best = (s, rec, calls)
+        live.remove(best[1])
+        for d in best[2]:
+            do(d)
+        pull(best[1])
+    for s in cnt:
+        g.wait_ge(sem[s], cnt[s])
+    for t in range(1, N):
+        g.wait_ge(sem["l%d" % t], len(topo.engines(T.cores[(rank - t) % N], core)[:8]))
+    for t in range(1, TS):
+        for h in range(2):
+            for k in KINDS:
+                g.wait_ge(sem["a%s%d%d" % (k, t, h)], len(topo.engines(prv, core)[:8]))
+    g.wait_ge(sem.sent, sent[0])

@@ -1,52 +1,35 @@
 from concourse.mybir import dt, AluOpType as A, AxisListType, ActivationFunctionType as F
 
 N, TS = 4, 5
-VPEN = 0.0
-WAKE, SHIP = 70.0, 4200.0
-SCRATCH = {
-    "X": ("sbuf", [128, 2112], "bfloat16"), "NM": ("sbuf", [128, 256], "int32"), "PR": ("sbuf", [128, 256], "int32"),
-    "TH": ("sbuf", [128, 5], "int32"), "LL": ("sbuf", [128, 4, 2, 128], "float32"), "NQH": ("sbuf", [128, 256], "float16"),
-    "PT": ("sbuf", [128, 256], "bfloat16"), "MA": ("sbuf", [128, 512], "float32"), "MB": ("sbuf", [128, 2048], "bfloat16"),
-    "FMG": ("sbuf", [128, 256], "bfloat16"), "KC": ("sbuf", [128, 16], "float32"),
-    "OO": ("sbuf", [128, 3, 2, 128], "float32"), "A1": ("sbuf", [128, 3, 2, 128], "float32"),
-    "B1": ("sbuf", [128, 3, 2, 128], "float32"), "SXY": ("sbuf", [128, 3, 2, 2, 128], "float32"),
-    "ONE": ("sbuf", [128, 128], "float32"), "If": ("sbuf", [128, 128], "float32"), "BOa": ("sbuf", [128, 128], "float32"),
-    "BO": ("sbuf", [128, 128], "float32"), "PX": ("sbuf", [128, 2, 64], "float32"), "PM": ("sbuf", [128, 4, 4, 2, 16], "float16"),
-    "II": ("sbuf", [128, 256], "bfloat16"), "nI": ("sbuf", [128, 128], "bfloat16"), "PN": ("sbuf", [128, 128], "bfloat16"),
-    "Ih": ("sbuf", [128, 128], "float16"), "BOb": ("sbuf", [128, 128], "bfloat16"), "BOh": ("sbuf", [128, 128], "float16"),
-    "SEL": ("sbuf", [128, 2048], "float16"), "RX": ("sbuf", [128, 16], "bfloat16"), "KD": ("sbuf", [128, 256], "bfloat16"),
-    "KDF": ("sbuf", [128, 256], "bfloat16"), "C2": ("sbuf", [128, 256], "bfloat16"), "OB": ("sbuf", [128, 128], "bfloat16"),
-    "O5": ("sbuf", [128, 128], "float16"), "THD": ("sbuf", [128, 640], "float16"), "D0": ("sbuf", [128, 256], "float32"),
-    "RLi": ("sbuf", [128, 24], "int32"), "RL": ("sbuf", [128, 24], "uint16"), "PI": ("sbuf", [128, 32], "int32"),
-    "RM": ("sbuf", [128, 2], "uint16"), "DJ": ("sbuf", [128, 128], "int32"), "DD": ("sbuf", [128, 128], "float32"),
-    "M8": ("sbuf", [128, 128], "bfloat16"), "M1": ("sbuf", [128, 128], "bfloat16"), "JI": ("sbuf", [128, 8], "int32"),
-    "JC": ("sbuf", [128, 8], "bfloat16"), "J8": ("sbuf", [128, 8], "bfloat16"), "KR": ("sbuf", [128, 384], "bfloat16"),
-    "CM": ("sbuf", [128, 128], "bfloat16"), "COL": ("sbuf", [128, 16], "float32"), "PI2": ("sbuf", [128, 16], "int32"),
-    "ZL": ("sbuf", [128, 1280], "bfloat16"), "ZN": ("sbuf", [128, 1280], "bfloat16"),
-    "HL": ("sbuf", [128, 10, 2, 128], "float16"), "HN": ("sbuf", [128, 10, 2, 128], "float16"),
-    "PK": ("sbuf", [128, 5120], "bfloat16"), "PS": ("sbuf", [128, 5120], "bfloat16"),
-    "RI": ("sbuf", [128, 1600], "int32"), "RS": ("sbuf", [128, 1600], "int32"),
-    "OFF": ("sbuf", [128, 512], "uint16"), "WW": ("sbuf", [128, 8192], "bfloat16"), "AY": ("sbuf", [128, 4096], "bfloat16"),
-    "XR": ("sbuf", [128, 4096], "bfloat16"), "SC": ("sbuf", [128, 512], "float32"), "SE": ("sbuf", [128, 16], "int32"),
-    "TM": ("sbuf", [128, 64], "float32"), "KQ": ("sbuf", [128, 16], "int32"), "GMx": ("sbuf", [128, 512], "bfloat16"),
-    "LS": ("sbuf", [128, 16], "uint16"), "LC": ("sbuf", [128, 16], "uint16"), "AW": ("sbuf", [128, 256], "bfloat16"),
-    "SZ": ("sbuf", [128, 256], "float32"), "HZ": ("sbuf", [128, 256], "int32"), "UI": ("sbuf", [128, 32], "int32"),
-    "SX2": ("sbuf", [128, 256], "float32"), "HX2": ("sbuf", [128, 256], "int32"), "ES": ("sbuf", [128, 320], "bfloat16"),
-    "M3": ("sbuf", [128, 48], "int32"), "DF": ("sbuf", [128, 128], "float32"),
-    "UO": ("sbuf", [128, 128], "float32"), "MaL": ("sbuf", [128, 128], "float32"), "R1": ("sbuf", [128, 128], "float32"),
-    "QI2": ("sbuf", [128, 256], "float32"), "LPi": ("sbuf", [128, 256], "int32"), "Pi": ("sbuf", [128, 256], "int32"),
-    "QQ": ("sbuf", [128, 256], "int32"), "HB": ("sbuf", [128, 256], "int32"), "HF": ("sbuf", [128, 256], "float16"),
-    "MSK": ("sbuf", [128, 512], "bfloat16"), "PRD": ("sbuf", [128, 512], "float16"), "T1": ("sbuf", [128, 256], "float32"),
-    "AT": ("sbuf", [128, 8], "float32"), "NC": ("sbuf", [128, 8], "float32"), "AI": ("sbuf", [128, 8], "int32"),
-    "YE": ("sbuf", [128, 5], "float32"), "YP": ("sbuf", [128, 256], "float32"), "YF": ("sbuf", [128, 256], "float32"),
-    "FA": ("sbuf", [128, 32], "bfloat16"), "P2": ("sbuf", [128, 256], "float32"),
-    "SB": ("psum", [128, 2048], "float32"), "KP": ("psum", [128, 512], "float32"), "HR": ("psum", [128, 2, 128], "float32"),
-    "ST": ("psum", [128, 512], "float32"), "TL": ("psum", [128, 512], "float32"),
+NV = 8
+WAKE, SHIP = 70.0, 4500.0
+CY, PE, FIX = 0.9, 0.5, 55.0
+BIG, M1_, M8_ = 2.0 ** 19, 1.5 * 2 ** 23, 1.5 * 2 ** 26
+f32, b16, h16, i32, u16 = "float32", "bfloat16", "float16", "int32", "uint16"
+SB_ = {
+    "X": ([2112], b16), "NM": ([256], i32), "PR": ([256], i32), "TH": ([5], i32), "Z0": ([256], b16), "ZO": ([256], b16),
+    "ONE": ([128], f32), "If": ([8, 16], f32), "BOa": ([128], f32), "BO": ([8, 16], f32), "LT": ([128], b16), "PERM": ([128], b16),
+    "PI": ([16], i32), "PI2": ([16], i32), "DJ": ([128], i32), "M1": ([128], b16), "COL": ([24], f32), "KC": ([32], f32),
+    "Ib": ([128], b16), "nI": ([128], b16), "I2": ([128], b16), "I14": ([128], b16), "Im": ([128], b16), "BOb": ([128], b16),
+    "Zf": ([2, 144], f32), "Z4": ([2, 144], f32), "Zb": ([2, 144], b16), "A12": ([256], f32), "SEL": ([256], b16), "D12": ([256], b16),
+    "SXY": ([256], b16), "SXa": ([256], b16), "WP": ([256], b16), "CAB": ([256], b16), "PX": ([2, 64], f32), "PM": ([4, 4, 2, 16], h16),
+    "RX": ([3, 8, 2], b16), "RY": ([8], b16), "CK": ([8, 2, 14], b16), "CKi": ([8, 2, 14], f32), "KR": ([8, 2, 14], b16),
+    "TM": ([TS, 8, 2, 14], h16), "OB": ([256], b16), "D0": ([224], f32), "RLi": ([8], i32), "RL": ([8], u16),
+    "JI": ([8], i32), "JC": ([24], b16), "J8": ([16], b16), "IN3": ([24], b16), "MV": ([64], i32), "OH": ([64], b16),
+    "MK": ([768], b16), "P16": ([256], b16), "NQ": ([256], h16), "AA": ([512], b16), "W1": ([256], b16), "W2": ([256], f32),
+    "R1": ([4096], b16), "R2": ([4096], f32),
+    "ML": ([3840], h16), "MS": ([3840], h16),
+    "PP": ([512], f32), "QQ": ([512], i32), "HB": ([512], i32), "HF": ([512], h16), "HT": ([2, 2, 128], h16), "DL": ([512], f32), "TT": ([512], f32),
+    "OFF": ([512], u16), "WW": ([8192], b16), "AY": ([4096], b16), "XR": ([4096], b16), "RU": ([4096], b16),
+    "SC": ([448], f32), "FF": ([16], f32), "SE": ([16], i32), "KQ": ([16], i32), "GM": ([256], b16), "LS": ([48], u16), "ES": ([16], b16),
+    "AW": ([256], b16), "SZ": ([256], f32), "HZ": ([256], i32), "K8": ([16], b16), "LC": ([16], u16), "SX2": ([256], f32), "HX2": ([256], i32),
+    "AT": ([8], f32), "NC": ([8], b16), "AI": ([8], i32), "YE": ([5], f32), "YP": ([256], f32), "YF": ([256], f32),
 }
+SCRATCH = {k: ("sbuf", [128] + v[0], v[1]) for k, v in SB_.items()}
+SCRATCH.update({"SB": ("psum", [128, 1536], f32), "KP": ("psum", [128, 512], f32), "HR": ("psum", [128, 2, 128], f32),
+                "ST": ("psum", [128, 1024], f32), "TL": ("psum", [128, 512], f32)})
 PSUM = ("SB", "KP", "ST", "TL", "HR")
-KINDS = ("z", "h", "p", "r")
-SEMAPHORES = ["v", "p", "s", "gq", "sent", "dm0", "dm1", "dm2", "dm3", "dx0", "out"] + \
-    ["a%s%d%d" % (k, t, h) for t in range(1, TS) for h in range(2) for k in KINDS] + ["l%d" % t for t in range(1, N)]
+SEMAPHORES = ["v", "p", "s", "gq", "sent", "dm0", "dm1", "dm2", "dm3", "dx0", "out"] + ["a%d%d" % (t, h) for t in range(1, TS) for h in range(2)]
 
 
 def rank_program(g, core, T, topo):
@@ -55,7 +38,7 @@ def rank_program(g, core, T, topo):
         return
     sem = T.sem
     Q = {"v": g.vector, "p": g.tensor, "s": g.scalar, "gq": g, "sy": g.sync}
-    cnt, know, hist, free, late = {}, {q: {} for q in Q}, {}, {q: 0.0 for q in Q}, [False]
+    cnt, know, hist, free = {}, {q: {} for q in Q}, {}, {q: 0.0 for q in Q}
 
     def needs(q, rd, wr):
         out = []
@@ -96,17 +79,15 @@ def rank_program(g, core, T, topo):
         if post:
             post(t0 + dur)
 
-    def give(d):
-        if late[0]:
-            return d
-        do(d)
-
     def ps(b, lo, hi):
         return (b, lo // 512, (hi + 511) // 512) if b in PSUM else (b, lo, hi)
 
     def c(b, lo=0, hi=None, st=1):
         hi = T[b].shape[1] if hi is None else hi
         return (T[b][:, lo:hi:st], ps(b, lo, hi))
+
+    def a(b, ap=None):
+        return (T[b][:] if ap is None else ap, ps(b, 0, 512 if b in PSUM else 1 << 20))
 
     def ind(w, o):
         return (w[0].indirect(o[0]), w[1], o[1])
@@ -119,517 +100,507 @@ def rank_program(g, core, T, topo):
 
     def op(q, fn, out, *ins, dur=300.0):
         rs = [r for x in ins for r in x[1:]]
-        return give((q, fn, [r for r in rs if r[0] not in PSUM], [out[1]] + [r for r in rs if r[0] in PSUM] + list(out[2:]), q, 1, dur, 0.0, None))
+        return (q, fn, [r for r in rs if r[0] not in PSUM], [out[1]] + [r for r in rs if r[0] in PSUM] + list(out[2:]), q, 1, dur, 0.0, None)
 
-    def span(n, f):
-        return max(64, f * n) + 60.0
+    def narrow(*xs):
+        return all(SCRATCH[x[1][0]][2] in (b16, h16, u16) for x in xs)
 
-    def tt(out, a, b, o):
-        n = size(b)
-        d = 60 + 1.56 * n if len(a) > 2 else span(n, 1 if a[1][0] in PSUM or b[1][0] in PSUM else 2)
-        return op("v", lambda e: e.tensor_tensor(out[0], a[0], b[0], o), out, a, b, dur=d)
+    def span(out, i, f):
+        if len(out) > 2:
+            return FIX + 3.8 * CY * size(i)
+        if len(i) > 2:
+            return FIX + 1.56 * CY * size(out)
+        return FIX + CY * max(64, f * size(out))
 
-    def ts(out, a, s1, s2, o0, o1=None):
-        x = [s for s in (s1, s2) if isinstance(s, tuple)]
+    def tt(out, x, y, o):
+        d = span(out, x, 1 if x[1][0] in PSUM or y[1][0] in PSUM else 2)
+        return op("v", lambda e: e.tensor_tensor(out[0], x[0], y[0], o), out, x, y, dur=d)
+
+    def ts(out, x, s1, s2, o0, o1=None):
+        y = [s for s in (s1, s2) if isinstance(s, tuple)]
         f1, f2 = [s[0] if isinstance(s, tuple) else s for s in (s1, s2)]
-        d = span(size(out), 1)
+        d = span(out, x, 0.5 if narrow(out, x) else 1)
         if o1 is None:
-            return op("v", lambda e: e.tensor_scalar(out[0], a[0], f1, None, o0), out, a, *x, dur=d)
-        return op("v", lambda e: e.tensor_scalar(out[0], a[0], f1, f2, o0, o1), out, a, *x, dur=d)
+            return op("v", lambda e: e.tensor_scalar(out[0], x[0], f1, None, o0), out, x, *y, dur=d)
+        return op("v", lambda e: e.tensor_scalar(out[0], x[0], f1, f2, o0, o1), out, x, *y, dur=d)
 
-    def cp(out, a):
-        d = 60 + 3.8 * size(a) if len(out) > 2 else (60 + 1.56 * size(out) if len(a) > 2 else span(size(out), 1))
-        return op("v", lambda e: e.tensor_copy(out[0], a[0]), out, a, dur=d)
+    def cp(out, x):
+        return op("v", lambda e: e.tensor_copy(out[0], x[0]), out, x, dur=span(out, x, 0.5 if narrow(out, x) else 1))
 
     def ms(out, k):
-        return op("v", lambda e: e.memset(out[0], k), out)
+        return op("v", lambda e: e.memset(out[0], k), out, dur=span(out, out, 0.5 if narrow(out) else 1))
 
-    def scan(out, d):
-        return op("v", lambda e: e.tensor_tensor_scan(out[0], T.D0[:, :], d[0], 0.0, A.add, A.max), out, c("D0"), d, dur=320.0)
-
-    def act(out, a, f, bias=0.0, scale=1.0):
-        x = [s for s in (bias, scale) if isinstance(s, tuple)]
+    def act(out, x, f, bias=0.0, scale=1.0):
+        y = [s for s in (bias, scale) if isinstance(s, tuple)]
         bb, sc = [s[0] if isinstance(s, tuple) else s for s in (bias, scale)]
-        return op("s", lambda e: e.activation(out[0], a[0], f, bias=bb, scale=sc), out, a, *x, dur=60 + (1.56 if len(a) > 2 else 1) * size(out))
+        return op("s", lambda e: e.activation(out[0], x[0], f, bias=bb, scale=sc), out, x, *y, dur=FIX + CY * (1.56 if len(x) > 2 else 1) * size(out))
 
     def mm(out, l, r, first, last):
-        d = max(64, size(r)) * (2.4 if l[1][0] in ("BO", "If") else 0.6)
-        return op("p", lambda e: e.matmul(out[0], l[0], r[0], first, last), out, l, r, dur=d)
+        d = max(min(64, size(l)), size(r)) * PE * (4 if SCRATCH[l[1][0]][2] == f32 else 1)
+
+        def fn(e):
+            if isinstance(last, list):
+                last[0] -= 1
+                return e.matmul(out[0], l[0], r[0], first, last[0] == 0)
+            return e.matmul(out[0], l[0], r[0], first, last)
+        return op("p", fn, out, l, r, dur=d)
+
+    def group(out, *terms):
+        return [mm(out, l, r, n == 0, n == len(terms) - 1) for n, (l, r) in enumerate(terms)]
 
     def dma(q, out, in_, s, rd, wr):
-        return give((q, lambda e: e.dma_start(out, in_), rd, wr, s, 16, 60.0, 2200.0, None))
+        return (q, lambda e: e.dma_start(out, in_), rd, wr, s, 16, 60.0, 2200.0, None)
+
+    def out_(dst, src, q="sy"):
+        return dma(q, dst, src[0], "out", [src[1]], [])
+
+    def gi(out, pat, base, cm):
+        d = 130 + 2 * CY * size(out)
+        if SCRATCH[out[1][0]][2] != i32:
+            return op("gq", lambda e: e.iota(out[0], pat, base, cm, allow_small_or_imprecise_dtypes=True), out, dur=d)
+        return op("gq", lambda e: e.iota(out[0], pat, base, cm), out, dur=d)
+
+    def gs(out, x, pat, cmp_, base, cm, fill=0.0):
+        return op("gq", lambda e: e.affine_select(out[0], x[0], pat, cmp_, fill, base, cm), out, x, dur=170 + 2 * CY * size(out))
 
     sent = [0]
     nxt, prv = T.cores[(rank + 1) % N], T.cores[(rank - 1) % N]
+    ein = len(topo.engines(prv, core)[:8])
 
-    def send(dst, src, s, outap, in_, lreg):
-        rid, pid = topo.addr(dst, core)
-        en = topo.engines(core, dst)[:8]
+    def send(i):
+        rid, pid = topo.addr(nxt, core)
+        en = topo.engines(core, nxt)[:8]
         sent[0] += len(en)
-        return give(("gq", lambda e: e.remote_dma(outap, in_[0], sem[s], sem.sent, pid, rid, sum(1 << x for x in en)), [in_[1]], [], None, 0, 1000.0, 0.0,
-                     lambda t: note("rem", [], [lreg], s, len(topo.engines(src, core)[:8]), {}, t + SHIP - 1000)))
+        s, src, dst = "a%d%d" % (i // 2 + 1, i % 2), c("MS", 384 * i, 384 * i + 384), c("ML", 384 * i + 768, 384 * i + 1152)
+        return ("gq", lambda e: e.remote_dma(dst[0], src[0], sem[s], sem.sent, pid, rid, sum(1 << x for x in en)), [src[1]], [], None, 0, 1000.0, 0.0,
+                lambda t: note("rem", [], [dst[1]], s, ein, {}, t + SHIP - 1000))
 
-    dma("sy", T.NM[:, :], T.nm[:, :], "dm0", [], [("NM", 0, 256)])
-    dma("sy", T.PR[:, :], T.pr[:, :], "dm1", [], [("PR", 0, 256)])
-    dma("sy", T.ZL[:, 0:256], T.z0[:, :], "dm2", [], [("ZL", 0, 256)])
-    dma("sy", T.TH[:, :], T.th[:, :], "dm3", [], [("TH", 0, 5)])
-    dma("s", T.X[:, 0:2048], T.xt[:, :], "dx0", [], [("X", 0, 2048)])
-    ms(c("ONE"), 1.0)
-
-    def gi(out, pat, base, cm, flag=False):
-        if flag:
-            op("gq", lambda e: e.iota(out[0], pat, base, cm, allow_small_or_imprecise_dtypes=True), out)
-        else:
-            op("gq", lambda e: e.iota(out[0], pat, base, cm), out)
-
-    def gs(out, a, pat, cmp_, base, cm):
-        op("gq", lambda e: e.affine_select(out[0], a[0], pat, cmp_, 0.0, base, cm), out, a)
-
-    gi(c("PI"), [[0, 32]], 0, 1)
-    gi(c("DJ"), [[-1, 128]], 128, 1)
-    gs(c("BOa"), c("ONE"), [[-16, 8], [0, 16]], A.is_ge, 0, 1)
-    gs(c("BO"), c("BOa"), [[16, 8], [0, 16]], A.is_ge, 15, -1)
-    gs(c("If"), c("ONE"), [[-1, 128]], A.is_equal, 0, 1)
-    L3 = lambda b, s: (T[b][:, s], (b, s * 256, s * 256 + 256))
-    Lh = lambda b, s, h: (T[b][:, s, h, :], (b, s * 256 + h * 128, s * 256 + h * 128 + 128))
     half = lambda b, h, n=128: c(b, h * n, h * n + n)
     col = lambda j: c("COL", j, j + 1)
-    for h in range(2):
-        cp(Lh("LL", 0, h), half("NM", h))
-    ts(c("PI2"), c("PI", 0, 16), 15, None, A.bitwise_and)
-    u0 = c("PI2", 0, 1)
-    ts(c("DJ"), c("DJ"), 15, None, A.bitwise_and)
-    ts(c("DD"), c("DJ"), 0, None, A.is_equal)
-    cp(c("BOh"), c("BO"))
-    ts(c("NQH"), c("NM"), -2048, None, A.add)
-    ts(c("PT"), c("PR"), -1, 15, A.mult, A.add)
-    gi(c("KR"), [[0, 24], [-1, 16]], 15, 0, True)
-    gi(c("RLi"), [[1, 24]], 0, 0)
-    gi(c("JI"), [[16, 8]], 0, 0)
-    for x4 in range(2):
-        gs((T.PX[:, x4, :], ("PX", x4 * 64, x4 * 64 + 64)), c("ONE", 0, 64), [[-32, 4], [-1, 16]], A.is_equal, -16 * x4, 1)
-    for t in range(1, N):
-        send(T.cores[(rank + t) % N], T.cores[(rank - t) % N], "l%d" % t, T.LL[:, t, :, :], L3("LL", 0), ("LL", t * 256, t * 256 + 256))
-    sset = lambda t: 0 if t % N == 0 else 1 + t % 2
-    ms(c("KC", 0, 1), 1.0)
-    late[0] = True
-    Ib, IND = c("II", 0, 128), c("BOb", 0, 128, 16)
+    msg = lambda b, i, k: c(b, 384 * i + 128 * k, 384 * i + 128 * k + 128)
+    Ib, nI, IND, u0 = c("Ib"), c("nI"), a("BO", T.BO[:, :, 0]), c("PI2", 0, 1)
+    CS = lambda b, s: a(b, T[b][:, 0, 15 - s:143 - s])
+    DS = lambda b, s: a(b, T[b][:, 1, 15 - s:143 - s])
+    SEL14 = c("SEL", 0, 128)
 
-    def statics(t):
-        if t == 3:
-            yield ("need", ("state", 1, 1))
-        if t:
-            yield ("need", ("sel", t - 1, 0))
-        yield ("need", "col")
-        s, ll = sset(t), L3("LL", t % N)
-        yield act(L3("OO", s), ll, F.Identity, bias=col(5), scale=16.0)
-        yield act(L3("A1", s), ll, F.Copy, bias=352.0)
-        yield act(L3("B1", s), ll, F.Copy, bias=1184.0)
-        for j, (w, k) in enumerate(((3232, 352), (2400, 1184))):
-            yield act((T.SXY[:, s, :, j, :], ("SXY", s * 512, s * 512 + 512)), ll, F.Copy, bias=float(w * k - 2 ** 23 - 13024 * 32), scale=float(w))
-        yield ("done", ("statics", t))
+    for d in (dma("sy", T.PR[:, :], T.pr[:, :], "dm1", [], [("PR", 0, 256)]), dma("sy", T.NM[:, :], T.nm[:, :], "dm0", [], [("NM", 0, 256)]),
+              dma("sy", T.Z0[:, :], T.z0[:, :], "dm2", [], [("Z0", 0, 256)]), dma("sy", T.TH[:, :], T.th[:, :], "dm3", [], [("TH", 0, 5)]),
+              dma("s", T.X[:, 0:2048], T.xt[:, :], "dx0", [], [("X", 0, 2048)]),
+              ms(c("ONE"), 1.0), gi(c("PI"), [[0, 16]], 0, 1),
+              gs(c("BOa"), c("ONE"), [[-16, 8], [0, 16]], A.is_ge, 0, 1), gs(a("BO"), c("BOa"), [[16, 8], [0, 16]], A.is_ge, 15, -1),
+              gs(c("LT"), a("BO"), [[1, 128]], A.is_gt, 0, -1), gs(a("If"), c("ONE"), [[-1, 128]], A.is_equal, 0, 1),
+              gi(c("KC", 0, 16), [[-1, 16]], 0, 0), gi(c("KC", 16, 32), [[-16, 16]], 0, 0),
+              ts(c("PI2"), c("PI"), 15, None, A.bitwise_and),
+              ts(col(0), u0, 1, 0, A.mult, A.add), ts(col(1), u0, 16, -240, A.mult, A.add),
+              ts(col(2), u0, 16 - 2.0 ** -16, -240 + 0.5 + 15 * 2.0 ** -16, A.mult, A.add),
+              ms(a("Zf"), 0.0), cp(a("Zf", T.Zf[:, 0, 15:143:16]), IND), cp(a("Zf", T.Zf[:, 1, 15:143:16]), IND),
+              ts(a("Zf", T.Zf[:, 1, 14:142:16]), IND, -1, None, A.mult), cp(a("Zb"), a("Zf")),
+              act(Ib, a("If"), F.Copy), act(c("I2"), a("If"), F.Copy, scale=2.0), act(c("I14"), a("If"), F.Copy, scale=14.0),
+              act(c("Im"), a("If"), F.Copy, scale=2.0 ** -12), act(a("Z4"), a("Zf"), F.Copy, scale=4096.0)):
+        do(d)
 
-    def rows_out():
-        for k in range(16):
-            b = 512 * (k % 4)
-            yield ts(c("SEL", k * 128, k * 128 + 128), c("BOh"), c("DD", k, k + 1), None, A.mult)
-            if k > 3:
-                yield ("need", ("kept", k - 4))
-            yield mm(c("SB", b, b + 256), c("SEL", k * 128, k * 128 + 128), c("NQH"), True, True)
-            yield ("done", ("row", k))
-
-    def some_masks():
-        for k in range(1, 16, 2):
-            a = c("MA", 256 * (k // 2 % 2), 256 * (k // 2 % 2) + 256)
-            yield ts(c("KC", k, k + 1), u0, 0, k - 15, A.mult, A.add)
-            yield act(a, c("PT"), F.Abs, bias=c("KC", k, k + 1))
-            yield act(c("MB", 256 * (k // 2), 256 * (k // 2) + 256), a, F.Relu, bias=c("KC", 0, 1), scale=-1.0)
-            yield ("done", ("mask", k))
-
-    def names():
-        yield cp(c("Ih"), c("If"))
-        for k in range(16):
-            b = 512 * (k % 4)
-            r = c("PRD", 256 * (k % 2), 256 * (k % 2) + 256)
-            if k % 2:
-                m = c("MB", 256 * (k // 2), 256 * (k // 2) + 256)
-                yield ("need", ("mask", k))
-            else:
-                m = c("MSK", 256 * (k // 2 % 2), 256 * (k // 2 % 2) + 256)
-                yield ts(m, c("PT"), 15 - k, None, A.is_equal)
-            yield ("need", ("row", k))
-            if k:
-                yield last
-            yield tt(r, m, c("SB", b, b + 256), A.mult)
-            yield ("done", ("kept", k))
-            last = mm(c("ST", 0, 256), c("Ih"), r, k == 0, k == 15)
-        yield last
-        yield cp(c("LPi"), c("ST", 0, 256))
-        yield ("done", "names")
+    def consts_g():
+        yield gs(c("PERM"), c("ONE"), [[-2, 64], [1, 2]], A.is_equal, -1, 1)
+        yield ("done", "perm")
+        for x4 in range(2):
+            yield gs(a("PX", T.PX[:, x4, :]), c("ONE", 0, 64), [[-32, 4], [-1, 16]], A.is_equal, -16 * x4, 1)
+        yield ("done", "px")
+        yield ("need", "sel")
+        for o, s, k in (("SXY", "SXa", (3232.0, 2400.0)), ("D12", "SEL", (-1.0, -1.0))):
+            for q in range(2):
+                yield gs(half(o, q), half(s, q), [[-1, 128]], A.not_equal, 0, 1, k[q])
+        yield ("done", "sxy")
+        yield gi(a("CKi"), [[0, 8], [16, 2], [1, 14]], 1, 0)
+        yield gi(c("DJ"), [[-1, 128]], 128, 1)
+        yield gi(c("RLi"), [[1, 8]], 0, 0)
+        yield gi(c("JI"), [[16, 8]], 0, 0)
+        yield ("need", "mv")
+        yield gi(c("MV", 1, 15), [[2, 7], [-1, 2]], 1, 0)
+        yield gi(c("MV", 17, 31), [[1, 14]], 0, 0)
+        yield gi(c("MV", 49, 63), [[2, 7], [-1, 2]], 1, 0)
+        yield ("done", "iotas")
 
     def consts():
-        yield ts(col(0), u0, 1, 0, A.mult, A.add)
-        yield ts(col(1), u0, -1, 15, A.mult, A.add)
-        yield ts(col(5), u0, -1, 15 - 32768, A.mult, A.add)
-        yield ("done", "col")
-        yield ts(c("FMG"), c("PT"), col(1), None, A.is_equal)
+        yield ms(c("MV"), 15)
+        yield ("done", "mv")
+        yield ts(col(5), u0, 4096, -63488, A.mult, A.add)
+        yield act(half("CAB", 0), c("ONE"), F.Copy, scale=col(5))
+        yield ms(half("CAB", 1), -15 / 32)
+        yield ("done", "cab")
         for q in range(2):
-            yield act(c("II", q * 128, q * 128 + 128), c("If"), F.Copy)
-        yield ts(col(3), u0, -1, 16, A.mult, A.add)
-        yield ts(col(4), u0, 1, 1, A.mult, A.add)
-        for q in range(2):
-            yield act(c("KDF", q * 128, q * 128 + 128), c("If"), F.Copy, scale=col(3 + q))
-        yield ms(c("D0"), 0.0)
-        yield ms(c("D0", 0, 256, 16), -1e9)
-        yield cp(c("RL"), c("RLi"))
-        yield act(c("BOb"), c("BO"), F.Copy)
-        yield ms(c("CM"), -128.0)
-        yield ms(c("M3"), 0)
-        yield ms(c("NC"), 0.0)
-        yield ms(c("AT"), 0.0)
-        yield ms((T.PM[:, :, :, :, :], ("PM", 0, 512)), 0.0)
+            yield ts(col(3 + q), u0, 14 + q, None, A.is_equal)
+            yield act(half("SEL", q), a("BO"), F.Copy, scale=col(3 + q))
+        yield ("need", "perm")
+        yield act(half("SXa", 0), c("PERM"), F.Copy, scale=2400.0)
+        yield act(half("SXa", 1), SEL14, F.Copy, scale=3232.0)
+        yield ("done", "sel")
+        yield ms(a("PM"), 0.0)
+        yield ("need", "px")
         for i in range(4):
-            yield cp((T.PM[:, i, :, i % 2, :], ("PM", i * 128, i * 128 + 128)), (T.PX[:, i // 2, :], ("PX", 64 * (i // 2), 64 * (i // 2) + 64)))
-        yield act(c("nI"), c("If"), F.Copy, scale=-1.0)
-        yield ms(c("COL", 15, 16), 128.0)
-        yield ("done", "consts")
+            yield cp(a("PM", T.PM[:, i, :, i % 2, :]), a("PX", T.PX[:, i // 2, :]))
+        yield ms(c("NC"), 0.0)
+        yield ("done", "pm")
         yield cp(c("X", 2048, 2112), c("X", 0, 64))
-        yield ("done", ("table", -1, 0))
-        yield ("done", ("table", -1, 1))
-        yield ("need", ("H", 0, 0))
         for h in range(2):
-            yield cp(c("PK", h * 512 + 384, h * 512 + 512), half("PT", h))
-        yield act(c("PN"), c("If"), F.Copy, scale=-2.0 ** 25)
-        yield ts(c("RX", 0, 8), IND, -512, None, A.mult)
-        yield ts(c("RX", 8, 16), IND, 512, None, A.mult)
-        yield ts(col(2), u0, -16, 240, A.mult, A.add)
-        for q in range(2):
-            yield act(c("KD", q * 128, q * 128 + 128), c("If"), F.Copy, scale=col(2))
-            yield ms(c("C2", q * 128, q * 128 + 128), (2.0 ** 20, 256.0)[q])
-        yield ms(c("OB"), 1.0)
-        yield ms(c("O5"), 512.0)
+            yield cp(msg("ML", h, 0), half("Z0", h))
+        yield act(nI, a("If"), F.Copy, scale=-1.0)
+        yield ms(col(15), 128.0)
+        yield ("done", ("table", -2))
+        yield ("done", ("table", -1))
+
+    def consts2():
+        yield ("need", "pm")
+        for n, k in enumerate((1.0, 2.0, -1.0)):
+            for q, w in enumerate((512 * BIG, -512.0)):
+                yield act(a("RX", T.RX[:, n, :, q]), IND, F.Copy, scale=k * w)
+        yield act(c("RY"), IND, F.Copy, scale=-512 * BIG)
+        for q, w in enumerate((512 * BIG, 512.0)):
+            yield act(a("KR", T.KR[:, :, q, :]), a("If", T.If[:, :, 0:14]), F.Copy, scale=w)
+        yield ms(c("OB", 0, 128), 1.0)
+        yield ms(c("OB", 128, 256), 32 * BIG)
+        yield ms(a("TM"), 0.0)
         yield ts(c("COL", 8, 13), c("TH"), -1, -1, A.mult, A.add)
         for t in range(TS):
-            yield ts(c("THD", t * 128, t * 128 + 128), c("Ih"), col(8 + t), None, A.mult)
-        yield ("done", ("scan", -1, 1))
-        yield ts(c("PI2", 2, 4), c("PI", 0, 2), 7, None, A.bitwise_and)
-        yield cp(c("RM"), c("PI2", 2, 4))
-        yield act(c("M8"), c("DD"), F.Copy, scale=-8.0)
-        yield act(c("M1"), c("DD"), F.Copy)
-        yield ts(c("JC"), c("JI"), col(0), None, A.add)
-        yield ts(c("J8"), c("JC"), 8, None, A.mult)
+            yield ts(a("TM", T.TM[:, t, :, 0, :]), a("BO", T.BO[:, :, 0:14]), col(8 + t), None, A.mult)
+        yield ("need", "iotas")
+        for q, w in enumerate((BIG, 1.0)):
+            yield ts(a("CK", T.CK[0:32, :, q, :]), a("CKi", T.CKi[0:32, :, q, :]), w / 32, None, A.mult)
+            yield ms(a("CK", T.CK[32:64, :, q, :]), 7.5 * w)
+            yield ms(a("CK", T.CK[64:128, :, q, :]), 8064.0 * q)
+        yield ("done", ("scan", -1))
+        yield ms(c("D0"), 0.0)
+        yield ms(c("D0", 0, 224, 28), -2.0 ** 60)
+        yield cp(c("RL"), c("RLi"))
+        yield ts(c("DJ"), c("DJ"), 15, None, A.bitwise_and)
+        yield ts(c("M1"), c("DJ"), 0, None, A.is_equal)
+        yield ts(c("JC", 0, 8), c("JI"), col(0), None, A.add)
+        yield ms(c("JC", 8, 16), 0.0)
+        yield ms(c("JC", 16, 24), 32.0)
+        yield ts(c("J8", 0, 8), c("JC", 0, 8), 8, None, A.mult)
+        yield ms(c("J8", 8, 16), -3.5)
+        for q, w in enumerate((128.0, 1.0, 1.0)):
+            yield act(half("IN3", q, 8), IND, F.Copy, scale=w)
+        yield ts(c("OH"), c("MV"), col(0), None, A.is_equal)
+        yield act(c("BOb"), a("BO"), F.Copy)
+        for q in range(2):
+            yield tt(half("A12", q), a("If"), CS("Zf", 14 + q), A.subtract)
+        for h in range(2):
+            for lo, hi in ((0, 128), (1920, 2176), (3968, 4096)):
+                yield ms(c("WW", 4096 * h + lo, 4096 * h + hi), 0.0)
         yield ("done", "rest")
+        yield ts(col(6), u0, 14, -16, A.is_lt, A.mult)
+        yield ts(col(7), col(6), -1, -272, A.mult, A.add)
+        yield act(half("WP", 0), c("PERM"), F.Copy, scale=col(6))
+        yield act(half("WP", 1), a("If"), F.Copy, scale=col(7))
+        yield ("done", "wp")
 
-    def masks(rows, P, i):
-        return tt(c(P, i * 512, i * 512 + 384), ind(rows, c("RL")), c("KR"), A.is_equal)
+    def cuts(key, w, R, n, step, ss, on_v):
+        yield ("need", key)
+        for s in ss:
+            r = c(R, 256 * s + n, 256 * s + n + size(w))
+            if on_v:
+                yield ts(r, w, -step * s, 0, A.add, A.max)
+            else:
+                yield act(r, w, F.Relu, bias=c("KC", s + (16 if step > 1 else 0), s + (17 if step > 1 else 1)))
+            yield ("done", (key, s))
 
-    def new_f(h, s, P, i):
-        yield mm(c("ST", 128, 256), c(P, i * 512 + 128, i * 512 + 256), Ib, True, True)
-        yield tt(c("MaL"), c("ST", 128, 256), Lh("LL", s[0], h), A.mult)
-        yield [mm(c("ST", 384, 512), c("BO"), c("MaL"), True, False), mm(c("ST", 384, 512), c("BOb"), c("CM"), False, True)]
-        yield tt(c("ST", 128, 256), c("ST", 384, 512), Lh("B1", s[1], h), A.mult)
+    def gather_cuts(key, out, Z, w, R, n, more):
+        yield ("need", key)
+        yield [mm(out, CS(Z, 0), w, True, False)] + [mm(out, l, r, False, False) for l, r in more]
+        for s in range(1, 16):
+            yield ("need", (key, s))
+            yield mm(out, DS(Z, s), c(R, 256 * s + n, 256 * s + n + size(w)), False, s == 15)
 
-    def names_to_H(h, s, H, i):
-        yield tt(c("ST", 0, 128), Lh("A1", s[1], h), half("LPi", h), A.mult)
-        q = s[1] * 512 + h * 256
-        yield tt(c("QQ"), c("ST", 0, 256), (T.SXY[:, s[1], h, :, :], ("SXY", s[1] * 512, s[1] * 512 + 512)), A.add)
-        yield ts(c("HB"), c("QQ"), 65535, 5, A.bitwise_and, A.logical_shift_right)
-        yield cp(c("HF"), c("HB"))
-        yield op("v", lambda e: e.transpose(T[H][:, i, :, :], T.HF[:, :]), (None, (H, i * 256, i * 256 + 256)), c("HF"), dur=190.0)
+    def split(o, b, i):
+        yield ts(msg(b, i, 1), o, M1_, -M1_, A.add, A.add)
+        yield tt(msg(b, i, 2), o, msg(b, i, 1), A.subtract)
 
-    def first_state(h):
-        if h:
-            yield ("need", ("state", -1, 0))
-        else:
-            for k in ("consts", "names", ("statics", 0)):
-                yield ("need", k)
-        yield mm(c("ST", 0, 256), half("FMG", h), c("KDF"), True, True)
-        sc, r = h * 256, h * 160
-        yield ts(c("T1", 0, 128), half("LPi", h), 16, None, A.mult)
-        yield tt(c("RI", r, r + 128), c("T1", 0, 128), half("PT", h), A.add)
-        yield scan(c("SC", sc, sc + 256), c("ST", 0, 256))
-        yield ts(c("M3", h * 24 + 8, h * 24 + 16), c("SC", sc + 15, sc + 128, 16), -1, None, A.add)
-        yield ts(c("M3", h * 24 + 16, h * 24 + 24), c("SC", sc + 143, sc + 256, 16), -1, 16, A.mult, A.add)
-        yield masks(c("M3", h * 24, h * 24 + 24), "PK", h)
-        for x in new_f(h, (0, 0), "PK", h):
+    def slots():
+        for q, o in enumerate((A.is_gt, A.is_equal)):
+            yield ts(half("MK", q, 256), c("PR"), col(0), None, o)
+        yield group(c("SB", 0, 512), (c("LT"), c("MK", 0, 512)))
+        yield ts(c("P16"), c("PR"), 16, None, A.mult)
+        yield tt(c("AA"), c("SB", 0, 512), c("MK", 0, 512), A.mult)
+        yield group(c("SB", 512, 768), (Ib, c("P16")), (c("I14"), half("MK", 1, 256)), (c("I2"), half("AA", 0, 256)), (Ib, half("AA", 1, 256)))
+        yield ts(half("MK", 2, 256), c("PR"), col(0), None, A.is_lt)
+        yield ts(c("NQ"), c("NM"), -2048, None, A.add)
+        yield cp(c("W1"), c("SB", 512, 768))
+        yield ("done", "w1")
+        for x in gather_cuts("w1", c("SB", 1024, 1280), "Zb", c("W1"), "R1", 0,
+                             [(c("I2"), half("AA", 0, 256)), (Ib, half("MK", 2, 256)), (c("Im"), c("NQ"))]):
             yield x
-        for x in names_to_H(h, (0, 0), "HL", h):
-            yield x
-        yield ("done", ("H", 0, h))
-        for e in (128, 152):
-            yield cp(c("RI", r + e, r + e + 8), c("M3", h * 24 + 16, h * 24 + 24))
-        for k in ("p", "r", "z"):
-            yield ("done", (k, 0, h))
-        yield ("done", ("state", -1, h))
+        yield ts(c("W2"), c("SB", 1024, 1280), col(2), None, A.add)
+        yield ("done", ("w2", 0))
+        yield ("done", ("w2", 1))
 
-    def lists(t, h):
-        i = t * 2 + h
-        yield ("need", ("H", t, h))
-        yield ("need", ("scan", t - 1, 1))
-        if h:
-            yield ("need", ("L", t, 0))
+    def first(h):
+        o = c("TL", 128, 256) if h else c("KP", 0, 128)
+        yield ("need", "cab")
+        for x in gather_cuts(("w2", h), o, "Z4", half("W2", h), "R2", 128 * h, [(Ib, half("CAB", 0)), (Ib, half("CAB", 1))]):
+            yield x
+        for x in split(o, "ML", h):
+            yield x
+        yield ("done", ("m", h))
+
+    def columns(i):
+        h = i % 2
+        nm_ = msg("ML", i, 1)
+        for k in (("m", i), "sxy", ("st0", i - 1)):
+            yield ("need", k)
+        yield group(c("ST", 0, 128), (c("PERM"), nm_)) + group(c("ST", 128, 256), (SEL14, nm_)) + \
+            group(c("ST", 256, 384), (half("SXY", 0), nm_)) + group(c("ST", 384, 512), (half("SXY", 1), nm_))
+        for q in range(2):
+            yield tt(half("PP", 2 * h + q), half("ST", q), nm_, A.mult)
+        yield tt(half("QQ", h, 256), c("ST", 256, 512), half("PP", h, 256), A.add)
+        yield ("done", ("st0", i))
+        yield ts(half("HB", h, 256), half("QQ", h, 256), 65535, 5, A.bitwise_and, A.logical_shift_right)
+        yield cp(half("HF", h, 256), half("HB", h, 256))
+        ht = (T.HT[:, h], ("HT", h, h + 1))
+        yield op("v", lambda e: e.transpose(ht[0], half("HF", h, 256)[0]), ht, half("HF", h, 256), dur=FIX + CY * 128)
+        yield ("need", ("L", i - 1))
+        yield ("need", "pm")
         for ib in range(4):
             p = []
             for x4 in range(2):
                 for g2 in range(2):
                     w = ib * 32 + g2 * 16
-                    p.append(mm((T.HR[:, :, 2 * ib + x4:128:8], ("HR", 0, 1)), (T.PM[:, 2 * x4 + g2], ("PM", 0, 512)),
-                                (T.HL[:, i, :, w:w + 16], ("HL", i * 256, i * 256 + 256)), g2 == 0, g2 == 1))
+                    p.append(mm(a("HR", T.HR[:, :, 2 * ib + x4:128:8]), a("PM", T.PM[:, 2 * x4 + g2]), (T.HT[:, h, :, w:w + 16], ht[1]), g2 == 0, g2 == 1))
             yield p
-        yield ("need", ("nc", t))
-        if h == 0:
-            yield ("need", ("g", t - 1, 0))
-        yield ts(c("OFF", h * 256, h * 256 + 256), (T.HR[:, :, :], ("HR", 0, 1)), c("NC", t, t + 1), None, A.add)
-        yield ("done", ("L", t, h))
+        yield ("need", ("nc", i // 2))
+        yield ts(half("OFF", h, 256), a("HR"), c("NC", i // 2, i // 2 + 1), None, A.add)
+        yield ("done", ("L", i))
+
+    def gaps(i):
+        for k in (("m", i), "sxy", ("dl", i - 1)):
+            yield ("need", k)
+        yield sum([group(c("ST", 512 + 128 * q, 640 + 128 * q), (half("D12", q), msg("ML", i, 1)), (half("D12", q), msg("ML", i, 2))) for q in range(2)], [])
+        yield act(half("DL", i % 2, 256), c("ST", 512, 768), F.Copy)
+        yield ("done", ("dl", i))
 
     XW = c("X", 0, 2112)
+    cut = lambda lo, hi: [(s, min(4, hi - s)) for s in range(lo, hi, 4)]
+    SCH = [(1,) + x for x in cut(0, 14)] + [(0,) + x for x in cut(NV, 14)]
+    rec = lambda h, y, s, n: c("WW", 4096 * h + 128 * (s + 1 + 16 * (1 - y)), 4096 * h + 128 * (s + n + 1 + 16 * (1 - y)))
+    tmp = lambda b, h, s, n: c(b, 2048 * h + 128 * s, 2048 * h + 128 * (s + n))
+    offs = lambda h, y, s, n: c("OFF", 256 * h + 128 * y + 8 * s, 256 * h + 128 * y + 8 * (s + n))
+    raw = lambda h, y, s, n: rec(h, y, s, n) if y else tmp("XR", h, s, n)
+    mag = lambda h, y, s, n: tmp("AY", h, s, n) if y else rec(h, y, s, n)
+    left = {}
 
-    def raw(h, j):
-        return c("WW", h * 4096 + 512 * j, h * 4096 + 512 * j + 512) if j < 4 else c("XR", h * 2048 + 512 * (j - 4), h * 2048 + 512 * (j - 4) + 512)
+    def ready(i):
+        t = i // 2
+        for k in (("L", i), ("table", 2 * t - 2), ("table", 2 * t - 1)):
+            yield ("need", k)
 
-    def gathers(t, h):
-        yield ("need", ("L", t, h))
-        yield ("need", ("table", t - 1, 0))
-        yield ("need", ("table", t - 1, 1))
-        if h:
-            yield ("need", ("g", t, 0))
-        for j in range(8):
-            o = h * 256 + (128 + 32 * j if j < 4 else 32 * (j - 4))
-            w = ind(XW, c("OFF", o, o + 32))
-            a = act(raw(h, j), w, F.Copy, bias=-128.0 if j < 4 else 0.0)
-            if j < 4:
-                yield a
-            else:
-                yield ("alt", a, cp(raw(h, j), w))
-            yield ("done", ("g", t, h, j))
-        yield ("done", ("g", t, h))
+    def gather_s(i):
+        for x in ready(i):
+            yield x
+        yield ("need", ("gs", i - 1))
+        for j, (y, s, n) in enumerate(SCH):
+            yield act(raw(i % 2, y, s, n), ind(XW, offs(i % 2, y, s, n)), F.Copy, bias=-128.0 * y)
+            yield ("done", ("g", i, j))
+        yield ("done", ("gs", i))
 
-    def minus_z(t, h):
-        i = t * 2 + h
-        yield ("need", ("z", t, h))
-        for j in range(8):
-            b, J = 512 * (j % 4), i * 8 + j - 4
-            yield ("need", ("g", t, h, j))
-            if J >= 0:
-                yield ("need", ("abs", J))
-            yield [mm(c("SB", b, b + 512), Ib, raw(h, j), True, False)] + \
-                [mm(c("SB", b + 128 * r, b + 128 * r + 128), c("nI"), c("ZL", i * 128, i * 128 + 128), False, r == 3) for r in range(4)]
-            yield ("done", ("d", t, h, j))
+    def gather_v(i):
+        h = i % 2
+        for x in ready(i):
+            yield x
+        yield ("need", ("gv", i - 1))
+        for s, n in cut(0, NV):
+            for k in range(s, s + n):
+                yield tt(rec(h, 0, k, 1), ind(XW, offs(h, 0, k, 1)), msg("ML", i, 0), A.subtract)
+            if s + n == NV:
+                yield ("done", ("gv", i))
+            yield ts(tmp("RU", h, s, n), rec(h, 0, s, n), 0, None, A.max)
+            yield ("done", ("ru", i, s))
 
-    def absval(t, h):
-        for j in range(8):
-            yield ("need", ("d", t, h, j))
-            b, w = 512 * (j % 4), h * 4096 + 2048 + 512 * (j - 4)
-            if j < 4:
-                yield act(c("AY", h * 2048 + 512 * j, h * 2048 + 512 * j + 512), c("SB", b, b + 512), F.Abs, bias=c("COL", 15, 16))
-            else:
-                yield act(c("WW", w, w + 512), c("SB", b, b + 512), F.Abs)
-            yield ("done", ("abs", (t * 2 + h) * 8 + j))
+    def minus_z(i):
+        for j, (y, s, n) in enumerate(SCH):
+            J = i * len(SCH) + j
+            b = 512 * (J % 3)
+            yield ("need", ("g", i, j))
+            yield ("need", ("abs", J - 3))
+            yield [mm(c("SB", b, b + 128 * n), Ib, raw(i % 2, y, s, n), True, False)] + \
+                [mm(c("SB", b + 128 * r, b + 128 * r + 128), nI, msg("ML", i, 0), False, r == n - 1) for r in range(n)]
+            yield ("done", ("d", J))
 
-    def sums(t, h):
-        i = (t * 2 + h) * 512
-        yield ("need", ("scan", t - 1 + h, 1 - h))
-        yield ("need", ("p", t, h))
-        kp = c("KP", 0, 256)
-        yield [mm(kp, Ib, c("C2"), True, False), mm(kp, c("OB"), c("KD"), False, False),
-               mm(c("KP", 128, 256), c("O5"), c("THD", t * 128, t * 128 + 128), False, False)]
-        yield [mm(kp, c("PK", i + 384, i + 512), c("II"), False, False)] + \
-            [mm(c("KP", q * 128, q * 128 + 128), c("PN"), c("PK", i + j, i + j + 128), False, False) for q in range(2) for j in (128, 256)]
-        for j in range(8):
-            yield ("need", ("abs", (t * 2 + h) * 8 + j))
-            p = []
-            for k in range(4 * (j % 4), 4 * (j % 4) + 4):
-                if j < 4:
-                    p.append(mm(c("KP", 128 + k, 256, 16), c("AY", h * 2048 + k * 128, h * 2048 + k * 128 + 128), c("RX", 0, 8), False, False))
-                else:
-                    w = h * 4096 + 2048 + k * 128
-                    p.append(mm(c("KP", k, 256, 16), c("WW", w, w + 128), c("RX"), False, k == 15))
-            yield p
-        yield ("done", ("sums", t, h))
+    def absval(i):
+        for j, (y, s, n) in enumerate(SCH):
+            J = i * len(SCH) + j
+            b = 512 * (J % 3)
+            yield ("need", ("d", J))
+            yield act(mag(i % 2, y, s, n), c("SB", b, b + 128 * n), F.Abs, bias=col(15) if y else 0.0)
+            yield ("done", ("abs", J))
 
-    def choose(t, h):
-        sc, e, i = h * 256, (t * 2 + h) * 32, t * 2 + h
-        yield ("need", ("sums", t, h))
-        yield scan(c("SC", sc, sc + 256), c("KP", 0, 256))
-        yield ("done", ("scan", t, h))
-        yield ("need", "rest")
-        mS, mD = c("SC", sc + 143, sc + 256, 16), c("SC", sc + 15, sc + 128, 16)
-        m, a, sel = c("TM", h * 16, h * 16 + 8), c("TM", 32 + h * 16, 40 + h * 16), c("SE", h * 8, h * 8 + 8)
-        yield ts(m, mS, 0, 2 ** 21, A.is_ge, A.mult)
-        yield tt(a, m, mS, A.add)
-        yield tt(sel, a, mD, A.max)
-        yield ts(half("KQ", h, 8), sel, 0x1F0, None, A.bitwise_and)
-        yield tt(half("GMx", h), ind(half("KQ", h, 8), c("RL", 0, 8)), c("M8"), A.mult)
-        yield [mm(c("TL", 0, 8), Ib, c("JC"), True, False), mm(c("TL", 0, 8), half("GMx", h), IND, False, True)]
-        yield ts(c("ES", e, e + 32), ind(sel, c("RM")), 2 ** 21, None, A.is_lt)
-        yield ("done", ("sel", t, h))
-        yield ts(half("LS", h, 8), c("TL", 0, 8), 3968, None, A.add)
-        yield act(half("AW", h), ind(half("WW", h, 4096), half("LS", h, 8)), F.Abs)
-        z, zn = c("ZL", i * 128, i * 128 + 128), c("ZN", i * 128, i * 128 + 128)
-        yield tt(half("SZ", h), ind(half("WW", h, 4096), half("LS", h, 8)), z, A.add)
+    def keys(i):
+        left[i] = [28 + NV]
+        kp = c("KP", 0, 224)
+        for k in (("scan", i - 1), ("m", i)):
+            yield ("need", k)
+        yield [mm(kp, half("OB", 0), a("CK"), True, False), mm(kp, half("OB", 1), a("TM", T.TM[:, i // 2]), False, False),
+               mm(kp, msg("ML", i, 2), a("KR"), False, False)]
+        yield ("done", ("k0", i))
+        for j, (y, s, n) in enumerate(SCH):
+            yield ("need", ("abs", i * len(SCH) + j))
+            yield [mm(c("KP", k, 224, 28 if y else 14), mag(i % 2, y, k, 1), c("RY") if y else a("RX", T.RX[:, 0]), False, left[i]) for k in range(s, s + n)]
+        yield ("done", ("ks", i))
+
+    def keys_v(i):
+        yield ("need", ("k0", i))
+        for s, n in cut(0, NV):
+            yield ("need", ("ru", i, s))
+            yield [mm(c("KP", k, 224, 14), x, a("RX", T.RX[:, q]), False, left[i]) for k in range(s, s + n)
+                   for q, x in ((2, rec(i % 2, 0, k, 1)), (1, tmp("RU", i % 2, k, 1)))]
+        yield ("done", ("kv", i))
+
+    def choose(i):
+        t, h = i // 2, i % 2
+        for k in (("ks", i), ("kv", i), "rest"):
+            yield ("need", k)
+        sc = half("SC", h, 224)
+        yield op("v", lambda e: e.tensor_tensor_scan(sc[0], T.D0[:, :], T.KP[:, 0:224], 0.0, A.add, A.max), sc, c("D0"), c("KP", 0, 224), dur=FIX + CY * 224)
+        yield ("done", ("scan", i))
+        w = c("SC", 224 * h + 27, 224 * h + 224, 28)
+        yield ts(half("FF", h, 8), w, BIG, 1 / BIG, A.is_lt, A.max)
+        yield tt(half("SE", h, 8), w, half("FF", h, 8), A.mult)
+        yield ts(half("KQ", h, 8), half("SE", h, 8), 31, None, A.bitwise_and)
+        yield tt(half("GM", h), ind(half("KQ", h, 8), c("RL")), c("M1"), A.mult)
+        yield ("need", ("m", 1))
+        yield ("lock", "TL")
+        yield group(c("TL", 0, 24), (Ib, c("JC")), (half("GM", h), c("IN3")))
+        yield cp(half("LS", h, 24), c("TL", 0, 24))
+        yield ("unlock", "TL")
+        yield ("done", ("LS", i))
+        pick = ind(half("WW", h, 4096), c("LS", 24 * h, 24 * h + 8))
+        zn = half("ZO", h) if t + 1 == TS else msg("MS", i, 0)
+        yield act(half("AW", h), pick, F.Abs)
+        yield tt(half("SZ", h), pick, msg("ML", i, 0), A.add)
         yield ts(half("HZ", h), half("SZ", h), 0.5, 63.75, A.mult, A.add)
         yield tt(zn, half("HZ", h), half("AW", h), A.min)
-        if t + 1 < TS:
-            n = (i + 2) * 128
-            yield send(nxt, prv, "az%d%d" % (t + 1, h), T.ZL[:, n:n + 128], zn, ("ZL", n, n + 128))
-            yield ("done", ("z", t + 1, h))
-        yield mm(c("TL", 8, 16), zn, IND, True, True)
-        yield cp(c("UI", h * 16, h * 16 + 8), c("TL", 8, 16))
-        yield ts(c("UI", h * 16 + 8, h * 16 + 16), c("UI", h * 16, h * 16 + 8), 7, None, A.bitwise_and)
-        yield tt(half("GMx", 2 + h), ind(c("UI", h * 16 + 8, h * 16 + 16), c("RL", 0, 8)), c("M1"), A.mult)
-        yield [mm(c("TL", 16, 24), Ib, c("J8"), True, False), mm(c("TL", 16, 24), half("GMx", 2 + h), IND, False, True)]
-        yield cp(half("LC", h, 8), c("TL", 16, 24))
+        yield ("done", ("zn", i))
+        p1, p2 = c("TL", 32, 40), c("TL", 40, 48)
+        zs = lambda k: (zn[0][:, k:128:16] if False else (T.ZO[:, 128 * h + k:128 * h + 128:16] if t + 1 == TS else T.MS[:, 384 * i + k:384 * i + 128:16]), zn[1])
+        yield ("lock", "TL")
+        yield group(p1, (Ib, half("J8", 1, 8)), *[(CS("Zb", k), zs(k)) for k in range(16)])
+        yield ts(half("K8", h, 8), p1, M8_, -M8_, A.add, A.add)
+        yield group(p2, (Ib, half("J8", 0, 8)), *([(CS("Zb", k), zs(k)) for k in range(16)] + [(nI, half("K8", h, 8))]))
+        yield cp(half("LC", h, 8), p2)
+        yield ("unlock", "TL")
         xw = c("X", 1024 * h, 1024 * h + 1024)
         yield tt(half("SX2", h), ind(xw, half("LC", h, 8)), zn, A.add)
         yield ts(half("HX2", h), half("SX2", h), 0.5, -0.25, A.mult, A.add)
-        yield ("need", ("g", t, 1))
+        yield ("need", ("gs", 2 * t + 1))
+        yield ("need", ("gv", 2 * t + 1))
         yield cp(ind(xw, half("LC", h, 8)), half("HX2", h))
-        if h == 0 and t + 1 < TS:
+        if t + 1 == TS:
+            yield out_(T.yx[:, 1024 * h:1024 * h + 1024], xw)
+            yield out_(T.yz[:, 128 * h:128 * h + 128], zn, "s")
+        elif h == 0:
             yield cp(c("X", 2048, 2112), c("X", 0, 64))
-        yield ("done", ("table", t, h))
+        yield ("done", ("table", i))
+
+    def state(i):
+        h = i % 2
+        for k in (("LS", i), ("dl", i), ("st1", i - 1)):
+            yield ("need", k)
+        yield tt(half("TT", h, 256), ind(c("OH"), c("LS", 24 * h + 8, 24 * h + 24)), half("DL", h, 256), A.mult)
+        o = c("ST", 768, 896)
+        yield group(o, (Ib, msg("ML", i, 1)), (Ib, msg("ML", i, 2)), (half("A12", 0), half("TT", 2 * h)), (half("A12", 1), half("TT", 2 * h + 1)))
+        for x in split(o, "MS", i):
+            yield x
+        yield ("done", ("st1", i))
+        if i // 2 + 1 < TS:
+            yield ("need", ("zn", i))
+            yield send(i)
+            yield ("done", ("m", i + 2))
 
     def count(t):
-        yield ("need", ("sel", t, 0))
-        yield ("need", ("sel", t, 1))
-        yield [mm(c("TL", 24, 32), c("OB"), c("ES", j * 32, j * 32 + 8), j == 0, j == 2 * t + 1) for j in range(2 * t + 2)]
-        yield tt(c("DF", 96, 104), c("TL", 24, 32), c("BO", 0, 128, 16), A.mult)
-        yield op("v", lambda e: e.tensor_reduce(T.AT[:, t + 1:t + 2], T.DF[:, 96:104], AxisListType.X, A.add), c("AT", t + 1, t + 2), c("DF", 96, 104), dur=130.0)
+        for h in range(2):
+            yield ("need", ("LS", 2 * t + h))
+            yield ts(half("ES", h, 8), c("LS", 24 * h + 8, 24 * h + 16), 16, None, A.is_ge)
+        p = c("TL", 64, 72)
+        yield ("lock", "TL")
+        yield [mm(p, c("BOb"), half("ES", 0, 8), True, False), mm(c("TL", 64, 65), Ib, c("NC", t, t + 1), False, False), mm(p, c("BOb"), half("ES", 1, 8), False, True)]
+        yield op("v", lambda e: e.tensor_reduce(T.AT[:, t:t + 1], p[0], AxisListType.X, A.add), c("AT", t, t + 1), p, dur=FIX + 64 * CY)
+        yield ("unlock", "TL")
         if t + 1 < TS:
-            yield ts(c("AI", t, t + 1), c("AT", t + 1, t + 2), 1 / 64, -63 / 128, A.mult, A.add)
-            yield ts(c("NC", t + 1, t + 2), c("AI", t, t + 1), -64, c("AT", t + 1, t + 2), A.mult, A.add)
+            yield ts(c("AI", t, t + 1), c("AT", t, t + 1), 1 / 64, -63 / 128, A.mult, A.add)
+            yield ts(c("NC", t + 1, t + 2), c("AI", t, t + 1), -64, c("AT", t, t + 1), A.mult, A.add)
             yield ("done", ("nc", t + 1))
         else:
-            yield tt(c("YE"), c("AT", 1, 6), c("AT", 0, 5), A.subtract)
-            yield out(T.ye[:, :], c("YE"))
-
-    def state(t, h):
-        i, s, d = t * 2 + h, (t % N, sset(t)), 48 * h
-        sel, e, b, j = c("SE", h * 8, h * 8 + 8), i * 32, i * 160 + 128, i * 512
-        yield ("need", ("sel", t, h))
-        yield ("need", ("r", t, h))
-        yield ts(c("RI", b + 8, b + 16), sel, 4, 15, A.logical_shift_right, A.bitwise_and)
-        yield ts(c("RI", b + 16, b + 24), sel, 15, None, A.bitwise_and)
-        yield tt(c("DF", d, d + 24), c("RI", b, b + 24), c("RI", b + 8, b + 32), A.subtract)
-        yield tt(c("DF", d + 24, d + 48), c("DF", d, d + 24), c("ES", e, e + 24), A.mult)
-        yield tt(c("RS", b + 8, b + 32), c("RI", b + 8, b + 32), c("DF", d + 24, d + 48), A.add)
-        yield masks(c("RS", b + 8, b + 32), "PS", i)
-        yield ("need", ("statics", t % N))
-        Qo, Qn, R = c("RI", i * 160, i * 160 + 128), c("RS", i * 160, i * 160 + 128), half("QI2", h)
-        yield tt(R, Qo, Lh("OO", s[1], h), A.add)
-        yield ("need", ("state", t - 1 + h, 1 - h))
-        yield [mm(c("ST", 0, 128), c("PS", j, j + 128), Ib, True, False), mm(c("ST", 0, 128), c("PK", j + 128, j + 256), Ib, False, True)]
-        yield tt(c("UO"), c("ST", 0, 128), Lh("OO", s[1], h), A.mult)
-        yield mm(c("ST", 256, 384), c("BO"), c("UO"), True, True)
-        if t + 1 < TS:
-            for x in new_f(h, s, "PS", i):
-                yield x
-        yield tt(c("R1"), c("ST", 256, 384), R, A.subtract)
-        yield tt(c("ST", 256, 384), c("ST", 0, 128), c("R1"), A.mult)
-        yield tt(Qn, c("ST", 256, 384), Qo, A.add)
-        if t + 1 == TS:
-            yield ts(half("Pi", h), Qn, 15, None, A.bitwise_and)
-            yield ("done", ("state", t, h))
-            return
-        yield ts(half("LPi", h), Qn, 4, None, A.arith_shift_right)
-        for x in names_to_H(h, s, "HN", i):
-            yield x
-        n = i + 2
-
-        def ship(k, outap, inap, reg, lreg):
-            return send(nxt, prv, "a%s%d%d" % (k, t + 1, h), outap, (inap, reg), lreg)
-        yield ship("h", T.HL[:, n, :, :], T.HN[:, i, :, :], ("HN", i * 256, i * 256 + 256), ("HL", n * 256, n * 256 + 256))
-        yield ("done", ("H", t + 1, h))
-        yield ts(half("Pi", h), Qn, 15, None, A.bitwise_and)
-        yield cp(c("PS", j + 384, j + 512), half("Pi", h))
-        yield ship("p", T.PK[:, n * 512 + 128:n * 512 + 512], T.PS[:, j + 128:j + 512], ("PS", j + 128, j + 512), ("PK", n * 512 + 128, n * 512 + 512))
-        yield ("done", ("p", t + 1, h))
-        yield cp(c("RS", b, b + 8), c("RS", b + 24, b + 32))
-        yield ship("r", T.RI[:, n * 160:n * 160 + 160], T.RS[:, i * 160:i * 160 + 160], ("RS", i * 160, i * 160 + 160), ("RI", n * 160, n * 160 + 160))
-        yield ("done", ("r", t + 1, h))
-        yield ("done", ("state", t, h))
-
-    def out(dst, src, q="sy"):
-        return give((q, lambda e: e.dma_start(dst, src[0]), [src[1]], [], "out", 16, 60.0, 2200.0, None))
+            yield tt(c("YE"), c("AT", 0, 5), c("NC", 0, 5), A.subtract)
+            yield out_(T.ye[:, :], c("YE"))
 
     def finish(h):
         i = 2 * (TS - 1) + h
-        j = i * 512
-        yield ("need", ("state", TS - 1, h))
-        if h:
-            yield ("need", ("finish", 0))
-        yield cp(half("FA", h, 8), c("RS", i * 160 + 144, i * 160 + 152))
-        o = (T.ST[0:8, 384:512], ("ST", 0, 1))
-        yield [mm(c("ST", 128, 256), c("PS", j + 128, j + 256), Ib, True, False), mm(c("ST", 128, 256), c("PS", j + 256, j + 384), Ib, False, True),
-               mm(o, half("FA", h, 8), Ib, True, True)]
-        p = c("P2", 128 * h, 128 * h + 128)
-        yield ts(p, half("Pi", h), -1, col(1), A.mult, A.add)
-        yield tt(c("T1", 128 * h, 128 * h + 128), c("ST", 128, 256), p, A.mult)
+        for k in (("st1", i), ("st0", 2 * TS - 1), ("L", 2 * TS - 1), "wp", ("fin", h - 1)):
+            yield ("need", k)
+        r, o = msg("MS", i, 2), (T.ST[0:8, 256:384], ("ST", 0, 1))
+        yield group(c("ST", 0, 128), (half("WP", 0), r), (half("WP", 1), r)) + group(o, (c("Ib", 14, 128, 16), r))
+        yield ts(half("W1", h), c("ST", 0, 128), 127.5, None, A.add)
+        yield ("done", ("w3", h))
         y = (T.YF[0:8, h * 128:h * 128 + 128], ("YF", h * 128, h * 128 + 128))
-        yield ts(y, o, -1, 15, A.mult, A.add)
-        yield ("done", ("finish", h))
-        yield out(T.yf[:, h * 128:h * 128 + 128], y)
-        yield tt(p, c("T1", 128 * h, 128 * h + 128), half("Pi", h), A.add)
-        yield ts(half("YP", h), p, -1, 15, A.mult, A.add)
-        yield out(T.yp[:, h * 128:h * 128 + 128], half("YP", h))
+        yield ts(y, o, -16, 7.5, A.mult, A.add)
+        yield out_(T.yf[:, h * 128:h * 128 + 128], y)
+        p = a("HR", T.HR[:, 0, :])
+        for x in gather_cuts(("w3", h), p, "Zb", half("W1", h), "R1", 128 * h, []):
+            yield x
+        yield ts(half("YP", h), p, col(1), None, A.add)
+        yield ("done", ("fin", h))
+        yield out_(T.yp[:, h * 128:h * 128 + 128], half("YP", h))
 
-    def last():
-        yield ("need", ("table", TS - 1, 0))
-        yield ("need", ("table", TS - 1, 1))
-        yield out(T.yx[:, :], c("X", 0, 2048))
-        yield out(T.yz[:, :], c("ZN", 8 * 128, 10 * 128), "s")
-
-    th = [(0, some_masks()), (0, rows_out()), (0, names()), (2, consts()), (3, first_state(0)), (4, first_state(1)), (0, last())]
-    for t in range(TS):
-        for h in range(2):
-            th += [(0, lists(t, h)), (0, choose(t, h)), (3 - h, state(t, h)), (5, gathers(t, h)), (4, minus_z(t, h)), (4, absval(t, h)), (4, sums(t, h))]
-        th.append((1, count(t)))
-        if t < N:
-            th.append((6, statics(t)))
+    third = [s for s in range(1, 16) if s % 3 == 2]
+    rest = [s for s in range(1, 16) if s % 3 != 2]
+    th = [(0, slots()), (1, consts_g()), (2, consts()), (7, consts2()),
+          (0, cuts("w1", c("W1"), "R1", 0, 16, rest, True)), (0, cuts("w1", c("W1"), "R1", 0, 16, third, False))]
     for h in range(2):
-        th.append((3, finish(h)))
-    ev, live, blocked = {("nc", 0), ("g", -1, 0)}, [], {}
+        th += [(h, first(h)), (h, cuts(("w2", h), half("W2", h), "R2", 128 * h, 1, range(1, 16, 2), False)),
+               (h, cuts(("w2", h), half("W2", h), "R2", 128 * h, 1, range(2, 16, 2), True)), (1, finish(h)),
+               (1, cuts(("w3", h), half("W1", h), "R1", 128 * h, 16, rest if h == 0 else third, True)),
+               (1, cuts(("w3", h), half("W1", h), "R1", 128 * h, 16, third if h == 0 else rest, False))]
+    for i in range(2 * TS):
+        th += [(0, choose(i)), (1, state(i)), (2, columns(i)), (6, gaps(i)), (5, gather_s(i)), (5, gather_v(i)), (4, minus_z(i)), (4, absval(i)),
+               (4, keys(i)), (4, keys_v(i))]
+    th += [(1, count(t)) for t in range(TS)]
+    ev = {("nc", 0), ("gs", -1), ("gv", -1), ("st0", -1), ("st1", -1), ("dl", -1), ("L", -1), ("fin", -1), ("abs", -1), ("abs", -2), ("abs", -3)}
+    live, blocked, held = [], {}, set()
 
-    def pull(rec):
-        for x in rec[1]:
-            if isinstance(x, tuple) and x[0] == "done":
-                ev.add(x[1])
+    def pull(rec_):
+        while True:
+            x, rec_[3] = rec_[3] or next(rec_[1], None), None
+            if x is None:
+                return
+            if isinstance(x, tuple) and x[0] in ("done", "unlock"):
+                if x[0] == "done":
+                    ev.add(x[1])
+                else:
+                    held.discard(x[1])
                 for r in blocked.pop(x[1], ()):
                     pull(r)
-            elif isinstance(x, tuple) and x[0] == "need":
-                if x[1] not in ev:
-                    blocked.setdefault(x[1], []).append(rec)
+            elif isinstance(x, tuple) and x[0] in ("need", "lock"):
+                if (x[1] not in ev) if x[0] == "need" else (x[1] in held):
+                    rec_[3] = x
+                    blocked.setdefault(x[1], []).append(rec_)
                     return
+                if x[0] == "lock":
+                    held.add(x[1])
             else:
-                rec[2] = x
-                live.append(rec)
+                rec_[2] = x if isinstance(x, list) else [x]
+                live.append(rec_)
                 return
 
-    def when(x):
-        if isinstance(x, list):
-            return start(x[0]), x
-        if x[0] == "alt":
-            a, v = start(x[1]), start(x[2])
-            return (v, [x[2]]) if v + x[2][6] + VPEN < a + x[1][6] else (a, [x[1]])
-        return start(x), [x]
-
     for n, (p, gen) in enumerate(th):
-        pull([p * 1000 + n, gen, None])
+        pull([p * 1000 + n, gen, None, None])
     while live:
-        best = None
-        for rec in live:
-            s, calls = when(rec[2])
-            if best is None or (s, rec[0]) < (best[0], best[1][0]):
-                best = (s, rec, calls)
-        live.remove(best[1])
+        best = min(live, key=lambda r: (start(r[2][0]), r[0]))
+        live.remove(best)
         for d in best[2]:
             do(d)
-        pull(best[1])
+        pull(best)
+    assert not blocked
     for s in cnt:
         g.wait_ge(sem[s], cnt[s])
-    for t in range(1, N):
-        g.wait_ge(sem["l%d" % t], len(topo.engines(T.cores[(rank - t) % N], core)[:8]))
     for t in range(1, TS):
         for h in range(2):
-            for k in KINDS:
-                g.wait_ge(sem["a%s%d%d" % (k, t, h)], len(topo.engines(prv, core)[:8]))
+            g.wait_ge(sem["a%d%d" % (t, h)], ein)
     g.wait_ge(sem.sent, sent[0])

@@ -1,35 +1,39 @@
 from concourse.mybir import dt, AluOpType as A, AxisListType, ActivationFunctionType as F
+from concourse.bass import DstId, RemoteDMATransfer
 
 N, TS = 4, 5
-NV = 8
-WAKE, SHIP = 70.0, 4500.0
-CY, PE, FIX = 0.9, 0.5, 55.0
+NV = 10
+WAKE, SHIP = 60.0, (4000.0, 4000.0, 2700.0)
+CY, PE, FIX = 0.85, 0.5, 55.0
+PASSES, AHEAD = 3, 2
+FIRST, PERIOD, GATHER, SLACK = 14000.0, 17000.0, 6300.0, 5000.0
 BIG, M1_, M8_ = 2.0 ** 19, 1.5 * 2 ** 23, 1.5 * 2 ** 26
+XN = 2112
 f32, b16, h16, i32, u16 = "float32", "bfloat16", "float16", "int32", "uint16"
 SB_ = {
-    "X": ([2112], b16), "NM": ([256], i32), "PR": ([256], i32), "TH": ([5], i32), "Z0": ([256], b16), "ZO": ([256], b16),
-    "ONE": ([128], f32), "If": ([8, 16], f32), "BOa": ([128], f32), "BO": ([8, 16], f32), "LT": ([128], b16), "PERM": ([128], b16),
-    "PI": ([16], i32), "PI2": ([16], i32), "DJ": ([128], i32), "M1": ([128], b16), "COL": ([24], f32), "KC": ([32], f32),
-    "Ib": ([128], b16), "nI": ([128], b16), "I2": ([128], b16), "I14": ([128], b16), "Im": ([128], b16), "BOb": ([128], b16),
-    "Zf": ([2, 144], f32), "Z4": ([2, 144], f32), "Zb": ([2, 144], b16), "A12": ([256], f32), "SEL": ([256], b16), "D12": ([256], b16),
-    "SXY": ([256], b16), "SXa": ([256], b16), "WP": ([256], b16), "CAB": ([256], b16), "PX": ([2, 64], f32), "PM": ([4, 4, 2, 16], h16),
-    "RX": ([3, 8, 2], b16), "RY": ([8], b16), "CK": ([8, 2, 14], b16), "CKi": ([8, 2, 14], f32), "KR": ([8, 2, 14], b16),
-    "TM": ([TS, 8, 2, 14], h16), "OB": ([256], b16), "D0": ([224], f32), "RLi": ([8], i32), "RL": ([8], u16),
-    "JI": ([8], i32), "JC": ([24], b16), "J8": ([16], b16), "IN3": ([24], b16), "MV": ([64], i32), "OH": ([64], b16),
+    "X": ([2 * XN], b16), "NM": ([256], i32), "PR": ([256], i32), "TH": ([10], i32),
+    "ONE": ([128], f32), "If": ([8, 16], f32), "BOa": ([128], f32), "BO": ([8, 16], f32), "LT": ([128], b16), "PERM": ([128], b16), "SW": ([128], b16),
+    "PI": ([16], i32), "PI2": ([16], i32), "DJ": ([128], i32), "M1": ([128], b16), "COL": ([32], f32), "KC": ([32], f32),
+    "Ib": ([128], b16), "nI": ([128], b16), "I2": ([128], b16), "I14": ([128], b16), "Im": ([128], b16), "BOb": ([128], b16), "BO2": ([128], b16),
+    "Zf": ([2, 144], f32), "Zb": ([2, 144], b16), "A12": ([256], f32), "SEL": ([256], b16), "D12": ([256], b16), "MV2": ([8, 2], f32),
+    "SXY": ([256], b16), "SXa": ([256], b16), "WP": ([256], b16), "CAB": ([128], b16), "PM": ([4, 128], b16),
+    "RX": ([3, 8, 2], b16), "RY": ([8], b16), "CK": ([8, 2, 16], b16), "CKi": ([8, 2, 16], f32), "KR": ([8, 2, 16], b16),
+    "TM": ([2, 8, 2, 16], h16), "OB": ([256], b16), "D0": ([256], f32), "RLi": ([8], i32), "RL": ([8], u16),
+    "JI": ([8], i32), "JC": ([32], b16), "J8": ([48], b16), "IN3": ([32], b16), "MV": ([64], i32), "OH": ([64], b16),
     "MK": ([768], b16), "P16": ([256], b16), "NQ": ([256], h16), "AA": ([512], b16), "W1": ([256], b16), "W2": ([256], f32),
-    "R1": ([4096], b16), "R2": ([4096], f32),
-    "ML": ([3840], h16), "MS": ([3840], h16),
+    "R1": ([4096], b16), "R2": ([4096], f32), "OC": ([256], f32),
+    "NL": ([1536], h16), "NO": ([1024], h16), "RO": ([1024], b16), "LR": ([128], u16), "ZL": ([4608], b16), "ZS": ([3840], b16),
     "PP": ([512], f32), "QQ": ([512], i32), "HB": ([512], i32), "HF": ([512], h16), "HT": ([2, 2, 128], h16), "DL": ([512], f32), "TT": ([512], f32),
     "OFF": ([512], u16), "WW": ([8192], b16), "AY": ([4096], b16), "XR": ([4096], b16), "RU": ([4096], b16),
-    "SC": ([448], f32), "FF": ([16], f32), "SE": ([16], i32), "KQ": ([16], i32), "GM": ([256], b16), "LS": ([48], u16), "ES": ([16], b16),
-    "AW": ([256], b16), "SZ": ([256], f32), "HZ": ([256], i32), "K8": ([16], b16), "LC": ([16], u16), "SX2": ([256], f32), "HX2": ([256], i32),
-    "AT": ([8], f32), "NC": ([8], b16), "AI": ([8], i32), "YE": ([5], f32), "YP": ([256], f32), "YF": ([256], f32),
+    "SC": ([512], f32), "FF": ([16], f32), "SE": ([16], i32), "KQ": ([16], i32), "GM": ([256], b16), "LS": ([320], u16), "ES": ([16], b16),
+    "AW": ([256], b16), "SZ": ([256], f32), "HZ": ([256], i32), "K8": ([32], b16), "UU": ([16], f32), "LC": ([32], u16), "SX2": ([512], f32), "HX2": ([512], i32),
+    "AT": ([16], f32), "NC": ([16], b16), "AI": ([16], i32), "YE": ([16], f32), "YP": ([256], f32), "YF": ([256], f32),
 }
 SCRATCH = {k: ("sbuf", [128] + v[0], v[1]) for k, v in SB_.items()}
 SCRATCH.update({"SB": ("psum", [128, 1536], f32), "KP": ("psum", [128, 512], f32), "HR": ("psum", [128, 2, 128], f32),
-                "ST": ("psum", [128, 1024], f32), "TL": ("psum", [128, 512], f32)})
+                "ST": ("psum", [128, 1024], f32), "TL": ("psum", [128, 32, 16], f32)})
 PSUM = ("SB", "KP", "ST", "TL", "HR")
-SEMAPHORES = ["v", "p", "s", "gq", "sent", "dm0", "dm1", "dm2", "dm3", "dx0", "out"] + ["a%d%d" % (t, h) for t in range(1, TS) for h in range(2)]
+SEMAPHORES = ["v", "p", "s", "gq", "sent", "out"] + ["tw0", "tw1"] + ["l%d" % k for k in range(24)] + ["a%d%d" % (i, k) for i in range(2 * TS - 2) for k in range(3)]
 
 
 def rank_program(g, core, T, topo):
@@ -38,7 +42,7 @@ def rank_program(g, core, T, topo):
         return
     sem = T.sem
     Q = {"v": g.vector, "p": g.tensor, "s": g.scalar, "gq": g, "sy": g.sync}
-    cnt, know, hist, free = {}, {q: {} for q in Q}, {}, {q: 0.0 for q in Q}
+    cnt, know, hist, free, dry, key = {}, {q: {} for q in Q}, {}, {q: 0.0 for q in Q}, [True], [None]
 
     def needs(q, rd, wr):
         out = []
@@ -55,7 +59,8 @@ def rank_program(g, core, T, topo):
     def acc(q, rd, wr):
         for e in sorted(needs(q, rd, wr), key=lambda e: -e[5]):
             if know[q].get(e[4], 0) < e[5]:
-                Q[q].wait_ge(sem[e[4]], e[5])
+                if not dry[0]:
+                    Q[q].wait_ge(sem[e[4]], e[5])
                 for s, n in list(e[6].items()) + [(e[4], e[5])]:
                     know[q][s] = max(know[q].get(s, 0), n)
 
@@ -63,19 +68,19 @@ def rank_program(g, core, T, topo):
         for regs, w in ((rd, False), (wr, True)):
             for (b, lo, hi) in regs:
                 old = [e for e in hist.get(b, []) if not (lo <= e[1] and e[2] <= hi and (w or (e[0] == q and not e[3])))]
-                hist[b] = old + [(q, lo, hi, w, s, n, snap, fin)]
+                hist[b] = old + [(q, lo, hi, w, s, n, snap, fin, key[0])]
 
     def do(d):
         q, fn, rd, wr, s, inc, dur, lat, post = d
         t0 = start(d)
         acc(q, rd, wr)
         free[q] = t0 + dur
-        if s is None:
-            fn(Q[q])
-        else:
+        call = None if dry[0] else fn(Q[q])
+        if s is not None:
             cnt[s] = cnt.get(s, 0) + inc
-            fn(Q[q]).then_inc(sem[s], inc)
-            note(q, rd, wr, s, cnt[s], dict(know[q]), t0 + dur + lat)
+            if call:
+                call.then_inc(sem[s], inc)
+            note(q if inc == 1 else s, rd, wr, s, cnt[s], dict(know[q]), t0 + dur + lat)
         if post:
             post(t0 + dur)
 
@@ -151,42 +156,69 @@ def rank_program(g, core, T, topo):
     def dma(q, out, in_, s, rd, wr):
         return (q, lambda e: e.dma_start(out, in_), rd, wr, s, 16, 60.0, 2200.0, None)
 
-    def out_(dst, src, q="sy"):
-        return dma(q, dst, src[0], "out", [src[1]], [])
+    def out_(dst, src, reg, q="sy"):
+        return dma(q, dst, src, "out", [reg], [])
 
     def gi(out, pat, base, cm):
         d = 130 + 2 * CY * size(out)
+        out = out + (("GQ", 0, 1),)
         if SCRATCH[out[1][0]][2] != i32:
             return op("gq", lambda e: e.iota(out[0], pat, base, cm, allow_small_or_imprecise_dtypes=True), out, dur=d)
         return op("gq", lambda e: e.iota(out[0], pat, base, cm), out, dur=d)
 
     def gs(out, x, pat, cmp_, base, cm, fill=0.0):
-        return op("gq", lambda e: e.affine_select(out[0], x[0], pat, cmp_, fill, base, cm), out, x, dur=170 + 2 * CY * size(out))
+        return op("gq", lambda e: e.affine_select(out[0], x[0], pat, cmp_, fill, base, cm), out + (("GQ", 0, 1),), x, dur=170 + 2 * CY * size(out))
 
     sent = [0]
     nxt, prv = T.cores[(rank + 1) % N], T.cores[(rank - 1) % N]
     ein = len(topo.engines(prv, core)[:8])
 
-    def send(i):
+    def send(i, k):
         rid, pid = topo.addr(nxt, core)
-        en = topo.engines(core, nxt)[:8]
+        en, to, s = topo.engines(core, nxt)[:8], DstId(rid=rid, pnc=pid), "a%d%d" % (i, k)
         sent[0] += len(en)
-        s, src, dst = "a%d%d" % (i // 2 + 1, i % 2), c("MS", 384 * i, 384 * i + 384), c("ML", 384 * i + 768, 384 * i + 1152)
-        return ("gq", lambda e: e.remote_dma(dst[0], src[0], sem[s], sem.sent, pid, rid, sum(1 << x for x in en)), [src[1]], [], None, 0, 1000.0, 0.0,
-                lambda t: note("rem", [], [dst[1]], s, ein, {}, t + SHIP - 1000))
+        mask = lambda es: sum(1 << x for x in es)
+        if k == 0:
+            src, dst, n = [names("L", i), rows("L", i)], [names("O", i), half("RO", i)], len(en) // 2
+            tr = [RemoteDMATransfer(dst_ids=[to], dma_engine_mask=mask(en[n * q:n * q + n]), remote_sem=sem[s], src=src[q][0], dst=dst[q][0]) for q in range(2)]
+        else:
+            src, dst = ([zed("S", i)], [half("ZL", 3 * i + 7 + q) for q in range(2)]) if k == 1 else ([c("LS", 32 * i + 8, 32 * i + 24)], [half("LR", i, 16)])
+            tr = [RemoteDMATransfer(dst_ids=[to] * len(dst), dma_engine_mask=mask(en), remote_sem=sem[s], srcs=[src[0][0]], dsts=[x[0] for x in dst])]
+        return ("gq", lambda e: e.remote_dma_fused(tr, local_sem=sem.sent), [x[1] for x in src], [], None, 0, 1000.0, 0.0,
+                lambda t: note("rem", [], [x[1] for x in dst], s, ein * (1 + k % 2), {}, t + SHIP[k]))
 
     half = lambda b, h, n=128: c(b, h * n, h * n + n)
     col = lambda j: c("COL", j, j + 1)
-    msg = lambda b, i, k: c(b, 384 * i + 128 * k, 384 * i + 128 * k + 128)
+    names = lambda b, i: half("N" + b, i)
+    rows = lambda b, i: half("Z" + b, 3 * i)
+    zed = lambda b, i: half("Z" + b, 3 * i + 1)
     Ib, nI, IND, u0 = c("Ib"), c("nI"), a("BO", T.BO[:, :, 0]), c("PI2", 0, 1)
     CS = lambda b, s: a(b, T[b][:, 0, 15 - s:143 - s])
     DS = lambda b, s: a(b, T[b][:, 1, 15 - s:143 - s])
     SEL14 = c("SEL", 0, 128)
+    P64 = lambda k: slice(64 * k, 64 * k + 64)
+    C128 = lambda k: slice(128 * k, 128 * k + 128)
 
-    for d in (dma("sy", T.PR[:, :], T.pr[:, :], "dm1", [], [("PR", 0, 256)]), dma("sy", T.NM[:, :], T.nm[:, :], "dm0", [], [("NM", 0, 256)]),
-              dma("sy", T.Z0[:, :], T.z0[:, :], "dm2", [], [("Z0", 0, 256)]), dma("sy", T.TH[:, :], T.th[:, :], "dm3", [], [("TH", 0, 5)]),
-              dma("s", T.X[:, 0:2048], T.xt[:, :], "dx0", [], [("X", 0, 2048)]),
-              ms(c("ONE"), 1.0), gi(c("PI"), [[0, 16]], 0, 1),
+    loads = []
+    for b, src in (("PR", T.pr), ("NM", T.nm)):
+        loads += [("sy" if k else "s", T[b][P64(k), C128(h)], src[P64(h), C128(k)], half(b, h)[1]) for h in range(2) for k in range(2)]
+    for h in range(2):
+        loads += [("sy" if k else "s", T.X[P64(k), XN * h:XN * h + 2048], T.xt[P64(h), :], ("X", XN * h + k, XN * h + 2048)) for k in range(2)]
+        loads += [("sy", T.ZL[P64(k), C128(3 * h + q)], T.z0[P64(h), C128(k)], half("ZL", 3 * h + q)[1]) for k in range(2) for q in (1, 2)]
+        loads += [("sy", T.TH[P64(k), 5 * h:5 * h + 5], T.th[P64(h), :], ("TH", 0, 10)) for k in range(2)]
+
+    def begin():
+        key[0] = None
+        for n, (q, o, src, reg) in enumerate(loads):
+            cnt["l%d" % n] = 16
+            if not dry[0]:
+                Q[q].dma_start(o, src).then_inc(sem["l%d" % n], 16)
+            free[q] += 60.0
+            hist.setdefault(reg[0], []).append(("l%d" % n, reg[1], reg[2], True, "l%d" % n, 16, {}, free[q] + (4500.0 if reg[0] == "X" else 2500.0), None))
+        for d in early:
+            do(d)
+
+    early = ( ms(c("ONE"), 1.0), gi(c("PI"), [[0, 16]], 0, 1),
               gs(c("BOa"), c("ONE"), [[-16, 8], [0, 16]], A.is_ge, 0, 1), gs(a("BO"), c("BOa"), [[16, 8], [0, 16]], A.is_ge, 15, -1),
               gs(c("LT"), a("BO"), [[1, 128]], A.is_gt, 0, -1), gs(a("If"), c("ONE"), [[-1, 128]], A.is_equal, 0, 1),
               gi(c("KC", 0, 16), [[-1, 16]], 0, 0), gi(c("KC", 16, 32), [[-16, 16]], 0, 0),
@@ -196,36 +228,52 @@ def rank_program(g, core, T, topo):
               ms(a("Zf"), 0.0), cp(a("Zf", T.Zf[:, 0, 15:143:16]), IND), cp(a("Zf", T.Zf[:, 1, 15:143:16]), IND),
               ts(a("Zf", T.Zf[:, 1, 14:142:16]), IND, -1, None, A.mult), cp(a("Zb"), a("Zf")),
               act(Ib, a("If"), F.Copy), act(c("I2"), a("If"), F.Copy, scale=2.0), act(c("I14"), a("If"), F.Copy, scale=14.0),
-              act(c("Im"), a("If"), F.Copy, scale=2.0 ** -12), act(a("Z4"), a("Zf"), F.Copy, scale=4096.0)):
-        do(d)
+              act(c("Im"), a("If"), F.Copy, scale=2.0 ** -12))
 
     def consts_g():
+        yield gi(a("CAB", T.CAB[0:64, :]), [[0, 8], [64, 16]], -992, 0)
+        yield ("done", "cab0")
         yield gs(c("PERM"), c("ONE"), [[-2, 64], [1, 2]], A.is_equal, -1, 1)
         yield ("done", "perm")
-        for x4 in range(2):
-            yield gs(a("PX", T.PX[:, x4, :]), c("ONE", 0, 64), [[-32, 4], [-1, 16]], A.is_equal, -16 * x4, 1)
-        yield ("done", "px")
+        for i in range(4):
+            yield gs(a("PM", T.PM[:, i]), c("ONE"), [[-32, 4], [1000, 2], [-1, 16]], A.is_equal, -16 * (i // 2) - 1000 * (i % 2), 1)
         yield ("need", "sel")
         for o, s, k in (("SXY", "SXa", (3232.0, 2400.0)), ("D12", "SEL", (-1.0, -1.0))):
             for q in range(2):
                 yield gs(half(o, q), half(s, q), [[-1, 128]], A.not_equal, 0, 1, k[q])
-        yield ("done", "sxy")
-        yield gi(a("CKi"), [[0, 8], [16, 2], [1, 14]], 1, 0)
-        yield gi(c("DJ"), [[-1, 128]], 128, 1)
+            yield ("done", o)
+        fill = lambda x, k: gi(x, [[0, size(x)]], k, 0)
+        yield gi(a("CKi"), [[0, 8], [-240, 2], [1, 16]], 241, 0)
+        for q, (k, pad) in enumerate(((0, -2 ** 23), (8128, -16))):
+            yield fill(a("CK", T.CK[64:128, :, q, 0:14]), k)
+            yield fill(a("CK", T.CK[64:128, :, q, 14:16]), pad)
+        yield ("done", "ck")
         yield gi(c("RLi"), [[1, 8]], 0, 0)
         yield gi(c("JI"), [[16, 8]], 0, 0)
-        yield ("need", "mv")
+        yield gi(c("DJ"), [[0, 8], [1, 16]], 0, 0)
+        yield gi(c("JC", 8, 32), [[32, 3], [0, 8]], 0, 0)
+        yield fill(c("MV"), 15)
         yield gi(c("MV", 1, 15), [[2, 7], [-1, 2]], 1, 0)
         yield gi(c("MV", 17, 31), [[1, 14]], 0, 0)
         yield gi(c("MV", 49, 63), [[2, 7], [-1, 2]], 1, 0)
+        yield fill(c("D0"), 1)
+        yield fill(c("D0", 0, 256, 32), 0)
+        for k in range(2):
+            yield fill(a("COL", T.COL[P64(k), 8:9]), 1024 * k)
+        yield gi(c("J8", 8, 24), [[28672, 2], [0, 8]], -14336, 0)
         yield ("done", "iotas")
+        for h in range(2):
+            for lo, hi in ((0, 128), (1920, 2176), (3968, 4096)):
+                yield fill(c("WW", 4096 * h + lo, 4096 * h + hi), 0)
+            yield ("done", ("ww", h))
 
     def consts():
-        yield ms(c("MV"), 15)
-        yield ("done", "mv")
-        yield ts(col(5), u0, 4096, -63488, A.mult, A.add)
-        yield act(half("CAB", 0), c("ONE"), F.Copy, scale=col(5))
-        yield ms(half("CAB", 1), -15 / 32)
+        yield ms(c("OB", 0, 128), 1.0)
+        yield ms(a("TM"), 0.0)
+        for q in range(2):
+            yield act(a("MV2", T.MV2[:, :, q]), IND, F.Copy, scale=4096.0 * (2 * q - 1))
+        yield ("need", "cab0")
+        yield ms(a("CAB", T.CAB[64:128, :]), -15 / 2048)
         yield ("done", "cab")
         for q in range(2):
             yield ts(col(3 + q), u0, 14 + q, None, A.is_equal)
@@ -234,19 +282,13 @@ def rank_program(g, core, T, topo):
         yield act(half("SXa", 0), c("PERM"), F.Copy, scale=2400.0)
         yield act(half("SXa", 1), SEL14, F.Copy, scale=3232.0)
         yield ("done", "sel")
-        yield ms(a("PM"), 0.0)
-        yield ("need", "px")
-        for i in range(4):
-            yield cp(a("PM", T.PM[:, i, :, i % 2, :]), a("PX", T.PX[:, i // 2, :]))
         yield ms(c("NC"), 0.0)
-        yield ("done", "pm")
-        yield cp(c("X", 2048, 2112), c("X", 0, 64))
-        for h in range(2):
-            yield cp(msg("ML", h, 0), half("Z0", h))
         yield act(nI, a("If"), F.Copy, scale=-1.0)
         yield ms(col(15), 128.0)
-        yield ("done", ("table", -2))
-        yield ("done", ("table", -1))
+        yield ("done", "pm")
+        for h in range(2):
+            yield cp(c("X", XN * h + 2048, XN * h + XN), c("X", XN * h, XN * h + 64))
+            yield ("done", ("table", h - 2))
 
     def consts2():
         yield ("need", "pm")
@@ -255,38 +297,27 @@ def rank_program(g, core, T, topo):
                 yield act(a("RX", T.RX[:, n, :, q]), IND, F.Copy, scale=k * w)
         yield act(c("RY"), IND, F.Copy, scale=-512 * BIG)
         for q, w in enumerate((512 * BIG, 512.0)):
-            yield act(a("KR", T.KR[:, :, q, :]), a("If", T.If[:, :, 0:14]), F.Copy, scale=w)
-        yield ms(c("OB", 0, 128), 1.0)
-        yield ms(c("OB", 128, 256), 32 * BIG)
-        yield ms(a("TM"), 0.0)
-        yield ts(c("COL", 8, 13), c("TH"), -1, -1, A.mult, A.add)
-        for t in range(TS):
-            yield ts(a("TM", T.TM[:, t, :, 0, :]), a("BO", T.BO[:, :, 0:14]), col(8 + t), None, A.mult)
-        yield ("need", "iotas")
-        for q, w in enumerate((BIG, 1.0)):
-            yield ts(a("CK", T.CK[0:32, :, q, :]), a("CKi", T.CKi[0:32, :, q, :]), w / 32, None, A.mult)
-            yield ms(a("CK", T.CK[32:64, :, q, :]), 7.5 * w)
-            yield ms(a("CK", T.CK[64:128, :, q, :]), 8064.0 * q)
-        yield ("done", ("scan", -1))
-        yield ms(c("D0"), 0.0)
-        yield ms(c("D0", 0, 224, 28), -2.0 ** 60)
-        yield cp(c("RL"), c("RLi"))
-        yield ts(c("DJ"), c("DJ"), 15, None, A.bitwise_and)
-        yield ts(c("M1"), c("DJ"), 0, None, A.is_equal)
-        yield ts(c("JC", 0, 8), c("JI"), col(0), None, A.add)
-        yield ms(c("JC", 8, 16), 0.0)
-        yield ms(c("JC", 16, 24), 32.0)
-        yield ts(c("J8", 0, 8), c("JC", 0, 8), 8, None, A.mult)
-        yield ms(c("J8", 8, 16), -3.5)
-        for q, w in enumerate((128.0, 1.0, 1.0)):
+            yield act(a("KR", T.KR[:, :, q, :]), a("If"), F.Copy, scale=w)
+        yield act(half("OB", 1), c("ONE"), F.Copy, scale=32 * BIG)
+        yield ts(c("COL", 16, 26), c("TH"), -1, -1, A.mult, A.add)
+        yield ("done", "th")
+        for k in range(2):
+            for q in range(2):
+                yield act(a("BO2", T.BO2[P64(k), P64(q)]), a("BO", T.BO[P64(k), 4 * k:4 * k + 4, :]), F.Copy)
+        for q, w in enumerate((128.0, 1.0, 1.0, 0.0)):
             yield act(half("IN3", q, 8), IND, F.Copy, scale=w)
-        yield ts(c("OH"), c("MV"), col(0), None, A.is_equal)
-        yield act(c("BOb"), a("BO"), F.Copy)
+        yield ("need", "ck")
+        for q, w in enumerate((BIG, 1.0)):
+            yield act(a("CK", T.CK[0:64, :, q, :]), a("CKi", T.CKi[0:64, :, q, :]), F.Copy, scale=w / 64)
+        yield ("done", ("scan", -1))
         for q in range(2):
             yield tt(half("A12", q), a("If"), CS("Zf", 14 + q), A.subtract)
-        for h in range(2):
-            for lo, hi in ((0, 128), (1920, 2176), (3968, 4096)):
-                yield ms(c("WW", 4096 * h + lo, 4096 * h + hi), 0.0)
+        yield ("need", "iotas")
+        yield cp(c("RL"), c("RLi"))
+        yield ts(c("M1"), c("DJ"), col(0), None, A.is_equal)
+        yield ts(c("JC", 0, 8), c("JI"), col(0), None, A.add)
+        yield act(half("J8", 0, 8), c("JC", 0, 8), F.Identity, bias=col(8), scale=8.0)
+        yield ts(c("OH"), c("MV"), col(0), None, A.is_equal)
         yield ("done", "rest")
         yield ts(col(6), u0, 14, -16, A.is_lt, A.mult)
         yield ts(col(7), col(6), -1, -272, A.mult, A.add)
@@ -312,8 +343,7 @@ def rank_program(g, core, T, topo):
             yield mm(out, DS(Z, s), c(R, 256 * s + n, 256 * s + n + size(w)), False, s == 15)
 
     def split(o, b, i):
-        yield ts(msg(b, i, 1), o, M1_, -M1_, A.add, A.add)
-        yield tt(msg(b, i, 2), o, msg(b, i, 1), A.subtract)
+        return ts(names(b, i), o, M1_, -M1_, A.add, A.add), tt(rows(b, i), o, names(b, i), A.subtract)
 
     def slots():
         for q, o in enumerate((A.is_gt, A.is_equal)):
@@ -334,18 +364,28 @@ def rank_program(g, core, T, topo):
         yield ("done", ("w2", 1))
 
     def first(h):
-        o = c("TL", 128, 256) if h else c("KP", 0, 128)
+        b, key = "TL", ("w2", h)
         yield ("need", "cab")
-        for x in gather_cuts(("w2", h), o, "Z4", half("W2", h), "R2", 128 * h, [(Ib, half("CAB", 0)), (Ib, half("CAB", 1))]):
+        yield ("need", key)
+        yield ("lock", "TL")
+        yield [mm(a(b, T[b][:, 0:8, :]), half("OB", 0), c("CAB"), True, False), mm(a(b, T[b][:, 0:8, 0]), half("W2", h), a("MV2", T.MV2[:, :, 1]), False, False)]
+        for s in range(1, 16):
+            yield ("need", (key, s))
+            yield mm(a(b, T[b][:, 0:8, s - 1:s + 1]), half("R2", 2 * s + h), a("MV2"), False, s == 15)
+        yield act(half("OC", h), a(b, T[b][:, 0:8, :]), F.Copy)
+        yield ("unlock", "TL")
+        yield ("need", ("st1", h - 3))
+        yield group(c("ST", 768, 896), (half("OC", h), a("If")))
+        for x in split(c("ST", 768, 896), "L", h):
             yield x
-        for x in split(o, "ML", h):
-            yield x
-        yield ("done", ("m", h))
+        for k in ("n", "m", "m2"):
+            yield ("done", (k, h))
+        yield ("done", ("st1", h - 2))
 
     def columns(i):
         h = i % 2
-        nm_ = msg("ML", i, 1)
-        for k in (("m", i), "sxy", ("st0", i - 1)):
+        nm_ = names("L", i)
+        for k in (("n", i), "SXY", ("st0", i - 1)):
             yield ("need", k)
         yield group(c("ST", 0, 128), (c("PERM"), nm_)) + group(c("ST", 128, 256), (SEL14, nm_)) + \
             group(c("ST", 256, 384), (half("SXY", 0), nm_)) + group(c("ST", 384, 512), (half("SXY", 1), nm_))
@@ -366,18 +406,25 @@ def rank_program(g, core, T, topo):
                     w = ib * 32 + g2 * 16
                     p.append(mm(a("HR", T.HR[:, :, 2 * ib + x4:128:8]), a("PM", T.PM[:, 2 * x4 + g2]), (T.HT[:, h, :, w:w + 16], ht[1]), g2 == 0, g2 == 1))
             yield p
-        yield ("need", ("nc", i // 2))
-        yield ts(half("OFF", h, 256), a("HR"), c("NC", i // 2, i // 2 + 1), None, A.add)
+        yield ("need", ("nc", i))
+        yield ts(half("OFF", h, 256), a("HR"), c("NC", i, i + 1), None, A.add)
         yield ("done", ("L", i))
 
     def gaps(i):
-        for k in (("m", i), "sxy", ("dl", i - 1)):
+        for k in ("th", ("m", i)):
             yield ("need", k)
-        yield sum([group(c("ST", 512 + 128 * q, 640 + 128 * q), (half("D12", q), msg("ML", i, 1)), (half("D12", q), msg("ML", i, 2))) for q in range(2)], [])
+        yield ts((T.TM[:, i % 2, :, 0, 0:14], ("TM", i % 2, i % 2 + 1)), a("BO", T.BO[:, :, 0:14]), col(16 + 5 * (i % 2) + i // 2), None, A.mult)
+        yield ("done", ("tm", i))
+        if i < 2 * TS - 2:
+            yield send(i, 0)
+        for k in (("L", i), ("gv", i), ("dl", i - 1), ("st1", i - 2), "D12"):
+            yield ("need", k)
+        yield sum([group(c("ST", 512 + 128 * q, 640 + 128 * q), (half("D12", q), old(i)[0]), (half("D12", q), old(i)[1])) for q in range(2)], [])
         yield act(half("DL", i % 2, 256), c("ST", 512, 768), F.Copy)
         yield ("done", ("dl", i))
 
-    XW = c("X", 0, 2112)
+    old = lambda i: (names("O", i), half("RO", i), half("LR", i, 16)) if i < 2 * TS - 2 else (names("L", i), rows("L", i), c("LS", 32 * i + 8, 32 * i + 24))
+    XW = lambda h: c("X", XN * h, XN * h + XN)
     cut = lambda lo, hi: [(s, min(4, hi - s)) for s in range(lo, hi, 4)]
     SCH = [(1,) + x for x in cut(0, 14)] + [(0,) + x for x in cut(NV, 14)]
     rec = lambda h, y, s, n: c("WW", 4096 * h + 128 * (s + 1 + 16 * (1 - y)), 4096 * h + 128 * (s + n + 1 + 16 * (1 - y)))
@@ -388,8 +435,7 @@ def rank_program(g, core, T, topo):
     left = {}
 
     def ready(i):
-        t = i // 2
-        for k in (("L", i), ("table", 2 * t - 2), ("table", 2 * t - 1)):
+        for k in (("L", i), ("m2", i), ("table", i - 2)):
             yield ("need", k)
 
     def gather_s(i):
@@ -397,7 +443,9 @@ def rank_program(g, core, T, topo):
             yield x
         yield ("need", ("gs", i - 1))
         for j, (y, s, n) in enumerate(SCH):
-            yield act(raw(i % 2, y, s, n), ind(XW, offs(i % 2, y, s, n)), F.Copy, bias=-128.0 * y)
+            if j >= AHEAD:
+                yield ("need", ("abs", i * len(SCH) + j - AHEAD))
+            yield act(raw(i % 2, y, s, n), ind(XW(i % 2), offs(i % 2, y, s, n)), F.Copy, bias=-128.0 * y)
             yield ("done", ("g", i, j))
         yield ("done", ("gs", i))
 
@@ -407,12 +455,11 @@ def rank_program(g, core, T, topo):
             yield x
         yield ("need", ("gv", i - 1))
         for s, n in cut(0, NV):
-            for k in range(s, s + n):
-                yield tt(rec(h, 0, k, 1), ind(XW, offs(h, 0, k, 1)), msg("ML", i, 0), A.subtract)
-            if s + n == NV:
-                yield ("done", ("gv", i))
+            for k in range(s, s + n, 2):
+                yield tt(rec(h, 0, k, 2), ind(XW(h), offs(h, 0, k, 2)), c("ZL", 384 * i + 128, 384 * i + 384), A.subtract)
             yield ts(tmp("RU", h, s, n), rec(h, 0, s, n), 0, None, A.max)
             yield ("done", ("ru", i, s))
+        yield ("done", ("gv", i))
 
     def minus_z(i):
         for j, (y, s, n) in enumerate(SCH):
@@ -421,7 +468,7 @@ def rank_program(g, core, T, topo):
             yield ("need", ("g", i, j))
             yield ("need", ("abs", J - 3))
             yield [mm(c("SB", b, b + 128 * n), Ib, raw(i % 2, y, s, n), True, False)] + \
-                [mm(c("SB", b + 128 * r, b + 128 * r + 128), nI, msg("ML", i, 0), False, r == n - 1) for r in range(n)]
+                [mm(c("SB", b + 128 * r, b + 128 * r + 128), nI, zed("L", i), False, r == n - 1) for r in range(n)]
             yield ("done", ("d", J))
 
     def absval(i):
@@ -432,175 +479,244 @@ def rank_program(g, core, T, topo):
             yield act(mag(i % 2, y, s, n), c("SB", b, b + 128 * n), F.Abs, bias=col(15) if y else 0.0)
             yield ("done", ("abs", J))
 
+    KP = lambda s, both: c("KP", s, 256, 16 if both else 32)
+
     def keys(i):
         left[i] = [28 + NV]
-        kp = c("KP", 0, 224)
-        for k in (("scan", i - 1), ("m", i)):
+        kp = c("KP", 0, 256)
+        for k in (("scan", i - 1), ("L", i), ("m", i), ("tm", i)):
             yield ("need", k)
-        yield [mm(kp, half("OB", 0), a("CK"), True, False), mm(kp, half("OB", 1), a("TM", T.TM[:, i // 2]), False, False),
-               mm(kp, msg("ML", i, 2), a("KR"), False, False)]
+        yield [mm(kp, half("OB", 0), a("CK"), True, False), mm(kp, half("OB", 1), (T.TM[:, i % 2], ("TM", i % 2, i % 2 + 1)), False, False),
+               mm(kp, rows("L", i), a("KR"), False, False)]
         yield ("done", ("k0", i))
         for j, (y, s, n) in enumerate(SCH):
             yield ("need", ("abs", i * len(SCH) + j))
-            yield [mm(c("KP", k, 224, 28 if y else 14), mag(i % 2, y, k, 1), c("RY") if y else a("RX", T.RX[:, 0]), False, left[i]) for k in range(s, s + n)]
+            yield [mm(KP(k, not y), mag(i % 2, y, k, 1), c("RY") if y else a("RX", T.RX[:, 0]), False, left[i]) for k in range(s, s + n)]
         yield ("done", ("ks", i))
 
     def keys_v(i):
         yield ("need", ("k0", i))
         for s, n in cut(0, NV):
             yield ("need", ("ru", i, s))
-            yield [mm(c("KP", k, 224, 14), x, a("RX", T.RX[:, q]), False, left[i]) for k in range(s, s + n)
+            yield [mm(KP(k, True), x, a("RX", T.RX[:, q]), False, left[i]) for k in range(s, s + n)
                    for q, x in ((2, rec(i % 2, 0, k, 1)), (1, tmp("RU", i % 2, k, 1)))]
         yield ("done", ("kv", i))
 
     def choose(i):
-        t, h = i // 2, i % 2
+        h = i % 2
         for k in (("ks", i), ("kv", i), "rest"):
             yield ("need", k)
-        sc = half("SC", h, 224)
-        yield op("v", lambda e: e.tensor_tensor_scan(sc[0], T.D0[:, :], T.KP[:, 0:224], 0.0, A.add, A.max), sc, c("D0"), c("KP", 0, 224), dur=FIX + CY * 224)
+        sc = half("SC", h, 256)
+        yield op("v", lambda e: e.tensor_tensor_scan(sc[0], T.D0[:, :], T.KP[:, 0:256], 0.0, A.mult, A.max), sc, c("D0"), a("KP"), dur=FIX + CY * 256)
         yield ("done", ("scan", i))
-        w = c("SC", 224 * h + 27, 224 * h + 224, 28)
+        w = c("SC", 256 * h + 31, 256 * h + 256, 32)
         yield ts(half("FF", h, 8), w, BIG, 1 / BIG, A.is_lt, A.max)
         yield tt(half("SE", h, 8), w, half("FF", h, 8), A.mult)
         yield ts(half("KQ", h, 8), half("SE", h, 8), 31, None, A.bitwise_and)
         yield tt(half("GM", h), ind(half("KQ", h, 8), c("RL")), c("M1"), A.mult)
         yield ("need", ("m", 1))
         yield ("lock", "TL")
-        yield group(c("TL", 0, 24), (Ib, c("JC")), (half("GM", h), c("IN3")))
-        yield cp(half("LS", h, 24), c("TL", 0, 24))
+        p = a("TL", T.TL[:, 0:2, :])
+        yield group(p, (Ib, c("JC")), (half("GM", h), c("IN3")))
+        yield cp(half("LS", i, 32), p)
         yield ("unlock", "TL")
         yield ("done", ("LS", i))
-        pick = ind(half("WW", h, 4096), c("LS", 24 * h, 24 * h + 8))
-        zn = half("ZO", h) if t + 1 == TS else msg("MS", i, 0)
+        if i < 2 * TS - 2:
+            yield send(i, 2)
+        yield ("done", ("LR", i))
+        if i < 2 * TS - 2:
+            yield ("need", ("zn", i))
+            yield send(i, 1)
+            yield ("done", ("m2", i + 2))
+
+    def table(i):
+        t, h = i // 2, i % 2
+        yield ("need", ("LS", i))
+        yield ("need", ("ww", h))
+        pick = ind(half("WW", h, 4096), c("LS", 32 * i, 32 * i + 8))
+        zn = zed("S", i)
         yield act(half("AW", h), pick, F.Abs)
-        yield tt(half("SZ", h), pick, msg("ML", i, 0), A.add)
+        yield tt(half("SZ", h), pick, zed("L", i), A.add)
         yield ts(half("HZ", h), half("SZ", h), 0.5, 63.75, A.mult, A.add)
         yield tt(zn, half("HZ", h), half("AW", h), A.min)
         yield ("done", ("zn", i))
-        p1, p2 = c("TL", 32, 40), c("TL", 40, 48)
-        zs = lambda k: (zn[0][:, k:128:16] if False else (T.ZO[:, 128 * h + k:128 * h + 128:16] if t + 1 == TS else T.MS[:, 384 * i + k:384 * i + 128:16]), zn[1])
+        if t + 1 == TS:
+            for k in range(2):
+                yield out_(T.yz[P64(h), C128(k)], T.ZS[P64(k), C128(3 * i + 1)], zn[1])
+        p1 = a("TL", T.TL[:, 2, 0:8])
         yield ("lock", "TL")
-        yield group(p1, (Ib, half("J8", 1, 8)), *[(CS("Zb", k), zs(k)) for k in range(16)])
-        yield ts(half("K8", h, 8), p1, M8_, -M8_, A.add, A.add)
-        yield group(p2, (Ib, half("J8", 0, 8)), *([(CS("Zb", k), zs(k)) for k in range(16)] + [(nI, half("K8", h, 8))]))
-        yield cp(half("LC", h, 8), p2)
+        yield group(p1, (c("Im"), half("J8", 1, 8)), *[(CS("Zb", k), c("ZS", 384 * i + 128 + k, 384 * i + 256, 16)) for k in range(16)])
+        yield act(half("UU", h, 8), p1, F.Copy)
+        yield ts(half("K8", h, 8), half("UU", h, 8), M8_, -M8_, A.add, A.add)
+        yield group(p1, (Ib, half("J8", 0, 8)), (c("Im"), half("J8", 2, 8)), (a("If"), half("UU", h, 8)), (nI, half("K8", h, 8)))
+        yield cp(half("LC", h, 8), p1)
         yield ("unlock", "TL")
-        xw = c("X", 1024 * h, 1024 * h + 1024)
+        xw, own = c("X", XN * h, XN * h + 2048), lambda k, p: T.X[P64(p), XN * h + 1024 * k:XN * h + 1024 * k + 1024]
         yield tt(half("SX2", h), ind(xw, half("LC", h, 8)), zn, A.add)
         yield ts(half("HX2", h), half("SX2", h), 0.5, -0.25, A.mult, A.add)
-        yield ("need", ("gs", 2 * t + 1))
-        yield ("need", ("gv", 2 * t + 1))
         yield cp(ind(xw, half("LC", h, 8)), half("HX2", h))
         if t + 1 == TS:
-            yield out_(T.yx[:, 1024 * h:1024 * h + 1024], xw)
-            yield out_(T.yz[:, 128 * h:128 * h + 128], zn, "s")
-        elif h == 0:
-            yield cp(c("X", 2048, 2112), c("X", 0, 64))
+            for k in range(2):
+                yield out_(T.yx[P64(h), 1024 * k:1024 * k + 1024], own(k, k), xw[1], ("s", "sy")[k])
+        else:
+            s = "tw%d" % h
+            cps = [(own(k, 1 - k), own(k, k)) for k in range(2)] + [(T.X[P64(k), XN * h + 2048:XN * h + XN], T.X[P64(0), XN * h:XN * h + 64]) for k in range(2)]
+
+            def fn(e):
+                for o, x in cps:
+                    e.dma_start(o, x).then_inc(sem[s], 16)
+            cnt[s] = 64 * (t + 1)
+            yield ("sy", fn, [], [XW(h)[1]], None, 0, 240.0, 0.0, lambda tm: note(s, [], [XW(h)[1]], s, cnt[s], dict(know["sy"]), tm + 2600.0))
         yield ("done", ("table", i))
 
     def state(i):
         h = i % 2
-        for k in (("LS", i), ("dl", i), ("st1", i - 1)):
+        for k in (("LR", i), ("dl", i), ("st1", i - 1)):
             yield ("need", k)
-        yield tt(half("TT", h, 256), ind(c("OH"), c("LS", 24 * h + 8, 24 * h + 24)), half("DL", h, 256), A.mult)
+        yield tt(half("TT", h, 256), ind(c("OH"), old(i)[2]), half("DL", h, 256), A.mult)
         o = c("ST", 768, 896)
-        yield group(o, (Ib, msg("ML", i, 1)), (Ib, msg("ML", i, 2)), (half("A12", 0), half("TT", 2 * h)), (half("A12", 1), half("TT", 2 * h + 1)))
-        for x in split(o, "MS", i):
-            yield x
+        yield group(o, (Ib, old(i)[0]), (Ib, old(i)[1]), (half("A12", 0), half("TT", 2 * h)), (half("A12", 1), half("TT", 2 * h + 1)))
+        n, r = split(o, "L", i + 2)
+        yield n
+        yield ("done", ("n", i + 2))
+        yield r
         yield ("done", ("st1", i))
-        if i // 2 + 1 < TS:
-            yield ("need", ("zn", i))
-            yield send(i)
-            yield ("done", ("m", i + 2))
+        yield ("done", ("m", i + 2))
 
-    def count(t):
-        for h in range(2):
-            yield ("need", ("LS", 2 * t + h))
-            yield ts(half("ES", h, 8), c("LS", 24 * h + 8, 24 * h + 16), 16, None, A.is_ge)
-        p = c("TL", 64, 72)
+    def count(i):
+        t, h = i // 2, i % 2
+        yield ("need", ("LS", i))
+        yield ts(half("ES", h, 8), c("LS", 32 * i + 8, 32 * i + 16), 16, None, A.is_ge)
+        p = a("TL", T.TL[:, 4, 0:8])
         yield ("lock", "TL")
-        yield [mm(p, c("BOb"), half("ES", 0, 8), True, False), mm(c("TL", 64, 65), Ib, c("NC", t, t + 1), False, False), mm(p, c("BOb"), half("ES", 1, 8), False, True)]
-        yield op("v", lambda e: e.tensor_reduce(T.AT[:, t:t + 1], p[0], AxisListType.X, A.add), c("AT", t, t + 1), p, dur=FIX + 64 * CY)
+        yield [mm(p, c("BO2"), half("ES", h, 8), True, False), mm(a("TL", T.TL[:, 4, 0:1]), Ib, c("NC", i, i + 1), False, True)]
+        yield op("v", lambda e: e.tensor_reduce(T.AT[:, i:i + 1], p[0], AxisListType.X, A.add), c("AT", i, i + 1), p, dur=FIX + 64 * CY)
         yield ("unlock", "TL")
         if t + 1 < TS:
-            yield ts(c("AI", t, t + 1), c("AT", t, t + 1), 1 / 64, -63 / 128, A.mult, A.add)
-            yield ts(c("NC", t + 1, t + 2), c("AI", t, t + 1), -64, c("AT", t, t + 1), A.mult, A.add)
-            yield ("done", ("nc", t + 1))
+            yield ts(c("AI", i, i + 1), c("AT", i, i + 1), 1 / 64, -63 / 128, A.mult, A.add)
+            yield ts(c("NC", i + 2, i + 3), c("AI", i, i + 1), -64, c("AT", i, i + 1), A.mult, A.add)
+            yield ("done", ("nc", i + 2))
         else:
-            yield tt(c("YE"), c("AT", 0, 5), c("NC", 0, 5), A.subtract)
-            yield out_(T.ye[:, :], c("YE"))
+            yield tt(c("YE", 8 * h, 8 * h + 5), c("AT", h, 10, 2), c("NC", h, 10, 2), A.subtract)
+            yield out_(T.ye[P64(h), :], T.YE[0:64, 8 * h:8 * h + 5], ("YE", 8 * h, 8 * h + 5))
 
     def finish(h):
         i = 2 * (TS - 1) + h
         for k in (("st1", i), ("st0", 2 * TS - 1), ("L", 2 * TS - 1), "wp", ("fin", h - 1)):
             yield ("need", k)
-        r, o = msg("MS", i, 2), (T.ST[0:8, 256:384], ("ST", 0, 1))
+        r, o = rows("L", i + 2), (T.ST[0:8, 256:384], ("ST", 0, 1))
         yield group(c("ST", 0, 128), (half("WP", 0), r), (half("WP", 1), r)) + group(o, (c("Ib", 14, 128, 16), r))
         yield ts(half("W1", h), c("ST", 0, 128), 127.5, None, A.add)
         yield ("done", ("w3", h))
-        y = (T.YF[0:8, h * 128:h * 128 + 128], ("YF", h * 128, h * 128 + 128))
+        y = (T.YF[0:8, C128(h)], half("YF", h)[1])
         yield ts(y, o, -16, 7.5, A.mult, A.add)
-        yield out_(T.yf[:, h * 128:h * 128 + 128], y)
+        for k in range(2):
+            yield out_(T.yf[4 * h:4 * h + 4, C128(k)], T.YF[4 * k:4 * k + 4, C128(h)], y[1])
         p = a("HR", T.HR[:, 0, :])
         for x in gather_cuts(("w3", h), p, "Zb", half("W1", h), "R1", 128 * h, []):
             yield x
         yield ts(half("YP", h), p, col(1), None, A.add)
         yield ("done", ("fin", h))
-        yield out_(T.yp[:, h * 128:h * 128 + 128], half("YP", h))
+        for k in range(2):
+            yield out_(T.yp[P64(h), C128(k)], T.YP[P64(k), C128(h)], half("YP", h)[1])
 
     third = [s for s in range(1, 16) if s % 3 == 2]
     rest = [s for s in range(1, 16) if s % 3 != 2]
-    th = [(0, slots()), (1, consts_g()), (2, consts()), (7, consts2()),
-          (0, cuts("w1", c("W1"), "R1", 0, 16, rest, True)), (0, cuts("w1", c("W1"), "R1", 0, 16, third, False))]
-    for h in range(2):
-        th += [(h, first(h)), (h, cuts(("w2", h), half("W2", h), "R2", 128 * h, 1, range(1, 16, 2), False)),
-               (h, cuts(("w2", h), half("W2", h), "R2", 128 * h, 1, range(2, 16, 2), True)), (1, finish(h)),
-               (1, cuts(("w3", h), half("W1", h), "R1", 128 * h, 16, rest if h == 0 else third, True)),
-               (1, cuts(("w3", h), half("W1", h), "R1", 128 * h, 16, third if h == 0 else rest, False))]
-    for i in range(2 * TS):
-        th += [(0, choose(i)), (1, state(i)), (2, columns(i)), (6, gaps(i)), (5, gather_s(i)), (5, gather_v(i)), (4, minus_z(i)), (4, absval(i)),
-               (4, keys(i)), (4, keys_v(i))]
-    th += [(1, count(t)) for t in range(TS)]
-    ev = {("nc", 0), ("gs", -1), ("gv", -1), ("st0", -1), ("st1", -1), ("dl", -1), ("L", -1), ("fin", -1), ("abs", -1), ("abs", -2), ("abs", -3)}
-    live, blocked, held = [], {}, set()
 
-    def pull(rec_):
-        while True:
-            x, rec_[3] = rec_[3] or next(rec_[1], None), None
-            if x is None:
-                return
-            if isinstance(x, tuple) and x[0] in ("done", "unlock"):
-                if x[0] == "done":
-                    ev.add(x[1])
-                else:
-                    held.discard(x[1])
-                for r in blocked.pop(x[1], ()):
-                    pull(r)
-            elif isinstance(x, tuple) and x[0] in ("need", "lock"):
-                if (x[1] not in ev) if x[0] == "need" else (x[1] in held):
-                    rec_[3] = x
-                    blocked.setdefault(x[1], []).append(rec_)
+    def threads():
+        th = [slots(), cuts("w1", c("W1"), "R1", 0, 16, rest, True), cuts("w1", c("W1"), "R1", 0, 16, third, False), consts_g(), consts(), consts2()]
+        th = [(None, 0, x) for x in th]
+        for h in range(2):
+            th += [(h - 2, 0, x) for x in (first(h), cuts(("w2", h), half("W2", h), "R2", 128 * h, 1, range(1, 16, 2), False),
+                                           cuts(("w2", h), half("W2", h), "R2", 128 * h, 1, range(2, 16, 2), True))]
+        for i in range(2 * TS):
+            th += [(i, 2 if f is choose else f in (gather_s, gather_v), f(i)) for f in (choose, state, columns, table, count, gaps, minus_z, absval, keys, keys_v, gather_s, gather_v)]
+        for h in range(2):
+            th += [(2 * TS + h, 0, x) for x in (finish(h), cuts(("w3", h), half("W1", h), "R1", 128 * h, 16, rest if h == 0 else third, True),
+                                                cuts(("w3", h), half("W1", h), "R1", 128 * h, 16, third if h == 0 else rest, False))]
+        return th
+
+    def plan(due):
+        for x in (cnt, hist, left) + tuple(know.values()):
+            x.clear()
+        for q in free:
+            free[q] = 0.0
+        sent[0] = 0
+        begin()
+        ev = {("nc", 0), ("nc", 1), ("gs", -1), ("gv", -1), ("st0", -1), ("st1", -3), ("dl", -1), ("L", -1), ("fin", -1), ("abs", -1), ("abs", -2), ("abs", -3)}
+        live, blocked, held, th, log, t_of, by, after = [], {}, set(), threads(), [], {}, {}, {}
+
+        def pull(r):
+            while True:
+                x, r[3] = r[3] or next(r[1], None), None
+                if x is None:
                     return
-                if x[0] == "lock":
-                    held.add(x[1])
-            else:
-                rec_[2] = x if isinstance(x, list) else [x]
-                live.append(rec_)
-                return
+                if isinstance(x, tuple) and x[0] in ("done", "unlock"):
+                    if x[0] == "done":
+                        ev.add(x[1])
+                        by[x[1]] = r[0]
+                    else:
+                        held.discard(x[1])
+                    for y in blocked.pop(x[1], ()):
+                        pull(y)
+                elif isinstance(x, tuple) and x[0] in ("need", "lock"):
+                    if (x[1] not in ev) if x[0] == "need" else (x[1] in held):
+                        r[3] = x
+                        blocked.setdefault(x[1], []).append(r)
+                        return
+                    if x[0] == "lock":
+                        held.add(x[1])
+                    elif by.get(x[1]) in t_of:
+                        after.setdefault((r[0][0], r[0][1] + 1), []).append(by[x[1]])
+                else:
+                    r[2], r[0] = x if isinstance(x, list) else [x], (r[0][0], r[0][1] + 1)
+                    live.append(r)
+                    return
 
-    for n, (p, gen) in enumerate(th):
-        pull([p * 1000 + n, gen, None, None])
-    while live:
-        best = min(live, key=lambda r: (start(r[2][0]), r[0]))
-        live.remove(best)
-        for d in best[2]:
-            do(d)
-        pull(best)
-    assert not blocked
+        def when(r):
+            t, o = 0.0, 0.0
+            for d in r[2]:
+                t, o = max(t, start(d) - o), o + d[6]
+            return t, o
+
+        for n, x in enumerate(th):
+            pull([(n, 0), x[2], None, None])
+        while live:
+            at = [when(r) + (due.get(r[0], 0.0), r) for r in live]
+            t0 = min(x[0] for x in at)
+            now = min([x for x in at if x[0] == t0], key=lambda x: (x[2], x[3][0]))
+            soon = [x for x in at if x[3][2][0][0] == now[3][2][0][0] and x[2] < now[2] and x[0] < t0 + now[1] and t0 + now[1] > x[2] + SLACK]
+            s, dur, _, best = min(soon, key=lambda x: x[2]) if soon else now
+            live.remove(best)
+            key[0] = best[0]
+            t_of[key[0]] = s
+            pre = [(e[8], e[7] + WAKE - t_of[e[8]]) for d in best[2] for e in needs(d[0], d[2], d[3]) if e[8] in t_of and e[8] != key[0]]
+            log.append((key[0], dur, pre, best[2][0][0]))
+            for d in best[2]:
+                do(d)
+            pull(best)
+        assert not blocked
+        end, nxt_due, queue, durs = FIRST + PERIOD * TS + 4000.0, {}, {x[0]: x[3] for x in log}, {x[0]: x[1] for x in log}
+        for k, dur, pre, q in reversed(log):
+            i = th[k[0]][0]
+            t = min(nxt_due.get(k, end), end - dur)
+            if th[k[0]][1] and k[1] == 1:
+                t = min(t, FIRST + i * PERIOD / 2 + (GATHER if th[k[0]][1] == 2 else 0.0))
+            nxt_due[k] = t
+            before = (k[0], k[1] - 1)
+            for p, lag in pre + [(p, durs[p]) for p in after.get(k, []) + ([before] if before in durs else [])]:
+                j = th[p[0]][0]
+                if j is None or (i is not None and i - j in (0, 2)):
+                    nxt_due[p] = min(nxt_due.get(p, end), t - lag)
+        return nxt_due
+
+    due = {}
+    for n in range(PASSES):
+        dry[0] = n + 1 < PASSES
+        due = plan(due)
     for s in cnt:
         g.wait_ge(sem[s], cnt[s])
-    for t in range(1, TS):
-        for h in range(2):
-            g.wait_ge(sem["a%d%d" % (t, h)], ein)
+    for i in range(2 * TS - 2):
+        for k in range(3):
+            g.wait_ge(sem["a%d%d" % (i, k)], ein * (1 + k % 2))
     g.wait_ge(sem.sent, sent[0])

@@ -3,22 +3,24 @@ from concourse.bass import DstId, RemoteDMATransfer
 
 N, TS = 4, 5
 NV = 10
-WAKE, SHIP = 60.0, (4000.0, 4000.0, 2700.0)
+WAKE, SHIP, TWIN = 60.0, (5000.0, 4500.0, 3200.0), 3500.0
 CY, PE, FIX = 0.85, 0.5, 55.0
-PASSES, AHEAD = 3, 2
-FIRST, PERIOD, GATHER, SLACK = 14000.0, 17000.0, 6300.0, 5000.0
+PASSES, AHEAD, DUE = 6, 2, {}
+FIRST, PERIOD, SKEW, GATHER, HOLD = 12000.0, 17500.0, 8750.0, 6300.0, 150.0
+EARLY, SLACK = 0.0, 0.0
+BULK, URGENT = 0, (0, 0, 0, 0, 0, 0, 0, 0, 0, 0, 0, 0)
 BIG, M1_, M8_ = 2.0 ** 19, 1.5 * 2 ** 23, 1.5 * 2 ** 26
 XN = 2112
 f32, b16, h16, i32, u16 = "float32", "bfloat16", "float16", "int32", "uint16"
 SB_ = {
-    "X": ([2 * XN], b16), "NM": ([256], i32), "PR": ([256], i32), "TH": ([10], i32),
+    "X": ([2 * XN], b16), "NM": ([256], i32), "PR": ([256], i32), "TH": ([16], i32),
     "ONE": ([128], f32), "If": ([8, 16], f32), "BOa": ([128], f32), "BO": ([8, 16], f32), "LT": ([128], b16), "PERM": ([128], b16), "SW": ([128], b16),
     "PI": ([16], i32), "PI2": ([16], i32), "DJ": ([128], i32), "M1": ([128], b16), "COL": ([32], f32), "KC": ([32], f32),
     "Ib": ([128], b16), "nI": ([128], b16), "I2": ([128], b16), "I14": ([128], b16), "Im": ([128], b16), "BOb": ([128], b16), "BO2": ([128], b16),
     "Zf": ([2, 144], f32), "Zb": ([2, 144], b16), "A12": ([256], f32), "SEL": ([256], b16), "D12": ([256], b16), "MV2": ([8, 2], f32),
     "SXY": ([256], b16), "SXa": ([256], b16), "WP": ([256], b16), "CAB": ([128], b16), "PM": ([4, 128], b16),
     "RX": ([3, 8, 2], b16), "RY": ([8], b16), "CK": ([8, 2, 16], b16), "CKi": ([8, 2, 16], f32), "KR": ([8, 2, 16], b16),
-    "TM": ([2, 8, 2, 16], h16), "OB": ([256], b16), "D0": ([256], f32), "RLi": ([8], i32), "RL": ([8], u16),
+    "TM": ([2 * TS * 256], h16), "ME": ([8, 2, 16], b16), "OB": ([256], b16), "D0": ([256], f32), "RLi": ([8], i32), "RL": ([8], u16),
     "JI": ([8], i32), "JC": ([32], b16), "J8": ([48], b16), "IN3": ([32], b16), "MV": ([64], i32), "OH": ([64], b16),
     "MK": ([768], b16), "P16": ([256], b16), "NQ": ([256], h16), "AA": ([512], b16), "W1": ([256], b16), "W2": ([256], f32),
     "R1": ([4096], b16), "R2": ([4096], f32), "OC": ([256], f32),
@@ -200,12 +202,12 @@ def rank_program(g, core, T, topo):
     C128 = lambda k: slice(128 * k, 128 * k + 128)
 
     loads = []
-    for b, src in (("PR", T.pr), ("NM", T.nm)):
-        loads += [("sy" if k else "s", T[b][P64(k), C128(h)], src[P64(h), C128(k)], half(b, h)[1]) for h in range(2) for k in range(2)]
     for h in range(2):
-        loads += [("sy" if k else "s", T.X[P64(k), XN * h:XN * h + 2048], T.xt[P64(h), :], ("X", XN * h + k, XN * h + 2048)) for k in range(2)]
+        loads += [("sy" if k else "s", T[b][P64(k), C128(h)], src[P64(h), C128(k)], half(b, h)[1]) for b, src in (("PR", T.pr), ("NM", T.nm)) for k in range(2)]
+    for h in range(2):
+        loads += [("sy", T.TH[P64(k), 8 * h:8 * h + 5], T.th[P64(h), :], half("TH", h, 8)[1]) for k in range(2)]
+        loads += [("sy", T.X[P64(k), XN * h:XN * h + 2048], T.xt[P64(h), :], ("X", XN * h, XN * h + 2048)) for k in range(2)]
         loads += [("sy", T.ZL[P64(k), C128(3 * h + q)], T.z0[P64(h), C128(k)], half("ZL", 3 * h + q)[1]) for k in range(2) for q in (1, 2)]
-        loads += [("sy", T.TH[P64(k), 5 * h:5 * h + 5], T.th[P64(h), :], ("TH", 0, 10)) for k in range(2)]
 
     def begin():
         key[0] = None
@@ -259,7 +261,7 @@ def rank_program(g, core, T, topo):
         yield fill(c("D0"), 1)
         yield fill(c("D0", 0, 256, 32), 0)
         for k in range(2):
-            yield fill(a("COL", T.COL[P64(k), 8:9]), 1024 * k)
+            yield fill((T.COL[P64(k), 8:9], col(8)[1]), 1024 * k)
         yield gi(c("J8", 8, 24), [[28672, 2], [0, 8]], -14336, 0)
         yield ("done", "iotas")
         for h in range(2):
@@ -269,7 +271,6 @@ def rank_program(g, core, T, topo):
 
     def consts():
         yield ms(c("OB", 0, 128), 1.0)
-        yield ms(a("TM"), 0.0)
         for q in range(2):
             yield act(a("MV2", T.MV2[:, :, q]), IND, F.Copy, scale=4096.0 * (2 * q - 1))
         yield ("need", "cab0")
@@ -299,8 +300,6 @@ def rank_program(g, core, T, topo):
         for q, w in enumerate((512 * BIG, 512.0)):
             yield act(a("KR", T.KR[:, :, q, :]), a("If"), F.Copy, scale=w)
         yield act(half("OB", 1), c("ONE"), F.Copy, scale=32 * BIG)
-        yield ts(c("COL", 16, 26), c("TH"), -1, -1, A.mult, A.add)
-        yield ("done", "th")
         for k in range(2):
             for q in range(2):
                 yield act(a("BO2", T.BO2[P64(k), P64(q)]), a("BO", T.BO[P64(k), 4 * k:4 * k + 4, :]), F.Copy)
@@ -345,23 +344,26 @@ def rank_program(g, core, T, topo):
     def split(o, b, i):
         return ts(names(b, i), o, M1_, -M1_, A.add, A.add), tt(rows(b, i), o, names(b, i), A.subtract)
 
-    def slots():
+    def slots(h):
+        pr, two, p1, p2, p3 = half("PR", h), c("MK", 384 * h, 384 * h + 256), half("SB", h, 256), half("SB", 4 + h), c(("SB", "KP")[h], 0, 128)
+        if h == 0:
+            p3 = half("SB", 8)
         for q, o in enumerate((A.is_gt, A.is_equal)):
-            yield ts(half("MK", q, 256), c("PR"), col(0), None, o)
-        yield group(c("SB", 0, 512), (c("LT"), c("MK", 0, 512)))
-        yield ts(c("P16"), c("PR"), 16, None, A.mult)
-        yield tt(c("AA"), c("SB", 0, 512), c("MK", 0, 512), A.mult)
-        yield group(c("SB", 512, 768), (Ib, c("P16")), (c("I14"), half("MK", 1, 256)), (c("I2"), half("AA", 0, 256)), (Ib, half("AA", 1, 256)))
-        yield ts(half("MK", 2, 256), c("PR"), col(0), None, A.is_lt)
-        yield ts(c("NQ"), c("NM"), -2048, None, A.add)
-        yield cp(c("W1"), c("SB", 512, 768))
-        yield ("done", "w1")
-        for x in gather_cuts("w1", c("SB", 1024, 1280), "Zb", c("W1"), "R1", 0,
-                             [(c("I2"), half("AA", 0, 256)), (Ib, half("MK", 2, 256)), (c("Im"), c("NQ"))]):
+            yield ts(half("MK", 3 * h + q), pr, col(0), None, o)
+        yield group(p1, (c("LT"), two))
+        yield ts(half("P16", h), pr, 16, None, A.mult)
+        yield tt(half("AA", h, 256), p1, two, A.mult)
+        yield group(p2, (Ib, half("P16", h)), (c("I14"), half("MK", 3 * h + 1)), (c("I2"), half("AA", 2 * h)), (Ib, half("AA", 2 * h + 1)))
+        yield cp(half("W1", h), p2)
+        yield ("done", ("w0", h))
+        yield ts(half("MK", 3 * h + 2), pr, col(0), None, A.is_lt)
+        yield ts(half("NQ", h), half("NM", h), -2048, None, A.add)
+        yield ("done", ("w1", h))
+        for x in gather_cuts(("w0", h), p3, "Zb", half("W1", h), "R1", 128 * h,
+                             [(c("I2"), half("AA", 2 * h)), (Ib, half("MK", 3 * h + 2)), (c("Im"), half("NQ", h))]):
             yield x
-        yield ts(c("W2"), c("SB", 1024, 1280), col(2), None, A.add)
-        yield ("done", ("w2", 0))
-        yield ("done", ("w2", 1))
+        yield ts(half("W2", h), p3, col(2), None, A.add)
+        yield ("done", ("w2", h))
 
     def first(h):
         b, key = "TL", ("w2", h)
@@ -410,11 +412,17 @@ def rank_program(g, core, T, topo):
         yield ts(half("OFF", h, 256), a("HR"), c("NC", i, i + 1), None, A.add)
         yield ("done", ("L", i))
 
+    def thresholds():
+        for h in range(2):
+            yield ts(c("COL", 16 + 5 * h, 21 + 5 * h), c("TH", 8 * h, 8 * h + 5), -1, -1, A.mult, A.add)
+        yield ms(a("ME"), 0.0)
+        yield cp(a("ME", T.ME[:, :, 0, 0:14]), a("BO", T.BO[:, :, 0:14]))
+        for i in range(2 * TS):
+            yield ts(half("TM", i, 256), a("ME"), col(16 + 5 * (i % 2) + i // 2), None, A.mult)
+            yield ("done", ("tm", i))
+
     def gaps(i):
-        for k in ("th", ("m", i)):
-            yield ("need", k)
-        yield ts((T.TM[:, i % 2, :, 0, 0:14], ("TM", i % 2, i % 2 + 1)), a("BO", T.BO[:, :, 0:14]), col(16 + 5 * (i % 2) + i // 2), None, A.mult)
-        yield ("done", ("tm", i))
+        yield ("need", ("m", i))
         if i < 2 * TS - 2:
             yield send(i, 0)
         for k in (("L", i), ("gv", i), ("dl", i - 1), ("st1", i - 2), "D12"):
@@ -426,7 +434,7 @@ def rank_program(g, core, T, topo):
     old = lambda i: (names("O", i), half("RO", i), half("LR", i, 16)) if i < 2 * TS - 2 else (names("L", i), rows("L", i), c("LS", 32 * i + 8, 32 * i + 24))
     XW = lambda h: c("X", XN * h, XN * h + XN)
     cut = lambda lo, hi: [(s, min(4, hi - s)) for s in range(lo, hi, 4)]
-    SCH = [(1,) + x for x in cut(0, 14)] + [(0,) + x for x in cut(NV, 14)]
+    SCH = sorted([(1,) + x for x in cut(0, 14)] + [(0,) + x for x in cut(NV, 14)], key=lambda x: -x[2])
     rec = lambda h, y, s, n: c("WW", 4096 * h + 128 * (s + 1 + 16 * (1 - y)), 4096 * h + 128 * (s + n + 1 + 16 * (1 - y)))
     tmp = lambda b, h, s, n: c(b, 2048 * h + 128 * s, 2048 * h + 128 * (s + n))
     offs = lambda h, y, s, n: c("OFF", 256 * h + 128 * y + 8 * s, 256 * h + 128 * y + 8 * (s + n))
@@ -484,9 +492,9 @@ def rank_program(g, core, T, topo):
     def keys(i):
         left[i] = [28 + NV]
         kp = c("KP", 0, 256)
-        for k in (("scan", i - 1), ("L", i), ("m", i), ("tm", i)):
+        for k in (("scan", i - 1), ("L", i), ("m", i), ("tm", i), ("w2", 1)):
             yield ("need", k)
-        yield [mm(kp, half("OB", 0), a("CK"), True, False), mm(kp, half("OB", 1), (T.TM[:, i % 2], ("TM", i % 2, i % 2 + 1)), False, False),
+        yield [mm(kp, half("OB", 0), a("CK"), True, False), mm(kp, half("OB", 1), half("TM", i, 256), False, False),
                mm(kp, rows("L", i), a("KR"), False, False)]
         yield ("done", ("k0", i))
         for j, (y, s, n) in enumerate(SCH):
@@ -566,7 +574,7 @@ def rank_program(g, core, T, topo):
                 for o, x in cps:
                     e.dma_start(o, x).then_inc(sem[s], 16)
             cnt[s] = 64 * (t + 1)
-            yield ("sy", fn, [], [XW(h)[1]], None, 0, 240.0, 0.0, lambda tm: note(s, [], [XW(h)[1]], s, cnt[s], dict(know["sy"]), tm + 2600.0))
+            yield ("sy", fn, [], [XW(h)[1]], None, 0, 240.0, 0.0, lambda tm: note(s, [], [XW(h)[1]], s, cnt[s], dict(know["sy"]), tm + TWIN))
         yield ("done", ("table", i))
 
     def state(i):
@@ -587,18 +595,19 @@ def rank_program(g, core, T, topo):
         t, h = i // 2, i % 2
         yield ("need", ("LS", i))
         yield ts(half("ES", h, 8), c("LS", 32 * i + 8, 32 * i + 16), 16, None, A.is_ge)
-        p = a("TL", T.TL[:, 4, 0:8])
+        p = a("TL", T.TL[:, 4, 0:1])
         yield ("lock", "TL")
-        yield [mm(p, c("BO2"), half("ES", h, 8), True, False), mm(a("TL", T.TL[:, 4, 0:1]), Ib, c("NC", i, i + 1), False, True)]
-        yield op("v", lambda e: e.tensor_reduce(T.AT[:, i:i + 1], p[0], AxisListType.X, A.add), c("AT", i, i + 1), p, dur=FIX + 64 * CY)
+        yield group(p, (Ib, c("NC", i, i + 1)), *[(c("BO2"), c("ES", 8 * h + k, 8 * h + k + 1)) for k in range(8)])
+        yield ts(c("AI", i, i + 1), p, 1 / 64, -63 / 128, A.mult, A.add)
+        yield ts(c("NC", i + 2, i + 3), c("AI", i, i + 1), -64, p, A.mult, A.add)
         yield ("unlock", "TL")
-        if t + 1 < TS:
-            yield ts(c("AI", i, i + 1), c("AT", i, i + 1), 1 / 64, -63 / 128, A.mult, A.add)
-            yield ts(c("NC", i + 2, i + 3), c("AI", i, i + 1), -64, c("AT", i, i + 1), A.mult, A.add)
-            yield ("done", ("nc", i + 2))
-        else:
-            yield tt(c("YE", 8 * h, 8 * h + 5), c("AT", h, 10, 2), c("NC", h, 10, 2), A.subtract)
-            yield out_(T.ye[P64(h), :], T.YE[0:64, 8 * h:8 * h + 5], ("YE", 8 * h, 8 * h + 5))
+        yield ("done", ("nc", i + 2))
+        if t + 1 == TS:
+            ye, at = c("YE", 8 * h, 8 * h + 5), c("AT", 8 * h, 8 * h + 5)
+            yield ts(at, c("AI", h, 10, 2), 64, None, A.mult)
+            yield tt(ye, c("NC", h + 2, 12, 2), c("NC", h, 10, 2), A.subtract)
+            yield tt(ye, ye, at, A.add)
+            yield out_(T.ye[P64(h), :], T.YE[0:64, 8 * h:8 * h + 5], ye[1])
 
     def finish(h):
         i = 2 * (TS - 1) + h
@@ -624,17 +633,19 @@ def rank_program(g, core, T, topo):
     rest = [s for s in range(1, 16) if s % 3 != 2]
 
     def threads():
-        th = [slots(), cuts("w1", c("W1"), "R1", 0, 16, rest, True), cuts("w1", c("W1"), "R1", 0, 16, third, False), consts_g(), consts(), consts2()]
-        th = [(None, 0, x) for x in th]
+        th = [(None, 0, x) for x in (consts_g(), consts(), consts2(), thresholds())]
         for h in range(2):
-            th += [(h - 2, 0, x) for x in (first(h), cuts(("w2", h), half("W2", h), "R2", 128 * h, 1, range(1, 16, 2), False),
+            th += [(h - 2, 0, x) for x in (slots(h), cuts(("w0", h), half("W1", h), "R1", 128 * h, 16, rest, True),
+                                           cuts(("w0", h), half("W1", h), "R1", 128 * h, 16, third, False), first(h), cuts(("w2", h), half("W2", h), "R2", 128 * h, 1, range(1, 16, 2), False),
                                            cuts(("w2", h), half("W2", h), "R2", 128 * h, 1, range(2, 16, 2), True))]
         for i in range(2 * TS):
             th += [(i, 2 if f is choose else f in (gather_s, gather_v), f(i)) for f in (choose, state, columns, table, count, gaps, minus_z, absval, keys, keys_v, gather_s, gather_v)]
         for h in range(2):
             th += [(2 * TS + h, 0, x) for x in (finish(h), cuts(("w3", h), half("W1", h), "R1", 128 * h, 16, rest if h == 0 else third, True),
                                                 cuts(("w3", h), half("W1", h), "R1", 128 * h, 16, third if h == 0 else rest, False))]
-        return th
+        return [x + (y,) for x, y in zip(th, [BULK] * 4 + [0] * 12 + list(URGENT) * 2 * TS + [0] * 6)]
+
+    took = [0.0]
 
     def plan(due):
         for x in (cnt, hist, left) + tuple(know.values()):
@@ -682,10 +693,10 @@ def rank_program(g, core, T, topo):
         for n, x in enumerate(th):
             pull([(n, 0), x[2], None, None])
         while live:
-            at = [when(r) + (due.get(r[0], 0.0), r) for r in live]
+            at = [when(r) + ((th[r[0][0]][3], due.get(r[0], 0.0)), r) for r in live]
             t0 = min(x[0] for x in at)
             now = min([x for x in at if x[0] == t0], key=lambda x: (x[2], x[3][0]))
-            soon = [x for x in at if x[3][2][0][0] == now[3][2][0][0] and x[2] < now[2] and x[0] < t0 + now[1] and t0 + now[1] > x[2] + SLACK]
+            soon = [x for x in at if x[3][2][0][0] == now[3][2][0][0] and x[2] < now[2] and x[0] < t0 + min(HOLD, now[1]) and x[2][1] < t0 + now[1] + SLACK]
             s, dur, _, best = min(soon, key=lambda x: x[2]) if soon else now
             live.remove(best)
             key[0] = best[0]
@@ -696,12 +707,13 @@ def rank_program(g, core, T, topo):
                 do(d)
             pull(best)
         assert not blocked
-        end, nxt_due, queue, durs = FIRST + PERIOD * TS + 4000.0, {}, {x[0]: x[3] for x in log}, {x[0]: x[1] for x in log}
+        took[0] = max(t_of.values())
+        end, nxt_due, queue, durs = took[0], {}, {x[0]: x[3] for x in log}, {x[0]: x[1] for x in log}
         for k, dur, pre, q in reversed(log):
             i = th[k[0]][0]
             t = min(nxt_due.get(k, end), end - dur)
             if th[k[0]][1] and k[1] == 1:
-                t = min(t, FIRST + i * PERIOD / 2 + (GATHER if th[k[0]][1] == 2 else 0.0))
+                t = min(t, t_of[k] - EARLY * (i + 1) if due else FIRST + i // 2 * PERIOD + i % 2 * SKEW + (GATHER if th[k[0]][1] == 2 else 0.0))
             nxt_due[k] = t
             before = (k[0], k[1] - 1)
             for p, lag in pre + [(p, durs[p]) for p in after.get(k, []) + ([before] if before in durs else [])]:
@@ -710,10 +722,16 @@ def rank_program(g, core, T, topo):
                     nxt_due[p] = min(nxt_due.get(p, end), t - lag)
         return nxt_due
 
-    due = {}
-    for n in range(PASSES):
-        dry[0] = n + 1 < PASSES
-        due = plan(due)
+    if not DUE:
+        due, best = plan({}), None
+        for n in range(PASSES):
+            nxt_ = plan(due)
+            if best is None or took[0] < best[0]:
+                best = (took[0], due)
+            due = nxt_
+        DUE.update(best[1])
+    dry[0] = False
+    plan(DUE)
     for s in cnt:
         g.wait_ge(sem[s], cnt[s])
     for i in range(2 * TS - 2):

@@ -3,28 +3,30 @@ from concourse.bass import DstId, RemoteDMATransfer
 
 N, TS = 4, 5
 NV = 10
-WAKE, SHIP, TWIN = 60.0, (5000.0, 4500.0, 3200.0), 3500.0
+WAKE, SHIP, TWIN = 130.0, (6000.0, 4500.0, 3300.0), 3600.0
 CY, PE, FIX = 0.85, 0.5, 55.0
-PASSES, AHEAD, DUE = 6, 2, {}
-FIRST, PERIOD, SKEW, GATHER, HOLD = 12000.0, 17500.0, 8750.0, 6300.0, 150.0
+PASSES, AHEAD, DUE = 5, 2, {}
+FIRST, PERIOD, SKEW, GATHER, HOLD = 12000.0, 17500.0, 8750.0, 6300.0, 60.0
 EARLY, SLACK = 0.0, 0.0
-BULK, URGENT = 0, (0, 0, 0, 0, 0, 0, 0, 0, 0, 0, 0, 0)
+BULK, URGENT = 0, (-1, -1, -1, 0, 0, 0, 0, 0, 0, 0, 0, 0, 0)
+NA, GM, US, LAST = 0, 1.2, 0, 9000.0
+ON_V, UQ = (), ("p", "gq")
 BIG, M1_, M8_ = 2.0 ** 19, 1.5 * 2 ** 23, 1.5 * 2 ** 26
 XN = 2112
 f32, b16, h16, i32, u16 = "float32", "bfloat16", "float16", "int32", "uint16"
 SB_ = {
     "X": ([2 * XN], b16), "NM": ([256], i32), "PR": ([256], i32), "TH": ([16], i32),
-    "ONE": ([128], f32), "If": ([8, 16], f32), "BOa": ([128], f32), "BO": ([8, 16], f32), "LT": ([128], b16), "PERM": ([128], b16), "SW": ([128], b16),
+    "ONE": ([128], f32), "If": ([8, 16], f32), "BOa": ([128], f32), "BO": ([8, 16], f32), "LT": ([128], b16), "PERM": ([128], b16), "Ih": ([128], b16), "CZ": ([256], b16), "PK": ([256], b16),
     "PI": ([16], i32), "PI2": ([16], i32), "DJ": ([128], i32), "M1": ([128], b16), "COL": ([32], f32), "KC": ([32], f32),
     "Ib": ([128], b16), "nI": ([128], b16), "I2": ([128], b16), "I14": ([128], b16), "Im": ([128], b16), "BOb": ([128], b16), "BO2": ([128], b16),
     "Zf": ([2, 144], f32), "Zb": ([2, 144], b16), "A12": ([256], f32), "SEL": ([256], b16), "D12": ([256], b16), "MV2": ([8, 2], f32),
     "SXY": ([256], b16), "SXa": ([256], b16), "WP": ([256], b16), "CAB": ([128], b16), "PM": ([4, 128], b16),
-    "RX": ([3, 8, 2], b16), "RY": ([8], b16), "CK": ([8, 2, 16], b16), "CKi": ([8, 2, 16], f32), "KR": ([8, 2, 16], b16),
+    "RX": ([3, 8, 2], b16), "RY": ([8], b16), "CK": ([8, 2, 16], b16), "CKi": ([8, 2, 16], f32), "KR": ([8, 2, 16], b16), "KZ": ([8, 2, 16], b16),
     "TM": ([2 * TS * 256], h16), "ME": ([8, 2, 16], b16), "OB": ([256], b16), "D0": ([256], f32), "RLi": ([8], i32), "RL": ([8], u16),
     "JI": ([8], i32), "JC": ([32], b16), "J8": ([48], b16), "IN3": ([32], b16), "MV": ([64], i32), "OH": ([64], b16),
     "MK": ([768], b16), "P16": ([256], b16), "NQ": ([256], h16), "AA": ([512], b16), "W1": ([256], b16), "W2": ([256], f32),
     "R1": ([4096], b16), "R2": ([4096], f32), "OC": ([256], f32),
-    "NL": ([1536], h16), "NO": ([1024], h16), "RO": ([1024], b16), "LR": ([128], u16), "ZL": ([4608], b16), "ZS": ([3840], b16),
+    "NL": ([3072], h16), "NO": ([2048], h16), "LR": ([128], u16), "ZL": ([4608], b16), "ZS": ([3840], b16),
     "PP": ([512], f32), "QQ": ([512], i32), "HB": ([512], i32), "HF": ([512], h16), "HT": ([2, 2, 128], h16), "DL": ([512], f32), "TT": ([512], f32),
     "OFF": ([512], u16), "WW": ([8192], b16), "AY": ([4096], b16), "XR": ([4096], b16), "RU": ([4096], b16),
     "SC": ([512], f32), "FF": ([16], f32), "SE": ([16], i32), "KQ": ([16], i32), "GM": ([256], b16), "LS": ([320], u16), "ES": ([16], b16),
@@ -32,9 +34,9 @@ SB_ = {
     "AT": ([16], f32), "NC": ([16], b16), "AI": ([16], i32), "YE": ([16], f32), "YP": ([256], f32), "YF": ([256], f32),
 }
 SCRATCH = {k: ("sbuf", [128] + v[0], v[1]) for k, v in SB_.items()}
-SCRATCH.update({"SB": ("psum", [128, 1536], f32), "KP": ("psum", [128, 512], f32), "HR": ("psum", [128, 2, 128], f32),
+SCRATCH.update({"SB": ("psum", [128, 2048], f32), "KP": ("psum", [128, 512], f32),
                 "ST": ("psum", [128, 1024], f32), "TL": ("psum", [128, 32, 16], f32)})
-PSUM = ("SB", "KP", "ST", "TL", "HR")
+PSUM = ("SB", "KP", "ST", "TL")
 SEMAPHORES = ["v", "p", "s", "gq", "sent", "out"] + ["tw0", "tw1"] + ["l%d" % k for k in range(24)] + ["a%d%d" % (i, k) for i in range(2 * TS - 2) for k in range(3)]
 
 
@@ -44,7 +46,7 @@ def rank_program(g, core, T, topo):
         return
     sem = T.sem
     Q = {"v": g.vector, "p": g.tensor, "s": g.scalar, "gq": g, "sy": g.sync}
-    cnt, know, hist, free, dry, key = {}, {q: {} for q in Q}, {}, {q: 0.0 for q in Q}, [True], [None]
+    ver, cnt, know, hist, free, dry, key = {}, {}, {q: {} for q in Q}, {}, {q: 0.0 for q in Q}, [True], [None]
 
     def needs(q, rd, wr):
         out = []
@@ -70,6 +72,7 @@ def rank_program(g, core, T, topo):
         for regs, w in ((rd, False), (wr, True)):
             for (b, lo, hi) in regs:
                 old = [e for e in hist.get(b, []) if not (lo <= e[1] and e[2] <= hi and (w or (e[0] == q and not e[3])))]
+                ver[b] = ver.get(b, 0) + 1000
                 hist[b] = old + [(q, lo, hi, w, s, n, snap, fin, key[0])]
 
     def do(d):
@@ -121,6 +124,7 @@ def rank_program(g, core, T, topo):
 
     def tt(out, x, y, o):
         d = span(out, x, 1 if x[1][0] in PSUM or y[1][0] in PSUM else 2)
+        d = GM * (d - FIX) + FIX if len(x) > 2 else d
         return op("v", lambda e: e.tensor_tensor(out[0], x[0], y[0], o), out, x, y, dur=d)
 
     def ts(out, x, s1, s2, o0, o1=None):
@@ -177,22 +181,19 @@ def rank_program(g, core, T, topo):
 
     def send(i, k):
         rid, pid = topo.addr(nxt, core)
-        en, to, s = topo.engines(core, nxt)[:8], DstId(rid=rid, pnc=pid), "a%d%d" % (i, k)
+        en, s = topo.engines(core, nxt)[:8], "a%d%d" % (i, k)
         sent[0] += len(en)
         mask = lambda es: sum(1 << x for x in es)
-        if k == 0:
-            src, dst, n = [names("L", i), rows("L", i)], [names("O", i), half("RO", i)], len(en) // 2
-            tr = [RemoteDMATransfer(dst_ids=[to], dma_engine_mask=mask(en[n * q:n * q + n]), remote_sem=sem[s], src=src[q][0], dst=dst[q][0]) for q in range(2)]
-        else:
-            src, dst = ([zed("S", i)], [half("ZL", 3 * i + 7 + q) for q in range(2)]) if k == 1 else ([c("LS", 32 * i + 8, 32 * i + 24)], [half("LR", i, 16)])
-            tr = [RemoteDMATransfer(dst_ids=[to] * len(dst), dma_engine_mask=mask(en), remote_sem=sem[s], srcs=[src[0][0]], dsts=[x[0] for x in dst])]
-        return ("gq", lambda e: e.remote_dma_fused(tr, local_sem=sem.sent), [x[1] for x in src], [], None, 0, 1000.0, 0.0,
-                lambda t: note("rem", [], [x[1] for x in dst], s, ein * (1 + k % 2), {}, t + SHIP[k]))
+        src, dst = ((half("NL", i, 256), half("NO", i, 256)), (zed("S", i), zed("L", i + 2)), (c("LS", 32 * i + 8, 32 * i + 24), half("LR", i, 16)))[k]
+        dst = [dst, half("ZL", 3 * i + 8)] if k == 1 else [dst]
+        tr = [RemoteDMATransfer(dst_ids=[DstId(rid=rid, pnc=pid)] * len(dst), dma_engine_mask=mask(en), remote_sem=sem[s], srcs=[src[0]], dsts=[x[0] for x in dst])]
+        return ("gq", lambda e: e.remote_dma_fused(tr, local_sem=sem.sent), [src[1]], [], None, 0, 1000.0, 0.0,
+                lambda t: note("rem", [], [x[1] for x in dst], s, ein * len(dst), {}, t + SHIP[k]))
 
     half = lambda b, h, n=128: c(b, h * n, h * n + n)
     col = lambda j: c("COL", j, j + 1)
-    names = lambda b, i: half("N" + b, i)
-    rows = lambda b, i: half("Z" + b, 3 * i)
+    names = lambda b, i: half("N" + b, 2 * i)
+    rows = lambda b, i: half("N" + b, 2 * i + 1)
     zed = lambda b, i: half("Z" + b, 3 * i + 1)
     Ib, nI, IND, u0 = c("Ib"), c("nI"), a("BO", T.BO[:, :, 0]), c("PI2", 0, 1)
     CS = lambda b, s: a(b, T[b][:, 0, 15 - s:143 - s])
@@ -293,8 +294,8 @@ def rank_program(g, core, T, topo):
 
     def consts2():
         yield ("need", "pm")
-        for n, k in enumerate((1.0, 2.0, -1.0)):
-            for q, w in enumerate((512 * BIG, -512.0)):
+        for q, w in enumerate((512 * BIG, -512.0)):
+            for n, k in enumerate((1.0, 2.0, -1.0)):
                 yield act(a("RX", T.RX[:, n, :, q]), IND, F.Copy, scale=k * w)
         yield act(c("RY"), IND, F.Copy, scale=-512 * BIG)
         for q, w in enumerate((512 * BIG, 512.0)):
@@ -387,7 +388,7 @@ def rank_program(g, core, T, topo):
     def columns(i):
         h = i % 2
         nm_ = names("L", i)
-        for k in (("n", i), "SXY", ("st0", i - 1)):
+        for k in (("n", i), "SXY", ("L", i - 1)):
             yield ("need", k)
         yield group(c("ST", 0, 128), (c("PERM"), nm_)) + group(c("ST", 128, 256), (SEL14, nm_)) + \
             group(c("ST", 256, 384), (half("SXY", 0), nm_)) + group(c("ST", 384, 512), (half("SXY", 1), nm_))
@@ -406,10 +407,10 @@ def rank_program(g, core, T, topo):
             for x4 in range(2):
                 for g2 in range(2):
                     w = ib * 32 + g2 * 16
-                    p.append(mm(a("HR", T.HR[:, :, 2 * ib + x4:128:8]), a("PM", T.PM[:, 2 * x4 + g2]), (T.HT[:, h, :, w:w + 16], ht[1]), g2 == 0, g2 == 1))
+                    p.append(mm(c("ST", 2 * ib + x4, 256, 8), a("PM", T.PM[:, 2 * x4 + g2]), (T.HT[:, h, :, w:w + 16], ht[1]), g2 == 0, g2 == 1))
             yield p
         yield ("need", ("nc", i))
-        yield ts(half("OFF", h, 256), a("HR"), c("NC", i, i + 1), None, A.add)
+        yield ts(half("OFF", h, 256), c("ST", 0, 256), c("NC", i, i + 1), None, A.add)
         yield ("done", ("L", i))
 
     def thresholds():
@@ -431,10 +432,11 @@ def rank_program(g, core, T, topo):
         yield act(half("DL", i % 2, 256), c("ST", 512, 768), F.Copy)
         yield ("done", ("dl", i))
 
-    old = lambda i: (names("O", i), half("RO", i), half("LR", i, 16)) if i < 2 * TS - 2 else (names("L", i), rows("L", i), c("LS", 32 * i + 8, 32 * i + 24))
+    old = lambda i: (names("O", i), rows("O", i), half("LR", i, 16)) if i < 2 * TS - 2 else (names("L", i), rows("L", i), c("LS", 32 * i + 8, 32 * i + 24))
     XW = lambda h: c("X", XN * h, XN * h + XN)
     cut = lambda lo, hi: [(s, min(4, hi - s)) for s in range(lo, hi, 4)]
     SCH = sorted([(1,) + x for x in cut(0, 14)] + [(0,) + x for x in cut(NV, 14)], key=lambda x: -x[2])
+    on_v = lambda j: j in ON_V
     rec = lambda h, y, s, n: c("WW", 4096 * h + 128 * (s + 1 + 16 * (1 - y)), 4096 * h + 128 * (s + n + 1 + 16 * (1 - y)))
     tmp = lambda b, h, s, n: c(b, 2048 * h + 128 * s, 2048 * h + 128 * (s + n))
     offs = lambda h, y, s, n: c("OFF", 256 * h + 128 * y + 8 * s, 256 * h + 128 * y + 8 * (s + n))
@@ -451,6 +453,8 @@ def rank_program(g, core, T, topo):
             yield x
         yield ("need", ("gs", i - 1))
         for j, (y, s, n) in enumerate(SCH):
+            if on_v(j):
+                continue
             if j >= AHEAD:
                 yield ("need", ("abs", i * len(SCH) + j - AHEAD))
             yield act(raw(i % 2, y, s, n), ind(XW(i % 2), offs(i % 2, y, s, n)), F.Copy, bias=-128.0 * y)
@@ -462,27 +466,46 @@ def rank_program(g, core, T, topo):
         for x in ready(i):
             yield x
         yield ("need", ("gv", i - 1))
+        for j, (y, s, n) in enumerate(SCH):
+            if on_v(j):
+                yield ts(raw(h, y, s, n), ind(XW(h), offs(h, y, s, n)), -128.0 * y, None, A.add)
+                yield ("done", ("g", i, j))
         for s, n in cut(0, NV):
             for k in range(s, s + n, 2):
                 yield tt(rec(h, 0, k, 2), ind(XW(h), offs(h, 0, k, 2)), c("ZL", 384 * i + 128, 384 * i + 384), A.subtract)
-            yield ts(tmp("RU", h, s, n), rec(h, 0, s, n), 0, None, A.max)
-            yield ("done", ("ru", i, s))
+            if s >= NA:
+                yield ts(tmp("RU", h, s, n), rec(h, 0, s, n), 0, None, A.max)
+            yield ("done", ("ru" if s >= NA else "dx", i, s))
         yield ("done", ("gv", i))
+
+    def abs_x(i):
+        for s, n in cut(0, NA):
+            yield ("need", ("dx", i, s))
+            yield act(rec(i % 2, 0, s, n), rec(i % 2, 0, s, n), F.Abs)
+            yield ("done", ("ru", i, s))
+
+    def keys_v(i):
+        yield ("need", ("k0", i))
+        for s, n in cut(0, NV):
+            yield ("need", ("ru", i, s))
+            yield [mm(KP(k, True), x, a("RX", T.RX[:, q]), False, left[i]) for k in range(s, s + n)
+                   for q, x in (((2, rec(i % 2, 0, k, 1)), (1, tmp("RU", i % 2, k, 1))) if s >= NA else ((0, rec(i % 2, 0, k, 1)),))]
+        yield ("done", ("kv", i))
 
     def minus_z(i):
         for j, (y, s, n) in enumerate(SCH):
             J = i * len(SCH) + j
-            b = 512 * (J % 3)
+            b = 512 * (J % 4)
             yield ("need", ("g", i, j))
-            yield ("need", ("abs", J - 3))
+            yield ("need", ("abs", J - 4))
             yield [mm(c("SB", b, b + 128 * n), Ib, raw(i % 2, y, s, n), True, False)] + \
-                [mm(c("SB", b + 128 * r, b + 128 * r + 128), nI, zed("L", i), False, r == n - 1) for r in range(n)]
+                [mm(c("SB", b + 128 * r, b + 128 * r + 256), nI, c("ZL", 384 * i + 128, 384 * i + 384), False, r == n - 2) for r in range(0, n, 2)]
             yield ("done", ("d", J))
 
     def absval(i):
         for j, (y, s, n) in enumerate(SCH):
             J = i * len(SCH) + j
-            b = 512 * (J % 3)
+            b = 512 * (J % 4)
             yield ("need", ("d", J))
             yield act(mag(i % 2, y, s, n), c("SB", b, b + 128 * n), F.Abs, bias=col(15) if y else 0.0)
             yield ("done", ("abs", J))
@@ -490,7 +513,7 @@ def rank_program(g, core, T, topo):
     KP = lambda s, both: c("KP", s, 256, 16 if both else 32)
 
     def keys(i):
-        left[i] = [28 + NV]
+        left[i] = [28 + NV - min(NA, NV)]
         kp = c("KP", 0, 256)
         for k in (("scan", i - 1), ("L", i), ("m", i), ("tm", i), ("w2", 1)):
             yield ("need", k)
@@ -501,14 +524,6 @@ def rank_program(g, core, T, topo):
             yield ("need", ("abs", i * len(SCH) + j))
             yield [mm(KP(k, not y), mag(i % 2, y, k, 1), c("RY") if y else a("RX", T.RX[:, 0]), False, left[i]) for k in range(s, s + n)]
         yield ("done", ("ks", i))
-
-    def keys_v(i):
-        yield ("need", ("k0", i))
-        for s, n in cut(0, NV):
-            yield ("need", ("ru", i, s))
-            yield [mm(KP(k, True), x, a("RX", T.RX[:, q]), False, left[i]) for k in range(s, s + n)
-                   for q, x in ((2, rec(i % 2, 0, k, 1)), (1, tmp("RU", i % 2, k, 1)))]
-        yield ("done", ("kv", i))
 
     def choose(i):
         h = i % 2
@@ -554,8 +569,8 @@ def rank_program(g, core, T, topo):
         p1 = a("TL", T.TL[:, 2, 0:8])
         yield ("lock", "TL")
         yield group(p1, (c("Im"), half("J8", 1, 8)), *[(CS("Zb", k), c("ZS", 384 * i + 128 + k, 384 * i + 256, 16)) for k in range(16)])
-        yield act(half("UU", h, 8), p1, F.Copy)
-        yield ts(half("K8", h, 8), half("UU", h, 8), M8_, -M8_, A.add, A.add)
+        yield ts(half("K8", h, 8), p1, M8_, -M8_, A.add, A.add)
+        yield act(half("UU", h, 8), p1, F.Copy) if US else cp(half("UU", h, 8), p1)
         yield group(p1, (Ib, half("J8", 0, 8)), (c("Im"), half("J8", 2, 8)), (a("If"), half("UU", h, 8)), (nI, half("K8", h, 8)))
         yield cp(half("LC", h, 8), p1)
         yield ("unlock", "TL")
@@ -579,9 +594,10 @@ def rank_program(g, core, T, topo):
 
     def state(i):
         h = i % 2
-        for k in (("LR", i), ("dl", i), ("st1", i - 1)):
-            yield ("need", k)
+        yield ("need", ("LR", i))
+        yield ("need", ("dl", i))
         yield tt(half("TT", h, 256), ind(c("OH"), old(i)[2]), half("DL", h, 256), A.mult)
+        yield ("need", ("st1", i - 1))
         o = c("ST", 768, 896)
         yield group(o, (Ib, old(i)[0]), (Ib, old(i)[1]), (half("A12", 0), half("TT", 2 * h)), (half("A12", 1), half("TT", 2 * h + 1)))
         n, r = split(o, "L", i + 2)
@@ -621,7 +637,7 @@ def rank_program(g, core, T, topo):
         yield ts(y, o, -16, 7.5, A.mult, A.add)
         for k in range(2):
             yield out_(T.yf[4 * h:4 * h + 4, C128(k)], T.YF[4 * k:4 * k + 4, C128(h)], y[1])
-        p = a("HR", T.HR[:, 0, :])
+        p = c("ST", 384, 512)
         for x in gather_cuts(("w3", h), p, "Zb", half("W1", h), "R1", 128 * h, []):
             yield x
         yield ts(half("YP", h), p, col(1), None, A.add)
@@ -639,7 +655,7 @@ def rank_program(g, core, T, topo):
                                            cuts(("w0", h), half("W1", h), "R1", 128 * h, 16, third, False), first(h), cuts(("w2", h), half("W2", h), "R2", 128 * h, 1, range(1, 16, 2), False),
                                            cuts(("w2", h), half("W2", h), "R2", 128 * h, 1, range(2, 16, 2), True))]
         for i in range(2 * TS):
-            th += [(i, 2 if f is choose else f in (gather_s, gather_v), f(i)) for f in (choose, state, columns, table, count, gaps, minus_z, absval, keys, keys_v, gather_s, gather_v)]
+            th += [(i, 2 if f is choose else f in (gather_s, gather_v), f(i)) for f in (choose, state, columns, table, count, gaps, minus_z, absval, keys, gather_s, gather_v, keys_v, abs_x)]
         for h in range(2):
             th += [(2 * TS + h, 0, x) for x in (finish(h), cuts(("w3", h), half("W1", h), "R1", 128 * h, 16, rest if h == 0 else third, True),
                                                 cuts(("w3", h), half("W1", h), "R1", 128 * h, 16, third if h == 0 else rest, False))]
@@ -654,7 +670,7 @@ def rank_program(g, core, T, topo):
             free[q] = 0.0
         sent[0] = 0
         begin()
-        ev = {("nc", 0), ("nc", 1), ("gs", -1), ("gv", -1), ("st0", -1), ("st1", -3), ("dl", -1), ("L", -1), ("fin", -1), ("abs", -1), ("abs", -2), ("abs", -3)}
+        ev = {("nc", 0), ("nc", 1), ("gs", -1), ("gv", -1), ("st0", -1), ("st1", -3), ("dl", -1), ("L", -1), ("fin", -1), ("abs", -1), ("abs", -2), ("abs", -3), ("abs", -4)}
         live, blocked, held, th, log, t_of, by, after = [], {}, set(), threads(), [], {}, {}, {}
 
         def pull(r):
@@ -681,22 +697,26 @@ def rank_program(g, core, T, topo):
                         after.setdefault((r[0][0], r[0][1] + 1), []).append(by[x[1]])
                 else:
                     r[2], r[0] = x if isinstance(x, list) else [x], (r[0][0], r[0][1] + 1)
+                    r[5] = {y[0] for d in r[2] for y in list(d[2]) + list(d[3])}
                     live.append(r)
                     return
 
         def when(r):
-            t, o = 0.0, 0.0
-            for d in r[2]:
-                t, o = max(t, start(d) - o), o + d[6]
-            return t, o
+            seen = (r[0], sum(len(hist.get(b, ())) + ver.get(b, 0) for b in r[5]))
+            if r[4][0] != seen:
+                t, o = 0.0, 0.0
+                for d in r[2]:
+                    t, o = max([t] + [e[7] + WAKE - o for e in needs(d[0], d[2], d[3])]), o + d[6]
+                r[4] = (seen, t, o)
+            return max(free[r[2][0][0]], r[4][1]), r[4][2]
 
         for n, x in enumerate(th):
-            pull([(n, 0), x[2], None, None])
+            pull([(n, 0), x[2], None, None, (None,), None])
         while live:
-            at = [when(r) + ((th[r[0][0]][3], due.get(r[0], 0.0)), r) for r in live]
+            at = [when(r) + ((th[r[0][0]][3] if r[2][0][0] in UQ else 0, due.get(r[0], 0.0)), r) for r in live]
             t0 = min(x[0] for x in at)
             now = min([x for x in at if x[0] == t0], key=lambda x: (x[2], x[3][0]))
-            soon = [x for x in at if x[3][2][0][0] == now[3][2][0][0] and x[2] < now[2] and x[0] < t0 + min(HOLD, now[1]) and x[2][1] < t0 + now[1] + SLACK]
+            soon = [x for x in at if x[3][2][0][0] == now[3][2][0][0] and x[2] < now[2] and x[0] < t0 + min(HOLD, now[1]) and (x[2][0] < now[2][0] or x[2][1] < t0 + now[1] + SLACK)]
             s, dur, _, best = min(soon, key=lambda x: x[2]) if soon else now
             live.remove(best)
             key[0] = best[0]
@@ -711,14 +731,14 @@ def rank_program(g, core, T, topo):
         end, nxt_due, queue, durs = took[0], {}, {x[0]: x[3] for x in log}, {x[0]: x[1] for x in log}
         for k, dur, pre, q in reversed(log):
             i = th[k[0]][0]
-            t = min(nxt_due.get(k, end), end - dur)
+            t = min(nxt_due.get(k, end), end - dur - (LAST if i in (2 * TS - 2, 2 * TS) else 0.0))
             if th[k[0]][1] and k[1] == 1:
                 t = min(t, t_of[k] - EARLY * (i + 1) if due else FIRST + i // 2 * PERIOD + i % 2 * SKEW + (GATHER if th[k[0]][1] == 2 else 0.0))
             nxt_due[k] = t
             before = (k[0], k[1] - 1)
             for p, lag in pre + [(p, durs[p]) for p in after.get(k, []) + ([before] if before in durs else [])]:
                 j = th[p[0]][0]
-                if j is None or (i is not None and i - j in (0, 2)):
+                if j is None or (i is not None and i - j in (0, 2)) or p in after.get(k, ()):
                     nxt_due[p] = min(nxt_due.get(p, end), t - lag)
         return nxt_due
 

@@ -1,43 +1,257 @@
+import math
 from concourse.mybir import dt, AluOpType as A, AxisListType, ActivationFunctionType as F
 from concourse.bass import DstId, RemoteDMATransfer
 
 N, TS = 4, 5
-NV = 10
-WAKE, SHIP, TWIN = 130.0, (6000.0, 4500.0, 3300.0), 3600.0
-CY, PE, FIX = 0.85, 0.5, 55.0
-PASSES, AHEAD, DUE = 5, 2, {}
-FIRST, PERIOD, SKEW, GATHER, HOLD = 12000.0, 17500.0, 8750.0, 6300.0, 60.0
-EARLY, SLACK = 0.0, 0.0
-BULK, URGENT = 0, (-1, -1, -1, 0, 0, 0, 0, 0, 0, 0, 0, 0, 0)
-NA, GM, US, LAST = 0, 1.2, 0, 9000.0
-ON_V, UQ = (), ("p", "gq")
-BIG, M1_, M8_ = 2.0 ** 19, 1.5 * 2 ** 23, 1.5 * 2 ** 26
-XN = 2112
+WAKE, CALL, SHIP, LOAD, ROW, RATE = 135.0, 1000.0, 2800.0, 1800.0, 40.0, 20.0
+CY, PE, FV, FS, GA, SCA = 0.85, 0.46, 47.0, 75.0, 1.75, 3.8
+ROUNDS, SKEWS, SWAPS, HEAT = 0, (), 15000, 50.0
+MARK, NEAR, HOLDS, WIDE = 0.2, 40, (100.0, 150.0, 220.0), 30
+AGAIN = 6
+PERIODS, START, STRETCH, LAST = ((12000.0, 6000.0), (13000.0, 6500.0), (14000.0, 7000.0)), 19000.0, 1.5, 8000.0
+HALF, LATE = 0, 500.0
+PLAN = {"SC0": 0, "FF0": .35, "SE0": .6, "KQ0": .84, "KL0": 1.05, "GM0": 1.16, "LS0": 1.7, "A20": 3.06, "ZS0": 3.28, "K80": 4.26, "UU0": 4.36, "TT0": 4.47, "TT1": 4.74,
+        "LC0": 5.19, "SX0": 5.2, "NL0": 5.82, "PP0": 6.47, "PP1": 6.63, "X0": 6.8, "NL1": 9.2, "TR0": 9.4, "KK0": 7.73, "OFF0": 8.9, "NC0": 8.65,
+        "MX0": 1.81, "MX1": 2.3, "MX2": 2.79, "MX3": 3.77, "MX4": 5.32, "MX5": 5.98, "MX6": 7.9, "MX7": 8.2,
+        "DL0": 0, "PK0": 1.98, "AW0": 2.68, "XO0": 5.41, "HX0": 6.0, "JK0": 5.2, "AI0": 7.4,
+        "WW0": .6, "WW1": 1.3, "WW2": 2.24, "WW3": 2.89, "WW4": 3.66, "WW5": 4.44, "WW6": 5.87, "WW7": 6.64}
+ORDER = {}
+ON = {"k8": "v", "a192": "v", "avg": "s", "mod": "p", "u": "v", "old": "v", "rows": "p"}
+CH = ((1, 0, 2, "v"), (1, 2, 4, "s"), (1, 6, 4, "s"), (1, 10, 4, "s"), (0, 0, 4, "s"), (0, 4, 4, "s"), (0, 8, 4, "s"), (0, 12, 2, "s"))
+MORE = {}
+NB = sum(x[2] for x in CH if x[3] == "b")
+BIG, M1_, MK_ = 2.0 ** 20, 1.5 * 2 ** 23, 1.5 * 2 ** 39
+KAP = 0.0 if ON["mod"] == "v" else 1024 - 31 / 64
+BOTH, G1, ALL = False, "T2", 16
+XN = 2176
 f32, b16, h16, i32, u16 = "float32", "bfloat16", "float16", "int32", "uint16"
 SB_ = {
-    "X": ([2 * XN], b16), "NM": ([256], i32), "PR": ([256], i32), "TH": ([16], i32),
-    "ONE": ([128], f32), "If": ([8, 16], f32), "BOa": ([128], f32), "BO": ([8, 16], f32), "LT": ([128], b16), "PERM": ([128], b16), "Ih": ([128], b16), "CZ": ([256], b16), "PK": ([256], b16),
-    "PI": ([16], i32), "PI2": ([16], i32), "DJ": ([128], i32), "M1": ([128], b16), "COL": ([32], f32), "KC": ([32], f32),
-    "Ib": ([128], b16), "nI": ([128], b16), "I2": ([128], b16), "I14": ([128], b16), "Im": ([128], b16), "BOb": ([128], b16), "BO2": ([128], b16),
-    "Zf": ([2, 144], f32), "Zb": ([2, 144], b16), "A12": ([256], f32), "SEL": ([256], b16), "D12": ([256], b16), "MV2": ([8, 2], f32),
-    "SXY": ([256], b16), "SXa": ([256], b16), "WP": ([256], b16), "CAB": ([128], b16), "PM": ([4, 128], b16),
-    "RX": ([3, 8, 2], b16), "RY": ([8], b16), "CK": ([8, 2, 16], b16), "CKi": ([8, 2, 16], f32), "KR": ([8, 2, 16], b16), "KZ": ([8, 2, 16], b16),
-    "TM": ([2 * TS * 256], h16), "ME": ([8, 2, 16], b16), "OB": ([256], b16), "D0": ([256], f32), "RLi": ([8], i32), "RL": ([8], u16),
-    "JI": ([8], i32), "JC": ([32], b16), "J8": ([48], b16), "IN3": ([32], b16), "MV": ([64], i32), "OH": ([64], b16),
+    "X": ([2 * XN], b16), "NM": ([256], i32), "PR": ([256], i32), "TH": ([16], i32), "CI": ([16], h16), "TB": ([448], h16), "ST": ([640], b16), "NIL": ([128], f32), "C3": ([512], b16), "PK": ([256], b16),
+    "ME": ([8, 2, 14], b16), "MZ": ([8, 2, 14], b16),
+    "ONE": ([128], f32), "If": ([8, 16], f32), "BOa": ([128], f32), "BO": ([8, 16], f32), "LT": ([128], b16), "PERM": ([128], b16),
+    "PI": ([16], i32), "PI2": ([16], i32), "DJ": ([128], i32), "M1": ([128], b16), "COL": ([16], f32), "KC": ([32], f32),
+    "Ib": ([128], b16), "nI": ([128], b16), "I2": ([128], b16), "I14": ([128], b16), "Im": ([128], b16), "Ih": ([128], b16), "I8": ([128], b16),
+    "BO2": ([128], f32), "Zb": ([2, 144], b16), "A12": ([256], f32), "SEL": ([256], b16), "D12": ([256], b16), "MV2": ([8, 2], f32), "MVb": ([8, 2], b16),
+    "PIf": ([112], f32), "LXY": ([224], b16), "WP": ([256], b16), "CAB": ([128], b16), "CF": ([128], b16), "CH": ([128], b16), "N128": ([272], b16),
+    "PMf": ([4, 128], f32), "PMa": ([4, 128], b16), "PMb": ([4, 128], b16),
+    "RX": ([3, 8, 2], b16), "RY": ([16], b16), "CK": ([8, 2, 14], b16), "CKi": ([8, 2, 14], f32), "OB": ([128], b16), "D0": ([224], f32), "RLi": ([8], i32), "RL": ([8], u16),
+    "JI": ([8], i32), "JC": ([24], b16), "RK": ([448], b16), "QQ": ([448], i32), "UU": ([16], f32), "J8": ([32], b16), "IN2": ([16], b16), "MV": ([64], i32), "OH": ([64], b16),
     "MK": ([768], b16), "P16": ([256], b16), "NQ": ([256], h16), "AA": ([512], b16), "W1": ([256], b16), "W2": ([256], f32),
-    "R1": ([4096], b16), "R2": ([4096], f32), "OC": ([256], f32),
-    "NL": ([3072], h16), "NO": ([2048], h16), "LR": ([128], u16), "ZL": ([4608], b16), "ZS": ([3840], b16),
-    "PP": ([512], f32), "QQ": ([512], i32), "HB": ([512], i32), "HF": ([512], h16), "HT": ([2, 2, 128], h16), "DL": ([512], f32), "TT": ([512], f32),
-    "OFF": ([512], u16), "WW": ([8192], b16), "AY": ([4096], b16), "XR": ([4096], b16), "RU": ([4096], b16),
-    "SC": ([512], f32), "FF": ([16], f32), "SE": ([16], i32), "KQ": ([16], i32), "GM": ([256], b16), "LS": ([320], u16), "ES": ([16], b16),
-    "AW": ([256], b16), "SZ": ([256], f32), "HZ": ([256], i32), "K8": ([32], b16), "UU": ([16], f32), "LC": ([32], u16), "SX2": ([512], f32), "HX2": ([512], i32),
-    "AT": ([16], f32), "NC": ([16], b16), "AI": ([16], i32), "YE": ([16], f32), "YP": ([256], f32), "YF": ([256], f32),
+    "R1": ([4096], b16), "R2": ([4096], f32), "OC": ([8, 32], f32), "TR": ([8, 32], h16), "RF": ([256], b16),
+    "NL": ([2560], h16), "NO": ([2048], h16), "KL": ([80], u16), "LR": ([64], u16), "ZL": ([2560], b16), "ZS": ([1280], b16),
+    "PP": ([512], f32), "KK": ([448], b16), "DL": ([512], f32), "TT": ([512], f32),
+    "OFF": ([448], u16), "WW": ([7168], b16), "MX": ([7168], b16),
+    "SC": ([448], f32), "FF": ([16], f32), "SE": ([16], i32), "KQ": ([16], i32), "GM": ([256], b16), "LS": ([16], u16), "JK": ([16], f32), "ES": ([2], f32),
+    "AW": ([256], b16), "A2": ([256], b16), "K8": ([16], b16), "LC": ([36], u16), "SX": ([256], f32), "HX": ([544], b16), "XO": ([544], b16),
+    "Df": ([2, 128], f32), "Db": ([2, 128], b16), "D8": ([2, 128], b16),
+    "NC": ([16], f32), "AI": ([16], b16), "AT": ([16], f32), "YE": ([16], f32), "YP": ([256], f32), "YF": ([256], f32), "ZO": ([256], b16),
 }
 SCRATCH = {k: ("sbuf", [128] + v[0], v[1]) for k, v in SB_.items()}
-SCRATCH.update({"SB": ("psum", [128, 2048], f32), "KP": ("psum", [128, 512], f32),
-                "ST": ("psum", [128, 1024], f32), "TL": ("psum", [128, 32, 16], f32)})
-PSUM = ("SB", "KP", "ST", "TL")
-SEMAPHORES = ["v", "p", "s", "gq", "sent", "out"] + ["tw0", "tw1"] + ["l%d" % k for k in range(24)] + ["a%d%d" % (i, k) for i in range(2 * TS - 2) for k in range(3)]
+PSUM = {"S0": [512], "S1": [512], "S2": [512], "KP": [512], "HP": [32, 16], "SP": [32, 16], "T1": [32, 16], "T2": [32, 16]}
+SCRATCH.update({k: ("psum", [128] + v, f32) for k, v in PSUM.items()})
+SEMAPHORES = ["v", "p", "s", "gq", "sent", "out", "tw0", "tw1"] + ["l%d" % k for k in range(12)] + ["a%d%d" % (i, k) for i in range(2 * TS - 2) for k in range(3)]
+
+
+def arrange(nodes, edges):
+    n = len(nodes)
+    dur = [x["dur"] for x in nodes]
+    pre, suc = [[] for _ in nodes], [[] for _ in nodes]
+    for (p, k), lag in edges.items():
+        pre[k].append((p, lag))
+        suc[p].append((k, lag + dur[k] - dur[p]))
+
+    def sweep(pre_, suc_, prio):
+        left, at, busy = [len(x) for x in pre_], [0.0] * n, {}
+        ready = sorted((prio[k], k) for k in range(n) if not left[k])
+        while ready:
+            k = ready.pop(0)[1]
+            t = max([0.0] + [at[p] + lag for p, lag in pre_[k]])
+            row = busy.setdefault(nodes[k]["q"], [])
+            j = len(row)
+            while j and row[j - 1][1] > t:
+                j -= 1
+            while j < len(row) and row[j][0] < t + dur[k]:
+                t = max(t, row[j][1])
+                j += 1
+            row.insert(j, (t, t + dur[k]))
+            at[k] = t
+            for m, _ in suc_[k]:
+                left[m] -= 1
+                if not left[m]:
+                    ready.append((prio[m], m))
+                    ready.sort()
+        return at, max(at[k] + dur[k] + nodes[k]["lat"] for k in range(n))
+
+    def deal(due, hold):
+        at, todo, late = [None] * n, {}, 0.0
+        for k in sorted(range(n), key=lambda k: due[k]):
+            todo.setdefault(nodes[k]["q"], []).append(k)
+        free, look = {q: 0.0 for q in todo}, {q: 0.0 for q in todo}
+        while look:
+            q = min(look, key=lambda q: look[q])
+            t, memo = look[q], {}
+
+            def soon(k):
+                if k not in memo:
+                    memo[k] = max([0.0] + [(at[p] if at[p] is not None else max(soon(p), free[nodes[p]["q"]], t)) + lag for p, lag in pre[k]])
+                return memo[k]
+            some, limit, pick = todo[q][:WIDE], 1e12, None
+            for k in some:
+                if soon(k) <= t + 1 and all(at[p] is not None for p, _ in pre[k]):
+                    if t + dur[k] <= limit:
+                        pick = k
+                        break
+                else:
+                    limit = min(limit, max(soon(k) + hold, due[k] + late))
+            if pick is None:
+                look[q] = max(t + 20, min(soon(k) for k in some))
+                continue
+            at[pick], free[q] = t, t + dur[pick]
+            look[q] = free[q]
+            if nodes[pick]["tag"] == ("choose", 0):
+                late = t - due[pick]
+            todo[q].remove(pick)
+            if not todo[q]:
+                del look[q]
+        return at, max(at[k] + dur[k] + nodes[k]["lat"] for k in range(n))
+
+    tail = [0.0] * n
+    for k in range(n - 1, -1, -1):
+        tail[k] = max([dur[k] + nodes[k]["lat"]] + [tail[m] + lag - dur[m] + dur[k] for m, lag in suc[k]])
+    best = None
+    for skew in SKEWS:
+        prio = [-tail[k] + skew * nodes[k]["h"] for k in range(n)]
+        for r in range(ROUNDS):
+            at, end = sweep(pre, suc, prio)
+            if best is None or end < best[0]:
+                best = (end, at)
+            back, _ = sweep(suc, pre, [-(at[k] + dur[k] + nodes[k]["lat"]) for k in range(n)])
+            prio = [-(back[k] + dur[k]) for k in range(n)]
+    seed = [1]
+
+    def rnd():
+        seed[0] = (seed[0] * 1103515245 + 12345) % 2147483648
+        return seed[0] / 2147483648
+
+    twins = {}
+    for k, x in enumerate(nodes):
+        twins.setdefault(x["tag"], []).append(k)
+    for period, skew in PERIODS:
+        due, after = [0.0] * n, {}
+        for k in range(n - 1, -1, -1):
+            x = nodes[k]
+            due[k] = min([START + 4 * period + skew + LAST - x["lat"] - dur[k]] + [due[m] - (lag - dur[m] + dur[k]) for m, lag in suc[k]])
+            if x["tag"] == ("choose", 0):
+                due[k] = min(due[k], START + x["i"] // 2 * period + x["h"] * skew)
+            if x["tag"][0] == "look" and x["q"] != "p":
+                due[k] = min(due[k], after.get((x["i"], x["q"]), 1e9) - STRETCH * dur[k])
+                after[(x["i"], x["q"])] = due[k]
+        for hold in HOLDS:
+            at, end = deal(due, hold)
+            for r in range(AGAIN + 1):
+                if best is None or end < best[0]:
+                    best = (end, at)
+                if r < AGAIN:
+                    back, _ = sweep(suc, pre, [-(at[k] + dur[k] + nodes[k]["lat"]) for k in range(n)])
+                    at, end = sweep(pre, suc, [-(back[k] + dur[k]) for k in range(n)])
+    line = sorted(range(n), key=lambda k: (best[1][k], k))
+    if HALF:
+        scan = {nodes[k]["i"]: best[1][k] for k in twins[("choose", 0)]}
+        when = list(best[1])
+        for k, x in enumerate(nodes):
+            if x["i"] >= 0:
+                t0 = scan[0] + x["i"] * HALF
+                if x["key"] in PLAN and x["q"] != "sy" and "'" not in x["tag"][0]:
+                    when[k] = t0 + 1000 * PLAN[x["key"]] - HALF * (x["tag"][0] in ("look", "ahead"))
+                elif x["q"] in "vs":
+                    when[k] += t0 - scan[x["i"]]
+                else:
+                    when[k] = max([t0 - HALF] + [when[p] + lag for p, lag in pre[k]])
+        left, line = [len(x) for x in pre], []
+        ready = [k for k in range(n) if not left[k]]
+        while ready:
+            k = min(ready, key=lambda k: when[k])
+            ready.remove(k)
+            line.append(k)
+            for m, _ in suc[k]:
+                left[m] -= 1
+                if not left[m]:
+                    ready.append(m)
+        pre2, suc2, tail_ = [list(x) for x in pre], [list(x) for x in suc], {}
+        for k in line:
+            q = nodes[k]["q"]
+            if (q in "vs" or "KP0" in PLAN) and q in tail_:
+                pre2[k].append((tail_[q], dur[tail_[q]]))
+                suc2[tail_[q]].append((k, 0.0))
+            tail_[q] = k
+        at = sweep(pre2, suc2, [when[k] + LATE * (x["key"][:2] == "KP") for k, x in enumerate(nodes)])[0]
+        line = sorted(range(n), key=lambda k: (at[k], k))
+    before, last, rest = [None] * n, {}, [dur[k] + nodes[k]["lat"] for k in range(n)]
+    for k in line:
+        before[k], last[nodes[k]["q"]] = last.get(nodes[k]["q"]), k
+    direct = [{p for p, _ in x} for x in pre]
+
+    def times(line, before, at, why, lo):
+        for k in line[lo:]:
+            t, w, b = 0.0, None, before[k]
+            for p, lag in pre[k]:
+                if at[p] + lag > t:
+                    t, w = at[p] + lag, p
+            if b is not None and at[b] + dur[b] >= t:
+                t, w = at[b] + dur[b], b
+            at[k], why[k] = t, w
+        return max(range(n), key=lambda k: at[k] + rest[k])
+
+    at, why = [0.0] * n, [None] * n
+    k = times(line, before, at, why, 0)
+    marks = twins[("choose", 0)]
+    cost = lambda at, k: at[k] + rest[k] + MARK * sum(at[x] for x in marks)
+    now = cost(at, k)
+    best = (at[k] + rest[k], [at[x] + 1e-4 * j for j, x in sorted(enumerate(line), key=lambda y: y[1])])
+    for r in range(SWAPS):
+        pairs = []
+        if rnd() < 0.7:
+            k = marks[int(rnd() * len(marks))]
+        while why[k] is not None:
+            if why[k] == before[k] and why[k] not in direct[k]:
+                pairs.append((why[k], k))
+            k = why[k]
+        u, v = pairs[int(rnd() * min(len(pairs), NEAR))]
+        line2, before2, at2, why2, first = line, list(before), list(at), list(why), n
+        up, far = rnd() < 0.5, 1 + int(6 * rnd() ** 2)
+        mover = v if up else u
+        some = [mover] if rnd() < 0.3 else [x for x in twins[nodes[mover]["tag"]] if rnd() < 0.5 or nodes[x]["h"] == nodes[mover]["h"]]
+        for x0 in [x for x in some for _ in range(far)]:
+            if up:
+                u, v = before2[x0], x0
+            else:
+                u, v = x0, before2.index(x0) if x0 in before2 else None
+            if u is None or v is None:
+                continue
+            lo, hi = line2.index(u), line2.index(v)
+            down, stay, move = {u}, [], []
+            for x in line2[lo + 1:hi]:
+                if before2[x] in down or direct[x] & down:
+                    down.add(x)
+                    move.append(x)
+                else:
+                    stay.append(x)
+            if not direct[v] & down:
+                for x in line2[hi + 1:]:
+                    if before2[x] == v:
+                        before2[x] = u
+                        break
+                line2, first = line2[:lo] + stay + [v, u] + move + line2[hi + 1:], min(first, lo)
+                before2[v], before2[u] = before2[u], v
+        if first < n:
+            k2 = times(line2, before2, at2, why2, first)
+            end, new = at2[k2] + rest[k2], cost(at2, k2)
+            if new < now - HEAT * (1 - r / SWAPS) * math.log(1e-9 + rnd()):
+                line, before, at, why, now = line2, before2, at2, why2, new
+                if end < best[0]:
+                    best = (end, [at[x] + 1e-4 * j for j, x in sorted(enumerate(line), key=lambda y: y[1])])
+        k = max(range(n), key=lambda k: at[k] + rest[k])
+    return best
 
 
 def rank_program(g, core, T, topo):
@@ -46,715 +260,524 @@ def rank_program(g, core, T, topo):
         return
     sem = T.sem
     Q = {"v": g.vector, "p": g.tensor, "s": g.scalar, "gq": g, "sy": g.sync}
-    ver, cnt, know, hist, free, dry, key = {}, {}, {q: {} for q in Q}, {}, {q: 0.0 for q in Q}, [True], [None]
+    nodes, edges, hist, stream, part, seen_ = [], {}, {}, [0], ["", -1, 0], {}
 
-    def needs(q, rd, wr):
-        out = []
+    def add(q, fns, rd, wr, dur, lat=0.0, s=None, inc=1, free=False, moving=0.0):
+        k, me = len(nodes), (q if inc == 1 else s)
+        nodes.append({"q": q, "fns": fns, "dur": dur, "lat": lat, "s": s or q, "inc": inc, "h": stream[0], "wait": set(), "i": part[1], "tag": (part[0], part[2] if inc > 0 else s[-1])})
+        part[2] += inc > 0
+        name = (q, part[1], (wr or rd)[0][0])
+        seen_[name] = seen_.get(name, -1) + 1
+        nodes[k]["key"] = name[2] + str(seen_[name])
+
+        def edge(p, wait):
+            e = nodes[p]
+            edges[(p, k)] = max(edges.get((p, k), 0.0), e["dur"] + (e["lat"] + WAKE if wait else 0.0))
+            if wait:
+                nodes[k]["wait"].add(p)
+        for b in {r[0] for r in rd + wr if r[0] in PSUM}:
+            old = hist.get(b, [])
+            for e in old:
+                if not (free and e[2]):
+                    edge(e[0], e[1] != q)
+            hist[b] = (old if free else []) + [(k, q, free)]
         for regs, w in ((rd, False), (wr, True)):
             for (b, lo, hi) in regs:
+                if b in PSUM:
+                    continue
                 for e in hist.get(b, ()):
-                    if e[1] < hi and lo < e[2] and (w or e[3]) and not (e[0] == q and (q == "p" or not e[3])):
-                        out.append(e)
-        return out
-
-    def start(d):
-        return max([free[d[0]]] + [e[7] + WAKE for e in needs(d[0], d[2], d[3])])
-
-    def acc(q, rd, wr):
-        for e in sorted(needs(q, rd, wr), key=lambda e: -e[5]):
-            if know[q].get(e[4], 0) < e[5]:
-                if not dry[0]:
-                    Q[q].wait_ge(sem[e[4]], e[5])
-                for s, n in list(e[6].items()) + [(e[4], e[5])]:
-                    know[q][s] = max(know[q].get(s, 0), n)
-
-    def note(q, rd, wr, s, n, snap, fin):
-        for regs, w in ((rd, False), (wr, True)):
-            for (b, lo, hi) in regs:
-                old = [e for e in hist.get(b, []) if not (lo <= e[1] and e[2] <= hi and (w or (e[0] == q and not e[3])))]
-                ver[b] = ver.get(b, 0) + 1000
-                hist[b] = old + [(q, lo, hi, w, s, n, snap, fin, key[0])]
-
-    def do(d):
-        q, fn, rd, wr, s, inc, dur, lat, post = d
-        t0 = start(d)
-        acc(q, rd, wr)
-        free[q] = t0 + dur
-        call = None if dry[0] else fn(Q[q])
-        if s is not None:
-            cnt[s] = cnt.get(s, 0) + inc
-            if call:
-                call.then_inc(sem[s], inc)
-            note(q if inc == 1 else s, rd, wr, s, cnt[s], dict(know[q]), t0 + dur + lat)
-        if post:
-            post(t0 + dur)
-
-    def ps(b, lo, hi):
-        return (b, lo // 512, (hi + 511) // 512) if b in PSUM else (b, lo, hi)
+                    if e[0] < k and e[2] < hi and lo < e[3] and (w or e[4]):
+                        edge(e[0], (e[4] or e[1] != me) and b != "GQ")
+                hist[b] = [e for e in hist.get(b, ()) if not (w and lo <= e[2] and e[3] <= hi)] + [(k + (moving > 0), me, lo, hi, w)]
+        if moving:
+            nodes.append(dict(nodes[k], q="e", dur=moving, lat=0.3 * lat, wait=set(), tag=nodes[k]["tag"] + ("e",), key="-"))
+            nodes[k]["lat"], edges[(k, k + 1)] = 0.0, dur + 0.7 * lat
 
     def c(b, lo=0, hi=None, st=1):
         hi = T[b].shape[1] if hi is None else hi
-        return (T[b][:, lo:hi:st], ps(b, lo, hi))
+        return (T[b][:, lo:hi:st], (b, lo, hi))
 
-    def a(b, ap=None):
-        return (T[b][:] if ap is None else ap, ps(b, 0, 512 if b in PSUM else 1 << 20))
+    def a(b, ap=None, lo=0, hi=1 << 20):
+        return (T[b][:] if ap is None else ap, (b, lo, hi))
 
     def ind(w, o):
         return (w[0].indirect(o[0]), w[1], o[1])
 
     def size(x):
-        n = 1
-        for k in list(x[0].shape)[1:]:
-            n *= int(k)
-        return n
+        return math.prod(int(k) for k in list(x[0].shape)[1:])
 
-    def op(q, fn, out, *ins, dur=300.0):
-        rs = [r for x in ins for r in x[1:]]
-        return (q, fn, [r for r in rs if r[0] not in PSUM], [out[1]] + [r for r in rs if r[0] in PSUM] + list(out[2:]), q, 1, dur, 0.0, None)
+    def op(q, fn, out, *ins, dur):
+        add(q, [fn], [r for x in ins for r in x[1:]] + list(out[2:]), [out[1]], dur)
 
     def narrow(*xs):
         return all(SCRATCH[x[1][0]][2] in (b16, h16, u16) for x in xs)
 
-    def span(out, i, f):
+    def span(out, i, f, fix=FV):
         if len(out) > 2:
-            return FIX + 3.8 * CY * size(i)
+            return fix + SCA * CY * size(i)
         if len(i) > 2:
-            return FIX + 1.56 * CY * size(out)
-        return FIX + CY * max(64, f * size(out))
+            return fix + max(f, GA) * CY * size(out)
+        return fix + CY * max(64, f * size(out))
 
     def tt(out, x, y, o):
-        d = span(out, x, 1 if x[1][0] in PSUM or y[1][0] in PSUM else 2)
-        d = GM * (d - FIX) + FIX if len(x) > 2 else d
-        return op("v", lambda e: e.tensor_tensor(out[0], x[0], y[0], o), out, x, y, dur=d)
+        op("v", lambda e: e.tensor_tensor(out[0], x[0], y[0], o), out, x, y, dur=span(out, x, 1 if x[1][0] in PSUM or y[1][0] in PSUM else 2))
 
     def ts(out, x, s1, s2, o0, o1=None):
         y = [s for s in (s1, s2) if isinstance(s, tuple)]
         f1, f2 = [s[0] if isinstance(s, tuple) else s for s in (s1, s2)]
-        d = span(out, x, 0.5 if narrow(out, x) else 1)
-        if o1 is None:
-            return op("v", lambda e: e.tensor_scalar(out[0], x[0], f1, None, o0), out, x, *y, dur=d)
-        return op("v", lambda e: e.tensor_scalar(out[0], x[0], f1, f2, o0, o1), out, x, *y, dur=d)
+        more = () if o1 is None else (o1,)
+        op("v", lambda e: e.tensor_scalar(out[0], x[0], f1, f2, o0, *more), out, x, *y, dur=span(out, x, 0.5 if narrow(out, x) else 1))
 
     def cp(out, x):
-        return op("v", lambda e: e.tensor_copy(out[0], x[0]), out, x, dur=span(out, x, 0.5 if narrow(out, x) else 1))
+        op("v", lambda e: e.tensor_copy(out[0], x[0]), out, x, dur=span(out, x, 0.5 if narrow(out, x) else 1))
 
     def ms(out, k):
-        return op("v", lambda e: e.memset(out[0], k), out, dur=span(out, out, 0.5 if narrow(out) else 1))
+        op("v", lambda e: e.memset(out[0], k), out, dur=span(out, out, 0.5 if narrow(out) else 1))
+
+    def turn(out, x):
+        op("v", lambda e: e.transpose(out[0], x[0]), out, x, dur=span(out, x, 0.5 if narrow(out, x) else 1))
 
     def act(out, x, f, bias=0.0, scale=1.0):
         y = [s for s in (bias, scale) if isinstance(s, tuple)]
         bb, sc = [s[0] if isinstance(s, tuple) else s for s in (bias, scale)]
-        return op("s", lambda e: e.activation(out[0], x[0], f, bias=bb, scale=sc), out, x, *y, dur=FIX + CY * (1.56 if len(x) > 2 else 1) * size(out))
+        op("s", lambda e: e.activation(out[0], x[0], f, bias=bb, scale=sc), out, x, *y, dur=span(out, x, 1, FS))
 
-    def mm(out, l, r, first, last):
-        d = max(min(64, size(l)), size(r)) * PE * (4 if SCRATCH[l[1][0]][2] == f32 else 1)
+    def lin(q, out, x, scale, bias):
+        if q == "v":
+            ts(out, x, scale, bias, A.mult, A.add)
+        else:
+            act(out, x, F.Copy, bias=bias, scale=scale)
 
-        def fn(e):
-            if isinstance(last, list):
-                last[0] -= 1
-                return e.matmul(out[0], l[0], r[0], first, last[0] == 0)
-            return e.matmul(out[0], l[0], r[0], first, last)
-        return op("p", fn, out, l, r, dur=d)
+    def mms(terms, free=False):
+        def call(out, l, r, first, last):
+            def fn(e):
+                if isinstance(last, list):
+                    last[0] -= 1
+                    return e.matmul(out[0], l[0], r[0], first, last[0] == 0)
+                return e.matmul(out[0], l[0], r[0], first, last)
+            return fn
+        d = sum(max(min(64, size(l)), size(r)) * PE * (4 if SCRATCH[l[1][0]][2] == f32 else 1) for _, l, r, _, _ in terms)
+        add("p", [call(*x) for x in terms], [y[1] for x in terms for y in x[1:3]], [x[0][1] for x in terms], d, free=free)
 
-    def group(out, *terms):
-        return [mm(out, l, r, n == 0, n == len(terms) - 1) for n, (l, r) in enumerate(terms)]
+    def group(out, *terms, more=False, done=True):
+        return [(out, l, r, n == 0 and not more, done and n == len(terms) - 1) for n, (l, r) in enumerate(terms)]
 
-    def dma(q, out, in_, s, rd, wr):
-        return (q, lambda e: e.dma_start(out, in_), rd, wr, s, 16, 60.0, 2200.0, None)
-
-    def out_(dst, src, reg, q="sy"):
-        return dma(q, dst, src, "out", [reg], [])
+    def dmas(q, pairs, rd, wr, s, n):
+        add(q, [lambda e, o=o, x=x: e.dma_start(o, x) for o, x in pairs], rd, wr, 60.0 * len(pairs), LOAD, s, 16, moving=sum(int(o.shape[0]) for o, _ in pairs) * (ROW + n / RATE) / 16)
 
     def gi(out, pat, base, cm):
-        d = 130 + 2 * CY * size(out)
-        out = out + (("GQ", 0, 1),)
-        if SCRATCH[out[1][0]][2] != i32:
-            return op("gq", lambda e: e.iota(out[0], pat, base, cm, allow_small_or_imprecise_dtypes=True), out, dur=d)
-        return op("gq", lambda e: e.iota(out[0], pat, base, cm), out, dur=d)
+        k = {} if SCRATCH[out[1][0]][2] == i32 else {"allow_small_or_imprecise_dtypes": True}
+        add("gq", [lambda e: e.iota(out[0], pat, base, cm, **k)], [], [out[1], ("GQ", 0, 1)], 130 + 2 * CY * size(out))
 
     def gs(out, x, pat, cmp_, base, cm, fill=0.0):
-        return op("gq", lambda e: e.affine_select(out[0], x[0], pat, cmp_, fill, base, cm), out + (("GQ", 0, 1),), x, dur=170 + 2 * CY * size(out))
+        add("gq", [lambda e: e.affine_select(out[0], x[0], pat, cmp_, fill, base, cm)], [x[1]], [out[1], ("GQ", 0, 1)], 170 + 2 * CY * size(out))
 
-    sent = [0]
     nxt, prv = T.cores[(rank + 1) % N], T.cores[(rank - 1) % N]
-    ein = len(topo.engines(prv, core)[:8])
+    ein, eout = len(topo.engines(prv, core)[:ALL]), topo.engines(core, nxt)[:ALL]
+    sent = [0]
 
     def send(i, k):
         rid, pid = topo.addr(nxt, core)
-        en, s = topo.engines(core, nxt)[:8], "a%d%d" % (i, k)
-        sent[0] += len(en)
-        mask = lambda es: sum(1 << x for x in es)
-        src, dst = ((half("NL", i, 256), half("NO", i, 256)), (zed("S", i), zed("L", i + 2)), (c("LS", 32 * i + 8, 32 * i + 24), half("LR", i, 16)))[k]
-        dst = [dst, half("ZL", 3 * i + 8)] if k == 1 else [dst]
-        tr = [RemoteDMATransfer(dst_ids=[DstId(rid=rid, pnc=pid)] * len(dst), dma_engine_mask=mask(en), remote_sem=sem[s], srcs=[src[0]], dsts=[x[0] for x in dst])]
-        return ("gq", lambda e: e.remote_dma_fused(tr, local_sem=sem.sent), [src[1]], [], None, 0, 1000.0, 0.0,
-                lambda t: note("rem", [], [x[1] for x in dst], s, ein * len(dst), {}, t + SHIP[k]))
+        s = "a%d%d" % (i, k)
+        sent[0] += len(eout)
+        src, dst = ((half("NL", i, 256), [half("NO", i, 256)]), (half("ZS", i), [half("ZL", i + 2)]), (half("KL", i, 8), [half("LR", i, 8)]))[k]
+        tr = [RemoteDMATransfer(dst_ids=[DstId(rid=rid, pnc=pid)] * len(dst), dma_engine_mask=sum(1 << x for x in eout), remote_sem=sem[s], srcs=[src[0]], dsts=[x[0] for x in dst])]
+        add("gq", [lambda e: e.remote_dma_fused(tr, local_sem=sem.sent)], [src[1]], [x[1] for x in dst], CALL, SHIP, s, -ein * len(dst), moving=16 * (ROW + (512, 256, 16)[k] / 10))
 
     half = lambda b, h, n=128: c(b, h * n, h * n + n)
     col = lambda j: c("COL", j, j + 1)
     names = lambda b, i: half("N" + b, 2 * i)
     rows = lambda b, i: half("N" + b, 2 * i + 1)
-    zed = lambda b, i: half("Z" + b, 3 * i + 1)
-    Ib, nI, IND, u0 = c("Ib"), c("nI"), a("BO", T.BO[:, :, 0]), c("PI2", 0, 1)
+    Ib, nI, IND, u0, ONE = c("Ib"), c("nI"), a("BO", T.BO[:, :, 0]), c("PI2", 0, 1), c("ONE")
     CS = lambda b, s: a(b, T[b][:, 0, 15 - s:143 - s])
     DS = lambda b, s: a(b, T[b][:, 1, 15 - s:143 - s])
-    SEL14 = c("SEL", 0, 128)
     P64 = lambda k: slice(64 * k, 64 * k + 64)
     C128 = lambda k: slice(128 * k, 128 * k + 128)
+    four = lambda b, h, lo=0, hi=32: a(b, T[b][:, 4 * h:4 * h + 4, lo:hi], h, h + 1)
+    ps = lambda b, r, n=8: a(b, T[b][:, r:r + n, :]) if len(PSUM[b]) > 1 else c(b, 16 * r, 16 * (r + n))
+    XW = lambda h: c("X", XN * h, XN * h + XN)
+    xs = lambda h, k, lo, n: T.X[P64(k), XN * h + lo:XN * h + lo + n]
 
-    loads = []
-    for h in range(2):
-        loads += [("sy" if k else "s", T[b][P64(k), C128(h)], src[P64(h), C128(k)], half(b, h)[1]) for b, src in (("PR", T.pr), ("NM", T.nm)) for k in range(2)]
-    for h in range(2):
-        loads += [("sy", T.TH[P64(k), 8 * h:8 * h + 5], T.th[P64(h), :], half("TH", h, 8)[1]) for k in range(2)]
-        loads += [("sy", T.X[P64(k), XN * h:XN * h + 2048], T.xt[P64(h), :], ("X", XN * h, XN * h + 2048)) for k in range(2)]
-        loads += [("sy", T.ZL[P64(k), C128(3 * h + q)], T.z0[P64(h), C128(k)], half("ZL", 3 * h + q)[1]) for k in range(2) for q in (1, 2)]
-
-    def begin():
-        key[0] = None
-        for n, (q, o, src, reg) in enumerate(loads):
-            cnt["l%d" % n] = 16
-            if not dry[0]:
-                Q[q].dma_start(o, src).then_inc(sem["l%d" % n], 16)
-            free[q] += 60.0
-            hist.setdefault(reg[0], []).append(("l%d" % n, reg[1], reg[2], True, "l%d" % n, 16, {}, free[q] + (4500.0 if reg[0] == "X" else 2500.0), None))
-        for d in early:
-            do(d)
-
-    early = ( ms(c("ONE"), 1.0), gi(c("PI"), [[0, 16]], 0, 1),
-              gs(c("BOa"), c("ONE"), [[-16, 8], [0, 16]], A.is_ge, 0, 1), gs(a("BO"), c("BOa"), [[16, 8], [0, 16]], A.is_ge, 15, -1),
-              gs(c("LT"), a("BO"), [[1, 128]], A.is_gt, 0, -1), gs(a("If"), c("ONE"), [[-1, 128]], A.is_equal, 0, 1),
-              gi(c("KC", 0, 16), [[-1, 16]], 0, 0), gi(c("KC", 16, 32), [[-16, 16]], 0, 0),
-              ts(c("PI2"), c("PI"), 15, None, A.bitwise_and),
-              ts(col(0), u0, 1, 0, A.mult, A.add), ts(col(1), u0, 16, -240, A.mult, A.add),
-              ts(col(2), u0, 16 - 2.0 ** -16, -240 + 0.5 + 15 * 2.0 ** -16, A.mult, A.add),
-              ms(a("Zf"), 0.0), cp(a("Zf", T.Zf[:, 0, 15:143:16]), IND), cp(a("Zf", T.Zf[:, 1, 15:143:16]), IND),
-              ts(a("Zf", T.Zf[:, 1, 14:142:16]), IND, -1, None, A.mult), cp(a("Zb"), a("Zf")),
-              act(Ib, a("If"), F.Copy), act(c("I2"), a("If"), F.Copy, scale=2.0), act(c("I14"), a("If"), F.Copy, scale=14.0),
-              act(c("Im"), a("If"), F.Copy, scale=2.0 ** -12))
-
-    def consts_g():
-        yield gi(a("CAB", T.CAB[0:64, :]), [[0, 8], [64, 16]], -992, 0)
-        yield ("done", "cab0")
-        yield gs(c("PERM"), c("ONE"), [[-2, 64], [1, 2]], A.is_equal, -1, 1)
-        yield ("done", "perm")
-        for i in range(4):
-            yield gs(a("PM", T.PM[:, i]), c("ONE"), [[-32, 4], [1000, 2], [-1, 16]], A.is_equal, -16 * (i // 2) - 1000 * (i % 2), 1)
-        yield ("need", "sel")
-        for o, s, k in (("SXY", "SXa", (3232.0, 2400.0)), ("D12", "SEL", (-1.0, -1.0))):
-            for q in range(2):
-                yield gs(half(o, q), half(s, q), [[-1, 128]], A.not_equal, 0, 1, k[q])
-            yield ("done", o)
-        fill = lambda x, k: gi(x, [[0, size(x)]], k, 0)
-        yield gi(a("CKi"), [[0, 8], [-240, 2], [1, 16]], 241, 0)
-        for q, (k, pad) in enumerate(((0, -2 ** 23), (8128, -16))):
-            yield fill(a("CK", T.CK[64:128, :, q, 0:14]), k)
-            yield fill(a("CK", T.CK[64:128, :, q, 14:16]), pad)
-        yield ("done", "ck")
-        yield gi(c("RLi"), [[1, 8]], 0, 0)
-        yield gi(c("JI"), [[16, 8]], 0, 0)
-        yield gi(c("DJ"), [[0, 8], [1, 16]], 0, 0)
-        yield gi(c("JC", 8, 32), [[32, 3], [0, 8]], 0, 0)
-        yield fill(c("MV"), 15)
-        yield gi(c("MV", 1, 15), [[2, 7], [-1, 2]], 1, 0)
-        yield gi(c("MV", 17, 31), [[1, 14]], 0, 0)
-        yield gi(c("MV", 49, 63), [[2, 7], [-1, 2]], 1, 0)
-        yield fill(c("D0"), 1)
-        yield fill(c("D0", 0, 256, 32), 0)
-        for k in range(2):
-            yield fill((T.COL[P64(k), 8:9], col(8)[1]), 1024 * k)
-        yield gi(c("J8", 8, 24), [[28672, 2], [0, 8]], -14336, 0)
-        yield ("done", "iotas")
+    def loads():
         for h in range(2):
-            for lo, hi in ((0, 128), (1920, 2176), (3968, 4096)):
-                yield fill(c("WW", 4096 * h + lo, 4096 * h + hi), 0)
-            yield ("done", ("ww", h))
+            for n, (b, src) in enumerate((("PR", T.pr), ("NM", T.nm))):
+                dmas("sy" if h else "s", [(T[b][P64(k), C128(h)], src[P64(h), C128(k)]) for k in range(2)], [], [half(b, h)[1]], "l%d" % (2 * h + n), 512)
+        dmas("sy", [(T.TH[P64(k), 8 * h:8 * h + 5], T.th[P64(h), :]) for k in range(2) for h in range(2)], [], [c("TH")[1]], "l4", 20)
+        dmas("sy", [(T.ZL[P64(k), C128(h)], T.z0[P64(h), C128(k)]) for k in range(2) for h in range(2)], [], [c("ZL", 0, 256)[1]], "l5", 256)
+        for h in range(2):
+            dmas("sy", [(xs(h, k, lo, n), T.xt[P64(h), src:src + n]) for k in range(2) for lo, src, n in ((0, 1024, 1024), (1024, 0, 1024), (2048, 1024, 128))],
+                 [], [XW(h)[1]], "l%d" % (6 + h), 1450)
+        for k in range(4, len(nodes) - 2):
+            edges[(k, k + 2)] = nodes[k]["dur"]
 
     def consts():
-        yield ms(c("OB", 0, 128), 1.0)
+        fill = lambda x, k: gi(x, [[0, size(x)]], k, 0)
+        If = a("If")
+        ms(ONE, 1.0)
+        gi(c("PI"), [[0, 16]], 0, 1)
+        gs(c("BOa"), ONE, [[-16, 8], [0, 16]], A.is_ge, 0, 1)
+        gs(a("BO"), c("BOa"), [[16, 8], [0, 16]], A.is_ge, 15, -1)
+        gs(c("LT"), a("BO"), [[1, 128]], A.is_gt, 0, -1)
+        gs(If, ONE, [[-1, 128]], A.is_equal, 0, 1)
+        gi(c("KC", 16, 32), [[-16, 16]], 0, 0)
+        gi(c("KC", 0, 16), [[-1, 16]], 0, 0)
+        gi(a("CAB", T.CAB[0:64, :]), [[0, 8], [64, 16]], -992, 0)
+        for i in range(4):
+            gs(a("PMf", T.PMf[:, i], i, i + 1), ONE, [[-32, 4], [1000, 2], [-1, 16]], A.is_equal, -16 * (i // 2) - 1000 * (i % 2), 1)
+        gs(c("PERM"), ONE, [[-2, 64], [1, 2]], A.is_equal, -1, 1)
+        one = c("ONE", 0, 112)
+        gs(c("PIf"), one, [[-1, 14], [-16, 8]], A.is_equal, 0, 1)
+        ms(c("NIL"), 0.0)
+        for q, (pat, base, k, l) in enumerate((([[-2, 7], [1, 2], [-16, 8]], -1, 2400.0, 3232.0), ([[0, 14], [-16, 8]], -14, 3232.0, 2400.0))):
+            gs(half("LXY", q, 112), c("NIL", 0, 112), pat, A.not_equal, base, 1, k)
+            gs(half("LXY", q, 112), half("LXY", q, 112), [[-1, 14], [-16, 8]], A.not_equal, 0, 1, l)
+        ts(c("PI2"), c("PI"), 15, None, A.bitwise_and)
+        ts(col(1), u0, 16, None, A.mult)
+        ts(col(0), u0, 1, None, A.mult)
+        ts(col(2), u0, 16 - 2.0 ** -16, -240 + 0.5 + 15 * 2.0 ** -16, A.mult, A.add)
+        ms(a("Zb"), 0.0)
+        for j, o, k in ((0, 15, 1), (1, 15, 1), (1, 14, -1)):
+            ts(a("Zb", T.Zb[:, j, o:o + 128:16]), IND, k, None, A.mult)
+        for b, k in (("Ib", 1.0), ("I2", 2.0), ("I14", 14.0), ("Im", 2.0 ** -12), ("nI", -1.0), ("Ih", 0.5), ("I8", -8.0)):
+            act(c(b), If, F.Copy, scale=k)
+        ms(c("OB"), 1.0)
+        for b in ("MV2", "MVb"):
+            for q in range(2):
+                act(a(b, T[b][:, :, q], q, q + 1), IND, F.Copy, scale=4096.0 * (2 * q - 1))
+        ms(a("CAB", T.CAB[64:128, :]), -15 / 2048)
         for q in range(2):
-            yield act(a("MV2", T.MV2[:, :, q]), IND, F.Copy, scale=4096.0 * (2 * q - 1))
-        yield ("need", "cab0")
-        yield ms(a("CAB", T.CAB[64:128, :]), -15 / 2048)
-        yield ("done", "cab")
+            ts(col(3 + q), u0, 14 + q, None, A.is_equal)
+            act(half("SEL", q), a("BO"), F.Copy, scale=col(3 + q))
+        ms(c("NC", 0, 2), KAP)
+        ts(c("ZL", 0, 256), c("ZL", 0, 256), 192, None, A.add)
+        for j, k in enumerate((-1.0, 2.0, 1.0)[:2 + (NB > 0)]):
+            for q, w in enumerate((512 * BIG, -512.0)):
+                act(a("RX", T.RX[:, j, :, q], j, j + 1), IND, F.Copy, scale=k * w)
+        for q, w in enumerate((512 * BIG, -1024 * BIG)):
+            act(half("RY", q, 8), IND, F.Copy, scale=w)
+        ms(c("C3"), -3.0)
+        ms(c("D0"), 1.0)
+        gs(a("ME"), c("D0"), [[-16, 8], [-1000, 2], [0, 14]], A.is_ge, 0, 1)
+        gs(a("ME"), a("ME"), [[16, 8], [0, 28]], A.is_ge, 15, -1)
+        for t in range(TS):
+            gs((T.ST[0:5, C128(t)], half("ST", t)[1]), (T.NIL[0:5, 0:128], c("NIL")[1]), [[0, 128]], A.not_equal, -t, 1, -32 * BIG)
+        if NB:
+            ms(a("MZ"), 0.0)
+            for q, w in enumerate((512 * BIG, -512.0)):
+                ts(a("MZ", T.MZ[:, :, q, 0:NB]), a("BO", T.BO[:, :, 0:NB]), w, None, A.mult)
+        for b, w in (("PMa", 512 * BIG), ("PMb", 512.0)):
+            act(a(b), a("PMf"), F.Copy, scale=w)
+        gi(a("CKi"), [[0, 8], [-210, 2], [1, 14]], 241, 0)
+        for q, (w, k, l) in enumerate(((BIG, -16 * 6144 * BIG, 0.0), (1.0, 16 * 5088.0, 16.0))):
+            act(a("CK", T.CK[0:64, :, q, :], q, q + 1), a("CKi", T.CKi[0:64, :, q, :]), F.Copy, scale=w / 64)
+            ms(a("CK", T.CK[64:96, :, q, :], 2 + q, 3 + q), k)
+            ms(a("CK", T.CK[96:128, :, q, :], 4 + q, 5 + q), l)
+        gs(c("D0"), c("D0"), [[0, 8], [1, 28]], A.is_gt, 0, 0)
         for q in range(2):
-            yield ts(col(3 + q), u0, 14 + q, None, A.is_equal)
-            yield act(half("SEL", q), a("BO"), F.Copy, scale=col(3 + q))
-        yield ("need", "perm")
-        yield act(half("SXa", 0), c("PERM"), F.Copy, scale=2400.0)
-        yield act(half("SXa", 1), SEL14, F.Copy, scale=3232.0)
-        yield ("done", "sel")
-        yield ms(c("NC"), 0.0)
-        yield act(nI, a("If"), F.Copy, scale=-1.0)
-        yield ms(col(15), 128.0)
-        yield ("done", "pm")
-        for h in range(2):
-            yield cp(c("X", XN * h + 2048, XN * h + XN), c("X", XN * h, XN * h + 64))
-            yield ("done", ("table", h - 2))
-
-    def consts2():
-        yield ("need", "pm")
-        for q, w in enumerate((512 * BIG, -512.0)):
-            for n, k in enumerate((1.0, 2.0, -1.0)):
-                yield act(a("RX", T.RX[:, n, :, q]), IND, F.Copy, scale=k * w)
-        yield act(c("RY"), IND, F.Copy, scale=-512 * BIG)
-        for q, w in enumerate((512 * BIG, 512.0)):
-            yield act(a("KR", T.KR[:, :, q, :]), a("If"), F.Copy, scale=w)
-        yield act(half("OB", 1), c("ONE"), F.Copy, scale=32 * BIG)
+            gs(half("D12", q), half("SEL", q), [[-1, 128]], A.not_equal, 0, 1, -1.0)
+        gi(c("RLi"), [[1, 8]], 0, 0)
+        gi(c("JI"), [[16, 8]], 0, 0)
+        gi(c("DJ"), [[0, 8], [1, 16]], 0, 0)
+        fill(c("MV"), 16)
+        gi(c("MV", 1, 15), [[2, 7], [-1, 2]], 1, 0)
+        gi(c("MV", 15, 29), [[1, 14]], 0, 0)
+        gi(c("MV", 47, 61), [[2, 7], [-1, 2]], 1, 0)
+        gi(c("CF"), [[0, 8], [512, 16]], -7680, 0)
+        cp(c("RL"), c("RLi"))
+        ts(c("M1"), c("DJ"), col(0), None, A.is_equal)
+        ts(c("JC", 0, 8), c("JI"), col(0), -128, A.add, A.add)
+        ms(c("JC", 8, 16), -14.5)
+        ms(c("JC", 16, 17), 65.5)
+        for k in range(2):
+            ms(a("COL", T.COL[P64(k), 8:9], 8, 9), 2048 - 1024 * k)
+            ms(a("CH", T.CH[P64(k), :], k, k + 1), (3.0, -0.25 / 64)[k])
+        ts(c("J8", 0, 8), c("JC", 0, 8), 8, col(8), A.mult, A.add)
+        if BOTH:
+            ms(c("JC", 17, 18), 16.0)
+            for o, n, k in ((8, 8, 1024), (16, 8, 2048), (24, 1, 1024)):
+                ts(c("J8", o, o + n), c("JC", 0, n), 8, k, A.mult, A.add)
+            for k in range(2):
+                gs(a("Df", T.Df[:, k], k, k + 1), ONE, [[0, 2], [-1, 64]], A.is_equal, -64 * k, 1)
+            for b, w in (("Db", 1.0), ("D8", -8.0)):
+                act(a(b), a("Df"), F.Copy, scale=w)
+        ms(c("N128"), -128.0)
+        ts(c("OH"), c("MV"), col(0), None, A.is_equal)
+        for q, w in enumerate((128.0, 1.0)):
+            act(half("IN2", q, 8), IND, F.Copy, scale=w)
         for k in range(2):
             for q in range(2):
-                yield act(a("BO2", T.BO2[P64(k), P64(q)]), a("BO", T.BO[P64(k), 4 * k:4 * k + 4, :]), F.Copy)
-        for q, w in enumerate((128.0, 1.0, 1.0, 0.0)):
-            yield act(half("IN3", q, 8), IND, F.Copy, scale=w)
-        yield ("need", "ck")
-        for q, w in enumerate((BIG, 1.0)):
-            yield act(a("CK", T.CK[0:64, :, q, :]), a("CKi", T.CKi[0:64, :, q, :]), F.Copy, scale=w / 64)
-        yield ("done", ("scan", -1))
+                act(a("BO2", T.BO2[P64(k), P64(q)], 2 * k + q, 2 * k + q + 1), a("BO", T.BO[P64(k), 4 * k:4 * k + 4, :]), F.Copy, scale=0.5)
+        act(c("BOa"), a("BO"), F.Copy, scale=-1.0)
         for q in range(2):
-            yield tt(half("A12", q), a("If"), CS("Zf", 14 + q), A.subtract)
-        yield ("need", "iotas")
-        yield cp(c("RL"), c("RLi"))
-        yield ts(c("M1"), c("DJ"), col(0), None, A.is_equal)
-        yield ts(c("JC", 0, 8), c("JI"), col(0), None, A.add)
-        yield act(half("J8", 0, 8), c("JC", 0, 8), F.Identity, bias=col(8), scale=8.0)
-        yield ts(c("OH"), c("MV"), col(0), None, A.is_equal)
-        yield ("done", "rest")
-        yield ts(col(6), u0, 14, -16, A.is_lt, A.mult)
-        yield ts(col(7), col(6), -1, -272, A.mult, A.add)
-        yield act(half("WP", 0), c("PERM"), F.Copy, scale=col(6))
-        yield act(half("WP", 1), a("If"), F.Copy, scale=col(7))
-        yield ("done", "wp")
-
-    def cuts(key, w, R, n, step, ss, on_v):
-        yield ("need", key)
-        for s in ss:
-            r = c(R, 256 * s + n, 256 * s + n + size(w))
-            if on_v:
-                yield ts(r, w, -step * s, 0, A.add, A.max)
-            else:
-                yield act(r, w, F.Relu, bias=c("KC", s + (16 if step > 1 else 0), s + (17 if step > 1 else 1)))
-            yield ("done", (key, s))
-
-    def gather_cuts(key, out, Z, w, R, n, more):
-        yield ("need", key)
-        yield [mm(out, CS(Z, 0), w, True, False)] + [mm(out, l, r, False, False) for l, r in more]
-        for s in range(1, 16):
-            yield ("need", (key, s))
-            yield mm(out, DS(Z, s), c(R, 256 * s + n, 256 * s + n + size(w)), False, s == 15)
-
-    def split(o, b, i):
-        return ts(names(b, i), o, M1_, -M1_, A.add, A.add), tt(rows(b, i), o, names(b, i), A.subtract)
-
-    def slots(h):
-        pr, two, p1, p2, p3 = half("PR", h), c("MK", 384 * h, 384 * h + 256), half("SB", h, 256), half("SB", 4 + h), c(("SB", "KP")[h], 0, 128)
-        if h == 0:
-            p3 = half("SB", 8)
-        for q, o in enumerate((A.is_gt, A.is_equal)):
-            yield ts(half("MK", 3 * h + q), pr, col(0), None, o)
-        yield group(p1, (c("LT"), two))
-        yield ts(half("P16", h), pr, 16, None, A.mult)
-        yield tt(half("AA", h, 256), p1, two, A.mult)
-        yield group(p2, (Ib, half("P16", h)), (c("I14"), half("MK", 3 * h + 1)), (c("I2"), half("AA", 2 * h)), (Ib, half("AA", 2 * h + 1)))
-        yield cp(half("W1", h), p2)
-        yield ("done", ("w0", h))
-        yield ts(half("MK", 3 * h + 2), pr, col(0), None, A.is_lt)
-        yield ts(half("NQ", h), half("NM", h), -2048, None, A.add)
-        yield ("done", ("w1", h))
-        for x in gather_cuts(("w0", h), p3, "Zb", half("W1", h), "R1", 128 * h,
-                             [(c("I2"), half("AA", 2 * h)), (Ib, half("MK", 3 * h + 2)), (c("Im"), half("NQ", h))]):
-            yield x
-        yield ts(half("W2", h), p3, col(2), None, A.add)
-        yield ("done", ("w2", h))
-
-    def first(h):
-        b, key = "TL", ("w2", h)
-        yield ("need", "cab")
-        yield ("need", key)
-        yield ("lock", "TL")
-        yield [mm(a(b, T[b][:, 0:8, :]), half("OB", 0), c("CAB"), True, False), mm(a(b, T[b][:, 0:8, 0]), half("W2", h), a("MV2", T.MV2[:, :, 1]), False, False)]
-        for s in range(1, 16):
-            yield ("need", (key, s))
-            yield mm(a(b, T[b][:, 0:8, s - 1:s + 1]), half("R2", 2 * s + h), a("MV2"), False, s == 15)
-        yield act(half("OC", h), a(b, T[b][:, 0:8, :]), F.Copy)
-        yield ("unlock", "TL")
-        yield ("need", ("st1", h - 3))
-        yield group(c("ST", 768, 896), (half("OC", h), a("If")))
-        for x in split(c("ST", 768, 896), "L", h):
-            yield x
-        for k in ("n", "m", "m2"):
-            yield ("done", (k, h))
-        yield ("done", ("st1", h - 2))
-
-    def columns(i):
-        h = i % 2
-        nm_ = names("L", i)
-        for k in (("n", i), "SXY", ("L", i - 1)):
-            yield ("need", k)
-        yield group(c("ST", 0, 128), (c("PERM"), nm_)) + group(c("ST", 128, 256), (SEL14, nm_)) + \
-            group(c("ST", 256, 384), (half("SXY", 0), nm_)) + group(c("ST", 384, 512), (half("SXY", 1), nm_))
-        for q in range(2):
-            yield tt(half("PP", 2 * h + q), half("ST", q), nm_, A.mult)
-        yield tt(half("QQ", h, 256), c("ST", 256, 512), half("PP", h, 256), A.add)
-        yield ("done", ("st0", i))
-        yield ts(half("HB", h, 256), half("QQ", h, 256), 65535, 5, A.bitwise_and, A.logical_shift_right)
-        yield cp(half("HF", h, 256), half("HB", h, 256))
-        ht = (T.HT[:, h], ("HT", h, h + 1))
-        yield op("v", lambda e: e.transpose(ht[0], half("HF", h, 256)[0]), ht, half("HF", h, 256), dur=FIX + CY * 128)
-        yield ("need", ("L", i - 1))
-        yield ("need", "pm")
-        for ib in range(4):
-            p = []
-            for x4 in range(2):
-                for g2 in range(2):
-                    w = ib * 32 + g2 * 16
-                    p.append(mm(c("ST", 2 * ib + x4, 256, 8), a("PM", T.PM[:, 2 * x4 + g2]), (T.HT[:, h, :, w:w + 16], ht[1]), g2 == 0, g2 == 1))
-            yield p
-        yield ("need", ("nc", i))
-        yield ts(half("OFF", h, 256), c("ST", 0, 256), c("NC", i, i + 1), None, A.add)
-        yield ("done", ("L", i))
+            gs(half("A12", q), c("BOa"), [[0, 8], [1, 16]], A.is_equal, -14 - q, 0)
+            gs(half("A12", q), half("A12", q), [[-1, 128]], A.not_equal, 0, 1, 1.0)
+        ts(col(6), u0, 14, -16, A.is_lt, A.mult)
+        ts(col(7), col(6), -1, -272, A.mult, A.add)
+        act(half("WP", 0), c("PERM"), F.Copy, scale=col(6))
+        act(half("WP", 1), If, F.Copy, scale=col(7))
 
     def thresholds():
         for h in range(2):
-            yield ts(c("COL", 16 + 5 * h, 21 + 5 * h), c("TH", 8 * h, 8 * h + 5), -1, -1, A.mult, A.add)
-        yield ms(a("ME"), 0.0)
-        yield cp(a("ME", T.ME[:, :, 0, 0:14]), a("BO", T.BO[:, :, 0:14]))
-        for i in range(2 * TS):
-            yield ts(half("TM", i, 256), a("ME"), col(16 + 5 * (i % 2) + i // 2), None, A.mult)
-            yield ("done", ("tm", i))
+            ts(c("CI", 8 * h, 8 * h + 5), c("TH", 8 * h, 8 * h + 5), 1, None, A.add)
+        mms(sum([group((T.KP[0:5, 224 * h:224 * h + 224], ("KP", 0, 1)), (c("CI", 8 * h, 8 * h + 5), a("ME"))) for h in range(2)], []))
+        cp((T.TB[0:5, :], c("TB")[1]), (T.KP[0:5, 0:448], ("KP", 0, 1)))
 
-    def gaps(i):
-        yield ("need", ("m", i))
-        if i < 2 * TS - 2:
-            yield send(i, 0)
-        for k in (("L", i), ("gv", i), ("dl", i - 1), ("st1", i - 2), "D12"):
-            yield ("need", k)
-        yield sum([group(c("ST", 512 + 128 * q, 640 + 128 * q), (half("D12", q), old(i)[0]), (half("D12", q), old(i)[1])) for q in range(2)], [])
-        yield act(half("DL", i % 2, 256), c("ST", 512, 768), F.Copy)
-        yield ("done", ("dl", i))
+    def cuts(w, R, h, step, on_v):
+        for s in range(1, 16):
+            r = c(R, 256 * s + 128 * h, 256 * s + 128 * h + size(w))
+            if on_v(s):
+                ts(r, w, -step * s, 0, A.add, A.max)
+            else:
+                act(r, w, F.Relu, bias=c("KC", s + (16 if step > 1 else 0), s + (17 if step > 1 else 1)))
 
-    old = lambda i: (names("O", i), rows("O", i), half("LR", i, 16)) if i < 2 * TS - 2 else (names("L", i), rows("L", i), c("LS", 32 * i + 8, 32 * i + 24))
-    XW = lambda h: c("X", XN * h, XN * h + XN)
-    cut = lambda lo, hi: [(s, min(4, hi - s)) for s in range(lo, hi, 4)]
-    SCH = sorted([(1,) + x for x in cut(0, 14)] + [(0,) + x for x in cut(NV, 14)], key=lambda x: -x[2])
-    on_v = lambda j: j in ON_V
-    rec = lambda h, y, s, n: c("WW", 4096 * h + 128 * (s + 1 + 16 * (1 - y)), 4096 * h + 128 * (s + n + 1 + 16 * (1 - y)))
-    tmp = lambda b, h, s, n: c(b, 2048 * h + 128 * s, 2048 * h + 128 * (s + n))
-    offs = lambda h, y, s, n: c("OFF", 256 * h + 128 * y + 8 * s, 256 * h + 128 * y + 8 * (s + n))
-    raw = lambda h, y, s, n: rec(h, y, s, n) if y else tmp("XR", h, s, n)
-    mag = lambda h, y, s, n: tmp("AY", h, s, n) if y else rec(h, y, s, n)
-    left = {}
+    def standing_sums(b, w, R, h, mv, base):
+        mms([(ps(b, 0), c("OB"), base, True, False), (a(b, T[b][:, 0:8, 0]), w, a(mv, T[mv][:, :, 1]), False, False)])
+        n_ = [15]
+        for s in range(1, 16):
+            mms([(a(b, T[b][:, 0:8, s - 1:s + 1]), half(R, 2 * s + h), a(mv), False, n_)], True)
 
-    def ready(i):
-        for k in (("L", i), ("m2", i), ("table", i - 2)):
-            yield ("need", k)
+    def exchange(out, pm, src, flags=None):
+        return [(out(x), a(pm, T[pm][:, 2 * x + y], 2 * x + y, 2 * x + y + 1), src(y)) + (flags or (y == 0, y == 1)) for x in range(2) for y in range(2)]
 
-    def gather_s(i):
-        for x in ready(i):
-            yield x
-        yield ("need", ("gs", i - 1))
-        for j, (y, s, n) in enumerate(SCH):
-            if on_v(j):
-                continue
-            if j >= AHEAD:
-                yield ("need", ("abs", i * len(SCH) + j - AHEAD))
-            yield act(raw(i % 2, y, s, n), ind(XW(i % 2), offs(i % 2, y, s, n)), F.Copy, bias=-128.0 * y)
-            yield ("done", ("g", i, j))
-        yield ("done", ("gs", i))
+    code, odd = a("SP", T.SP[:, 16:24, :]), lambda x: a("SP", T.SP[:, 16 + x:24:2, :])
 
-    def gather_v(i):
-        h = i % 2
-        for x in ready(i):
-            yield x
-        yield ("need", ("gv", i - 1))
-        for j, (y, s, n) in enumerate(SCH):
-            if on_v(j):
-                yield ts(raw(h, y, s, n), ind(XW(h), offs(h, y, s, n)), -128.0 * y, None, A.add)
-                yield ("done", ("g", i, j))
-        for s, n in cut(0, NV):
-            for k in range(s, s + n, 2):
-                yield tt(rec(h, 0, k, 2), ind(XW(h), offs(h, 0, k, 2)), c("ZL", 384 * i + 128, 384 * i + 384), A.subtract)
-            if s >= NA:
-                yield ts(tmp("RU", h, s, n), rec(h, 0, s, n), 0, None, A.max)
-            yield ("done", ("ru" if s >= NA else "dx", i, s))
-        yield ("done", ("gv", i))
+    def split(i):
+        ts(names("L", i), code, M1_, -M1_, A.add, A.add)
+        tt(rows("L", i), code, names("L", i), A.subtract)
 
-    def abs_x(i):
-        for s, n in cut(0, NA):
-            yield ("need", ("dx", i, s))
-            yield act(rec(i % 2, 0, s, n), rec(i % 2, 0, s, n), F.Abs)
-            yield ("done", ("ru", i, s))
+    def slots():
+        pr, mk, aa, p2 = c("P16"), lambda q: half("MK", q, 256), lambda q: half("AA", q, 256), c("S2", 0, 256)
+        ts(pr, c("PR"), 16, None, A.mult)
+        for q, o in enumerate((A.is_gt, A.is_equal)):
+            ts(mk(q), c("PR"), col(0), None, o)
+            mms(group(c("S%d" % q, 0, 256), (c("LT"), mk(q))))
+            tt(aa(q), c("S%d" % q, 0, 256), mk(q), A.mult)
+        for x in group(p2, (Ib, c("P16")), (c("I14"), mk(1)), (c("I2"), aa(0)), (Ib, aa(1))):
+            mms([x])
+        cp(c("W1"), p2)
+        ts(mk(2), pr, col(1), None, A.is_lt)
+        ts(c("NQ"), c("NM"), -2048, None, A.add)
+        cuts(c("W1"), "R1", 0, 16, lambda s: s % 3 != 2)
 
-    def keys_v(i):
-        yield ("need", ("k0", i))
-        for s, n in cut(0, NV):
-            yield ("need", ("ru", i, s))
-            yield [mm(KP(k, True), x, a("RX", T.RX[:, q]), False, left[i]) for k in range(s, s + n)
-                   for q, x in (((2, rec(i % 2, 0, k, 1)), (1, tmp("RU", i % 2, k, 1))) if s >= NA else ((0, rec(i % 2, 0, k, 1)),))]
-        yield ("done", ("kv", i))
+    def first(h):
+        b, p3 = ("T2", "T1")[h], c(("KP", "S0")[h], 0, 128)
+        mms([(p3, l, r, n == 0, False) for n, (l, r) in enumerate(((CS("Zb", 0), half("W1", h)), (c("I2"), half("AA", h)), (Ib, half("MK", 4 + h)), (c("Im"), half("NQ", h))))])
+        n_ = [15]
+        for s in range(1, 16):
+            mms([(p3, DS("Zb", s), half("R1", 2 * s + h), False, n_)], True)
+        ts(half("W2", h), p3, col(2), None, A.add)
+        cuts(half("W2", h), "R2", h, 1, lambda s: s % 7 % 2 == 0 or s == 15)
+        standing_sums(b, half("W2", h), "R2", h, "MV2", c("CAB"))
+        turn(four("OC", h), ps(b, 0))
+        mms(exchange(odd, "PMf", lambda y: four("OC", h, 16 * y, 16 * y + 16)))
+        split(h)
 
-    def minus_z(i):
-        for j, (y, s, n) in enumerate(SCH):
-            J = i * len(SCH) + j
-            b = 512 * (J % 4)
-            yield ("need", ("g", i, j))
-            yield ("need", ("abs", J - 4))
-            yield [mm(c("SB", b, b + 128 * n), Ib, raw(i % 2, y, s, n), True, False)] + \
-                [mm(c("SB", b + 128 * r, b + 128 * r + 256), nI, c("ZL", 384 * i + 128, 384 * i + 384), False, r == n - 2) for r in range(0, n, 2)]
-            yield ("done", ("d", J))
+    last = lambda i: i >= 2 * TS - 2
+    zz = lambda i: half("ZL", i)
+    rec = lambda h, x, s, n: c("WW", 3584 * h + 128 * (s + 14 * x), 3584 * h + 128 * (s + n + 14 * x))
+    tmp = lambda b, h, s, n: c(b, 1792 * h + 128 * s, 1792 * h + 128 * (s + n))
+    offs = lambda h, y, s, n: c("OFF", 224 * h + 112 * y + 8 * s, 224 * h + 112 * y + 8 * (s + n))
+    KP = lambda s, both: c("KP", s, 224, 14 if both else 28)
+    chunks = lambda ns: [(sum(ns[:j]), n) for j, n in enumerate(ns)]
+    bank = [0]
 
-    def absval(i):
-        for j, (y, s, n) in enumerate(SCH):
-            J = i * len(SCH) + j
-            b = 512 * (J % 4)
-            yield ("need", ("d", J))
-            yield act(mag(i % 2, y, s, n), c("SB", b, b + 128 * n), F.Abs, bias=col(15) if y else 0.0)
-            yield ("done", ("abs", J))
+    def columns(i):
+        h, nm_ = i % 2, names("L", i)
+        total = lambda b, r, done: [(ps(b, r, 14), nm_, c("LXY"), True, False)] + [(ps(b, r + 7 * q, 7), half("PP", 2 * h + q), c("PIf"), False, done and q == 1) for q in range(2)]
+        mms(group(ps("HP", 0), (c("PERM"), nm_)) + group(ps("HP", 8), (half("SEL", 0), nm_)))
+        for q in range(2):
+            tt(half("PP", 2 * h + q), ps("HP", 8 * q), nm_, A.mult)
+        for x in total(G1, 16, True):
+            mms([x])
+        if ON["mod"] == "v":
+            ts(half("QQ", h, 224), ps(G1, 16, 14), 32768, None, A.add)
+            ts(half("QQ", h, 224), half("QQ", h, 224), 5, 2047, A.arith_shift_right, A.bitwise_and)
+            ts(half("OFF", h, 224), half("QQ", h, 224), c("NC", i, i + 1), None, A.add)
+        else:
+            ts(half("KK", h, 224), ps(G1, 16, 14), MK_, -MK_, A.add, A.add)
+            b = "T2" if NB else "S0"
+            mms(total(b, 0, False))
+            mms(group(ps(b, 0, 14), (nI, half("KK", h, 224)), more=True))
+            ts(half("OFF", h, 224), ps(b, 0, 14), 1 / 32, c("NC", i, i + 1), A.mult, A.add)
+        turn(four("TR", h), rows("L", i))
+        if ON["rows"] == "s":
+            mms(sum([exchange(lambda x: a("HP", T.HP[:, 2 * x + q:16:4, 0:14]), pm, lambda y: four("TR", h, 16 * y, 16 * y + 14)) for q, pm in enumerate(("PMa", "PMb"))], []))
+            act(half("RK", h, 224), a("HP", T.HP[:, 0:16, 0:14]), F.Copy)
 
-    KP = lambda s, both: c("KP", s, 256, 16 if both else 32)
-
-    def keys(i):
-        left[i] = [28 + NV - min(NA, NV)]
-        kp = c("KP", 0, 256)
-        for k in (("scan", i - 1), ("L", i), ("m", i), ("tm", i), ("w2", 1)):
-            yield ("need", k)
-        yield [mm(kp, half("OB", 0), a("CK"), True, False), mm(kp, half("OB", 1), half("TM", i, 256), False, False),
-               mm(kp, rows("L", i), a("KR"), False, False)]
-        yield ("done", ("k0", i))
-        for j, (y, s, n) in enumerate(SCH):
-            yield ("need", ("abs", i * len(SCH) + j))
-            yield [mm(KP(k, not y), mag(i % 2, y, k, 1), c("RY") if y else a("RX", T.RX[:, 0]), False, left[i]) for k in range(s, s + n)]
-        yield ("done", ("ks", i))
+    def look(i):
+        t, h, n_ = i // 2, i % 2, [(1 if ON["rows"] == "s" else 32) + (NB > 0) + 4 * 14 - NB]
+        kp, w = c("KP", 0, 224), lambda x, j: a("RX", T.RX[:, j], j, j + 1) if x else half("RY", j, 8)
+        mms([(kp, c("OB"), a("CK"), True, False), (kp, (T.ST[0:5, C128(t)], half("ST", t)[1]), (T.TB[0:5, 224 * h:224 * h + 224], half("TB", h, 224)[1]), False, False)])
+        for l, r in [(Ib, half("RK", h, 224))][ON["rows"] != "s":] + [(zz(i), a("MZ"))][NB == 0:]:
+            mms([(kp, l, r, False, n_)], True)
+        for j in range(4 * (ON["rows"] != "s")):
+            mms(sum([exchange(lambda x: c("KP", 56 * j + 28 * x + 14 * q, 56 * j + 28 * x + 14 * q + 14), pm,
+                              lambda y: a("TR", T.TR[:, 4 * h + j, 16 * y:16 * y + 14], h, h + 1), (False, n_)) for q, pm in enumerate(("PMa", "PMb"))], []), True)
+        if NB < 14:
+            mms([(half("S1", k), Ib, zz(i), True, True) for k in range(4)])
+        mms([(c("S2"), c("OB"), c("C3"), True, False)] + [(half("S2", k), Ib, zz(i), False, k == 3) for k in range(4)])
+        for j, (x, s, n, q) in enumerate(CH):
+            q = "v" if j in MORE.get(i, ()) else q
+            raw, top = rec(h, x, s, n), c("MX", 3584 * h + 128 * (s + 14 * x), 3584 * h + 128 * (s + n + 14 * x))
+            one = lambda b, k: c(b, 3584 * h + 128 * (k + 14 * x), 3584 * h + 128 * (k + 1 + 14 * x))
+            if q == "v":
+                ts(raw, ind(XW(h), offs(h, 1 - x, s, n)), 384 * x - 192, None, A.add)
+            else:
+                act(raw, ind(XW(h), offs(h, 1 - x, s, n)), F.Copy, bias=384.0 * x - 192)
+            if q == "b":
+                b = "S%d" % (s // 4 % 2 if NB == 14 else 0)
+                mms([(c(b, 0, 128 * n), Ib, raw, True, False)] + [(half(b, k), nI, zz(i), False, k == n - 1) for k in range(n)])
+                act(top, c(b, 0, 128 * n), F.Abs)
+                mms([(KP(k, x), one("MX", k), w(x, 2), False, n_) for k in range(s, s + n)], True)
+            else:
+                mms([(KP(k, x), one("WW", k), w(x, 0), False, n_) for k in range(s, s + n)], True)
+                tt(top, raw, c("S1" if x else "S2", 0, 128 * n), A.max)
+                mms([(KP(k, x), one("MX", k), w(x, 1), False, n_) for k in range(s, s + n)], True)
 
     def choose(i):
         h = i % 2
-        for k in (("ks", i), ("kv", i), "rest"):
-            yield ("need", k)
-        sc = half("SC", h, 256)
-        yield op("v", lambda e: e.tensor_tensor_scan(sc[0], T.D0[:, :], T.KP[:, 0:256], 0.0, A.mult, A.max), sc, c("D0"), a("KP"), dur=FIX + CY * 256)
-        yield ("done", ("scan", i))
-        w = c("SC", 256 * h + 31, 256 * h + 256, 32)
-        yield ts(half("FF", h, 8), w, BIG, 1 / BIG, A.is_lt, A.max)
-        yield tt(half("SE", h, 8), w, half("FF", h, 8), A.mult)
-        yield ts(half("KQ", h, 8), half("SE", h, 8), 31, None, A.bitwise_and)
-        yield tt(half("GM", h), ind(half("KQ", h, 8), c("RL")), c("M1"), A.mult)
-        yield ("need", ("m", 1))
-        yield ("lock", "TL")
-        p = a("TL", T.TL[:, 0:2, :])
-        yield group(p, (Ib, c("JC")), (half("GM", h), c("IN3")))
-        yield cp(half("LS", i, 32), p)
-        yield ("unlock", "TL")
-        yield ("done", ("LS", i))
-        if i < 2 * TS - 2:
-            yield send(i, 2)
-        yield ("done", ("LR", i))
-        if i < 2 * TS - 2:
-            yield ("need", ("zn", i))
-            yield send(i, 1)
-            yield ("done", ("m2", i + 2))
-
-    def table(i):
-        t, h = i // 2, i % 2
-        yield ("need", ("LS", i))
-        yield ("need", ("ww", h))
-        pick = ind(half("WW", h, 4096), c("LS", 32 * i, 32 * i + 8))
-        zn = zed("S", i)
-        yield act(half("AW", h), pick, F.Abs)
-        yield tt(half("SZ", h), pick, zed("L", i), A.add)
-        yield ts(half("HZ", h), half("SZ", h), 0.5, 63.75, A.mult, A.add)
-        yield tt(zn, half("HZ", h), half("AW", h), A.min)
-        yield ("done", ("zn", i))
-        if t + 1 == TS:
-            for k in range(2):
-                yield out_(T.yz[P64(h), C128(k)], T.ZS[P64(k), C128(3 * i + 1)], zn[1])
-        p1 = a("TL", T.TL[:, 2, 0:8])
-        yield ("lock", "TL")
-        yield group(p1, (c("Im"), half("J8", 1, 8)), *[(CS("Zb", k), c("ZS", 384 * i + 128 + k, 384 * i + 256, 16)) for k in range(16)])
-        yield ts(half("K8", h, 8), p1, M8_, -M8_, A.add, A.add)
-        yield act(half("UU", h, 8), p1, F.Copy) if US else cp(half("UU", h, 8), p1)
-        yield group(p1, (Ib, half("J8", 0, 8)), (c("Im"), half("J8", 2, 8)), (a("If"), half("UU", h, 8)), (nI, half("K8", h, 8)))
-        yield cp(half("LC", h, 8), p1)
-        yield ("unlock", "TL")
-        xw, own = c("X", XN * h, XN * h + 2048), lambda k, p: T.X[P64(p), XN * h + 1024 * k:XN * h + 1024 * k + 1024]
-        yield tt(half("SX2", h), ind(xw, half("LC", h, 8)), zn, A.add)
-        yield ts(half("HX2", h), half("SX2", h), 0.5, -0.25, A.mult, A.add)
-        yield cp(ind(xw, half("LC", h, 8)), half("HX2", h))
-        if t + 1 == TS:
-            for k in range(2):
-                yield out_(T.yx[P64(h), 1024 * k:1024 * k + 1024], own(k, k), xw[1], ("s", "sy")[k])
-        else:
-            s = "tw%d" % h
-            cps = [(own(k, 1 - k), own(k, k)) for k in range(2)] + [(T.X[P64(k), XN * h + 2048:XN * h + XN], T.X[P64(0), XN * h:XN * h + 64]) for k in range(2)]
-
-            def fn(e):
-                for o, x in cps:
-                    e.dma_start(o, x).then_inc(sem[s], 16)
-            cnt[s] = 64 * (t + 1)
-            yield ("sy", fn, [], [XW(h)[1]], None, 0, 240.0, 0.0, lambda tm: note(s, [], [XW(h)[1]], s, cnt[s], dict(know["sy"]), tm + TWIN))
-        yield ("done", ("table", i))
-
-    def state(i):
-        h = i % 2
-        yield ("need", ("LR", i))
-        yield ("need", ("dl", i))
-        yield tt(half("TT", h, 256), ind(c("OH"), old(i)[2]), half("DL", h, 256), A.mult)
-        yield ("need", ("st1", i - 1))
-        o = c("ST", 768, 896)
-        yield group(o, (Ib, old(i)[0]), (Ib, old(i)[1]), (half("A12", 0), half("TT", 2 * h)), (half("A12", 1), half("TT", 2 * h + 1)))
-        n, r = split(o, "L", i + 2)
-        yield n
-        yield ("done", ("n", i + 2))
-        yield r
-        yield ("done", ("st1", i))
-        yield ("done", ("m", i + 2))
+        sc, sm = half("SC", h, 224), lambda b: half(b, h, 8)
+        op("v", lambda e: e.tensor_tensor_scan(sc[0], T.D0[:, :], T.KP[:, 0:224], 0.0, A.mult, A.max), sc, a("D0"), a("KP"), dur=FV + CY * 224)
+        w = c("SC", 224 * h + 27, 224 * h + 224, 28)
+        ts(sm("FF"), w, BIG, 1 / BIG, A.is_lt, A.max)
+        tt(sm("SE"), w, sm("FF"), A.mult)
+        ts(half("KQ", h, 8), sm("SE"), 31, None, A.bitwise_and)
+        cp(half("KL", i, 8), half("KQ", h, 8))
+        if not last(i):
+            send(i, 2)
+        tt(half("GM", h), ind(half("KQ", h, 8), c("RL")), c("M1"), A.mult)
+        mms(group(a("T1", T.T1[:, 0, :]), (Ib, c("JC", 0, 16)), (half("GM", h), c("IN2"))))
+        cp(half("LS", h, 8), a("T1", T.T1[:, 0, 0:8]))
 
     def count(i):
         t, h = i // 2, i % 2
-        yield ("need", ("LS", i))
-        yield ts(half("ES", h, 8), c("LS", 32 * i + 8, 32 * i + 16), 16, None, A.is_ge)
-        p = a("TL", T.TL[:, 4, 0:1])
-        yield ("lock", "TL")
-        yield group(p, (Ib, c("NC", i, i + 1)), *[(c("BO2"), c("ES", 8 * h + k, 8 * h + k + 1)) for k in range(8)])
-        yield ts(c("AI", i, i + 1), p, 1 / 64, -63 / 128, A.mult, A.add)
-        yield ts(c("NC", i + 2, i + 3), c("AI", i, i + 1), -64, p, A.mult, A.add)
-        yield ("unlock", "TL")
-        yield ("done", ("nc", i + 2))
-        if t + 1 == TS:
+        p, terms = a("T1", T.T1[:, 1, 0:1]), [(a("If"), c("NC", i, i + 1)), (c("OB"), c("JC", 16, 17)), (c("BO2"), c("ES", h, h + 1))]
+        mms(group(p, *terms))
+        act(c("AI", i, i + 1), p, F.Copy, bias=-63 / 128 - KAP / 64, scale=1 / 64)
+        ts(c("NC", i + 2, i + 3), c("AI", i, i + 1), -64, p, A.mult, A.add)
+        if last(i):
             ye, at = c("YE", 8 * h, 8 * h + 5), c("AT", 8 * h, 8 * h + 5)
-            yield ts(at, c("AI", h, 10, 2), 64, None, A.mult)
-            yield tt(ye, c("NC", h + 2, 12, 2), c("NC", h, 10, 2), A.subtract)
-            yield tt(ye, ye, at, A.add)
-            yield out_(T.ye[P64(h), :], T.YE[0:64, 8 * h:8 * h + 5], ye[1])
+            ts(at, c("AI", h, 10, 2), -129, 64, A.add, A.mult)
+            tt(ye, c("NC", h + 2, 12, 2), c("NC", h, 10, 2), A.subtract)
+            tt(ye, ye, at, A.add)
+            dmas("sy", [(T.ye[P64(h), :], T.YE[0:64, 8 * h:8 * h + 5])], [ye[1]], [], "out", 20)
+
+    def table(i):
+        h = i % 2
+        zn, p, u = half("ZS", i), a("T2", T.T2[:, 0:8, :]), a("T2", T.T2[:, 8, 0:8])
+        act(half("PK", h), ind(half("WW", h, 3584), half("LS", h, 8)), F.Copy)
+        mms(group(ps("T2", 16), (nI, zz(i)), (Ib, half("PK", h))))
+        act(half("AW", h), ps("T2", 16), F.Abs)
+        mms(group(p, (c("OB"), c("CH")), (c("Ih"), zz(i)), (c("Ih"), half("PK", h))))
+        lin(ON["a192"], half("A2", h), half("AW", h), 1.0, 192.0)
+        tt(zn, p, half("A2", h), A.min)
+        if not last(i):
+            send(i, 1)
+        sums = [(CS("Zb", k), c("ZS", 128 * i + k, 128 * i + 128, 16)) for k in range(16)]
+        mms(group(a("T1", T.T1[:, 2, 0:8]), *sums))
+        lin(ON["k8"], half("K8", h, 8), a("T1", T.T1[:, 2, 0:8]), 1 / 8, -255.4375)
+        lin(ON["u"], half("UU", h, 8), a("T1", T.T1[:, 2, 0:8]), 1.0, 0.0)
+        jk, es = half("JK", h, 8), c("ES", h, h + 1)
+        add("s", [lambda e: e.activation(jk[0], T.T1[:, 0, 8:16], F.Sign, accum_out=es[0])], [("T1", 0, 1)], [jk[1], es[1]], FS + 75.0)
+        if BOTH and not last(i):
+            dup = lambda b, k: a(b, T[b][:, k], k, k + 1)
+            u, val, lc = a("T2", T.T2[:, 8:25, 0]), ps("T2", 8, 17), c("LC", 18 * h, 18 * h + 17)
+            parts = ((1, 0, 8), (0, 8, 8), (1, 16, 1))
+            mms([(u, Ib, c("J8", 8, 25), True, False), (a("T2", T.T2[:, 24:25, 0]), c("OB"), c("JC", 17, 18), False, False)] + [(a("T2", T.T2[:, 8 + o:8 + o + n, 0]), dup(b, k), c(x, 8 * h, 8 * h + n), False, o == 16 and b == "D8")
+                                                         for k, o, n in parts for b, x in (("Df", "UU"), ("D8", "K8"))])
+            ts(lc, u, -2040, None, A.add)
+            act(half("XO", h, 272), ind(XW(h), lc), F.Copy)
+            mms([(val, Ib, half("XO", h, 272), True, False)] + [(ps("T2", 8 + o, n), dup("Db", k), c("ZS", 128 * i, 128 * i + 16 * n), False, o == 16) for k, o, n in parts])
+            lin(ON["avg"], half("HX", h, 272), val, 0.5, 32 - 0.1875)
+            tt(ind(XW(h), lc), half("HX", h, 272), c("N128"), A.add)
+            return
+        mms(group(u, (Ib, c("J8", 0, 8)), (c("I8"), half("K8", h, 8)), (a("If"), half("UU", h, 8))))
+        xw, lc, hx = c("X", XN * h, XN * h + 2048), c("LC", 18 * h, 18 * h + 8), c("HX", 272 * h, 272 * h + 128)
+        ts(lc, u, -2040, None, A.add)
+        tt(half("SX", h), ind(xw, lc), zn, A.add)
+        lin(ON["avg"], hx, half("SX", h), 0.5, 32 - 0.1875)
+        tt(ind(xw, lc), hx, c("N128", 0, 128), A.add)
+        if last(i):
+            for k in range(2):
+                dmas(("s", "sy")[k], [(T.yx[P64(h), 1024 * k:1024 * k + 1024], xs(h, k, 1024 - 1024 * k, 1024))], [xw[1]], [], "out", 2048)
+            ts(half("ZO", h), zn, -192, None, A.add)
+            dmas("sy", [(T.yz[P64(h), C128(k)], T.ZO[P64(k), C128(h)]) for k in range(2)], [half("ZO", h)[1]], [], "out", 256)
+        else:
+            dmas("sy", [(xs(h, 1 - k, 1024 - 1024 * k, 1024), xs(h, k, 1024 - 1024 * k, 1024)) for k in range(2)] + [(xs(h, k, 2048, 64), xs(h, 1, 0, 64)) for k in range(2)],
+                 [], [XW(h)[1]], "tw%d" % h, 1088)
+
+    def state(i):
+        h = i % 2
+        old, lst = ((rows("L", i),), half("KL", i, 8)) if last(i) else ((names("O", i), rows("O", i)), half("LR", i, 8))
+        mms(sum([group(a("SP", T.SP[:, 8 * q:8 * q + 8, :]), *[(half("D12", q), x) for x in old]) for q in range(2)], []))
+        act(half("DL", h, 256), a("SP", T.SP[:, 0:16, :]), F.Copy)
+        mms(group(code, *[(Ib, x) for x in old], done=False))
+        for q in range(2):
+            tt(half("TT", 2 * h + q), ind(half("OH", q, 32), lst), half("DL", 2 * h + q), A.mult)
+            mms(group(code, (half("A12", q), half("TT", 2 * h + q)), more=True, done=q == 1))
+        if last(i):
+            act(half("RF", h), code, F.Copy)
+        else:
+            split(i + 2)
 
     def finish(h):
-        i = 2 * (TS - 1) + h
-        for k in (("st1", i), ("st0", 2 * TS - 1), ("L", 2 * TS - 1), "wp", ("fin", h - 1)):
-            yield ("need", k)
-        r, o = rows("L", i + 2), (T.ST[0:8, 256:384], ("ST", 0, 1))
-        yield group(c("ST", 0, 128), (half("WP", 0), r), (half("WP", 1), r)) + group(o, (c("Ib", 14, 128, 16), r))
-        yield ts(half("W1", h), c("ST", 0, 128), 127.5, None, A.add)
-        yield ("done", ("w3", h))
-        y = (T.YF[0:8, C128(h)], half("YF", h)[1])
-        yield ts(y, o, -16, 7.5, A.mult, A.add)
-        for k in range(2):
-            yield out_(T.yf[4 * h:4 * h + 4, C128(k)], T.YF[4 * k:4 * k + 4, C128(h)], y[1])
-        p = c("ST", 384, 512)
-        for x in gather_cuts(("w3", h), p, "Zb", half("W1", h), "R1", 128 * h, []):
-            yield x
-        yield ts(half("YP", h), p, col(1), None, A.add)
-        yield ("done", ("fin", h))
-        for k in range(2):
-            yield out_(T.yp[P64(h), C128(k)], T.YP[P64(k), C128(h)], half("YP", h)[1])
+        r, y = half("RF", h), (T.YF[0:8, C128(h)], half("YF", h)[1])
+        mms(group(ps("HP", 0), (half("WP", 0), r), (half("WP", 1), r)))
+        ts(half("W1", h), ps("HP", 0), 127.5, None, A.add)
+        mms([(a("SP", T.SP[0:8, 0:8, k]), c("RF", 128 * h + k, 128 * h + 128, 16), c("Ib", 14, 128, 16), True, True) for k in range(16)])
+        act(y, a("SP", T.SP[0:8, 0:8, :]), F.Copy, scale=-16.0, bias=7.5)
+        dmas("sy", [(T.yf[4 * h:4 * h + 4, C128(k)], T.YF[4 * k:4 * k + 4, C128(h)]) for k in range(2)], [y[1]], [], "out", 512)
+        cuts(half("W1", h), "R1", h, 16, lambda s: s % 3 != 2)
+        standing_sums("HP", half("W1", h), "R1", h, "MVb", c("CF"))
+        turn(four("OC", h), ps("HP", 0))
+        mms(exchange(lambda x: a("HP", T.HP[:, 16 + x:24:2, :]), "PMf", lambda y: four("OC", h, 16 * y, 16 * y + 16)))
+        act(half("YP", h), ps("HP", 16), F.Copy, scale=1 / 4096)
+        dmas("sy", [(T.yp[P64(h), C128(k)], T.YP[P64(k), C128(h)]) for k in range(2)], [half("YP", h)[1]], [], "out", 512)
 
-    third = [s for s in range(1, 16) if s % 3 == 2]
-    rest = [s for s in range(1, 16) if s % 3 != 2]
+    loads()
+    consts()
+    slots()
+    for h in range(2):
+        stream[0] = h
+        first(h)
+    for h in range(2):
+        stream[0] = h
+        columns(h)
+    thresholds()
+    ahead = lambda i: send(i, 0)
+    for i in range(2 * TS):
+        stream[0] = i % 2
+        for name, f in [("ahead", ahead)][last(i):] + [("look", look), ("choose", choose), ("table", table), ("count", count), ("state", state),
+                                                       ("next", (lambda i: finish(i % 2)) if last(i) else (lambda i: columns(i + 2)))]:
+            part[:] = [name + ("'" if last(i) and name in ("state", "next") else ""), i, 0]
+            f(i)
 
-    def threads():
-        th = [(None, 0, x) for x in (consts_g(), consts(), consts2(), thresholds())]
-        for h in range(2):
-            th += [(h - 2, 0, x) for x in (slots(h), cuts(("w0", h), half("W1", h), "R1", 128 * h, 16, rest, True),
-                                           cuts(("w0", h), half("W1", h), "R1", 128 * h, 16, third, False), first(h), cuts(("w2", h), half("W2", h), "R2", 128 * h, 1, range(1, 16, 2), False),
-                                           cuts(("w2", h), half("W2", h), "R2", 128 * h, 1, range(2, 16, 2), True))]
-        for i in range(2 * TS):
-            th += [(i, 2 if f is choose else f in (gather_s, gather_v), f(i)) for f in (choose, state, columns, table, count, gaps, minus_z, absval, keys, gather_s, gather_v, keys_v, abs_x)]
-        for h in range(2):
-            th += [(2 * TS + h, 0, x) for x in (finish(h), cuts(("w3", h), half("W1", h), "R1", 128 * h, 16, rest if h == 0 else third, True),
-                                                cuts(("w3", h), half("W1", h), "R1", 128 * h, 16, third if h == 0 else rest, False))]
-        return [x + (y,) for x, y in zip(th, [BULK] * 4 + [0] * 12 + list(URGENT) * 2 * TS + [0] * 6)]
-
-    took = [0.0]
-
-    def plan(due):
-        for x in (cnt, hist, left) + tuple(know.values()):
-            x.clear()
-        for q in free:
-            free[q] = 0.0
-        sent[0] = 0
-        begin()
-        ev = {("nc", 0), ("nc", 1), ("gs", -1), ("gv", -1), ("st0", -1), ("st1", -3), ("dl", -1), ("L", -1), ("fin", -1), ("abs", -1), ("abs", -2), ("abs", -3), ("abs", -4)}
-        live, blocked, held, th, log, t_of, by, after = [], {}, set(), threads(), [], {}, {}, {}
-
-        def pull(r):
-            while True:
-                x, r[3] = r[3] or next(r[1], None), None
-                if x is None:
-                    return
-                if isinstance(x, tuple) and x[0] in ("done", "unlock"):
-                    if x[0] == "done":
-                        ev.add(x[1])
-                        by[x[1]] = r[0]
-                    else:
-                        held.discard(x[1])
-                    for y in blocked.pop(x[1], ()):
-                        pull(y)
-                elif isinstance(x, tuple) and x[0] in ("need", "lock"):
-                    if (x[1] not in ev) if x[0] == "need" else (x[1] in held):
-                        r[3] = x
-                        blocked.setdefault(x[1], []).append(r)
-                        return
-                    if x[0] == "lock":
-                        held.add(x[1])
-                    elif by.get(x[1]) in t_of:
-                        after.setdefault((r[0][0], r[0][1] + 1), []).append(by[x[1]])
-                else:
-                    r[2], r[0] = x if isinstance(x, list) else [x], (r[0][0], r[0][1] + 1)
-                    r[5] = {y[0] for d in r[2] for y in list(d[2]) + list(d[3])}
-                    live.append(r)
-                    return
-
-        def when(r):
-            seen = (r[0], sum(len(hist.get(b, ())) + ver.get(b, 0) for b in r[5]))
-            if r[4][0] != seen:
-                t, o = 0.0, 0.0
-                for d in r[2]:
-                    t, o = max([t] + [e[7] + WAKE - o for e in needs(d[0], d[2], d[3])]), o + d[6]
-                r[4] = (seen, t, o)
-            return max(free[r[2][0][0]], r[4][1]), r[4][2]
-
-        for n, x in enumerate(th):
-            pull([(n, 0), x[2], None, None, (None,), None])
-        while live:
-            at = [when(r) + ((th[r[0][0]][3] if r[2][0][0] in UQ else 0, due.get(r[0], 0.0)), r) for r in live]
-            t0 = min(x[0] for x in at)
-            now = min([x for x in at if x[0] == t0], key=lambda x: (x[2], x[3][0]))
-            soon = [x for x in at if x[3][2][0][0] == now[3][2][0][0] and x[2] < now[2] and x[0] < t0 + min(HOLD, now[1]) and (x[2][0] < now[2][0] or x[2][1] < t0 + now[1] + SLACK)]
-            s, dur, _, best = min(soon, key=lambda x: x[2]) if soon else now
-            live.remove(best)
-            key[0] = best[0]
-            t_of[key[0]] = s
-            pre = [(e[8], e[7] + WAKE - t_of[e[8]]) for d in best[2] for e in needs(d[0], d[2], d[3]) if e[8] in t_of and e[8] != key[0]]
-            log.append((key[0], dur, pre, best[2][0][0]))
-            for d in best[2]:
-                do(d)
-            pull(best)
-        assert not blocked
-        took[0] = max(t_of.values())
-        end, nxt_due, queue, durs = took[0], {}, {x[0]: x[3] for x in log}, {x[0]: x[1] for x in log}
-        for k, dur, pre, q in reversed(log):
-            i = th[k[0]][0]
-            t = min(nxt_due.get(k, end), end - dur - (LAST if i in (2 * TS - 2, 2 * TS) else 0.0))
-            if th[k[0]][1] and k[1] == 1:
-                t = min(t, t_of[k] - EARLY * (i + 1) if due else FIRST + i // 2 * PERIOD + i % 2 * SKEW + (GATHER if th[k[0]][1] == 2 else 0.0))
-            nxt_due[k] = t
-            before = (k[0], k[1] - 1)
-            for p, lag in pre + [(p, durs[p]) for p in after.get(k, []) + ([before] if before in durs else [])]:
-                j = th[p[0]][0]
-                if j is None or (i is not None and i - j in (0, 2)) or p in after.get(k, ()):
-                    nxt_due[p] = min(nxt_due.get(p, end), t - lag)
-        return nxt_due
-
-    if not DUE:
-        due, best = plan({}), None
-        for n in range(PASSES):
-            nxt_ = plan(due)
-            if best is None or took[0] < best[0]:
-                best = (took[0], due)
-            due = nxt_
-        DUE.update(best[1])
-    dry[0] = False
-    plan(DUE)
+    if not ORDER:
+        end, at = arrange(nodes, edges)
+        ORDER.update({"end": end, "at": at})
+    needed = {p for x in nodes for p in x["wait"]}
+    cnt, know, seen = {}, {q: {} for q in Q}, {}
+    for k in sorted(range(len(nodes)), key=lambda k: (ORDER["at"][k], k)):
+        x = nodes[k]
+        q, s = x["q"], x["s"]
+        if q == "e":
+            seen[k] = seen[k - 1]
+            continue
+        for p in sorted(x["wait"], key=lambda p: -ORDER["at"][p]):
+            ps, pn, snap = seen[p]
+            if know[q].get(ps, 0) < pn:
+                Q[q].wait_ge(sem[ps], pn)
+                for y, n in list(snap.items()) + [(ps, pn)]:
+                    know[q][y] = max(know[q].get(y, 0), n)
+        calls = [fn(Q[q]) for fn in x["fns"]]
+        if x["inc"] < 0:
+            cnt[s] = -x["inc"]
+            seen[k] = (s, cnt[s], {})
+            continue
+        for call in (calls if x["inc"] == 16 else calls[-1:] if k in needed else []):
+            call.then_inc(sem[s], x["inc"])
+            cnt[s] = cnt.get(s, 0) + x["inc"]
+        seen[k] = (s, cnt.get(s, 0), dict(know[q]))
     for s in cnt:
         g.wait_ge(sem[s], cnt[s])
-    for i in range(2 * TS - 2):
-        for k in range(3):
-            g.wait_ge(sem["a%d%d" % (i, k)], ein * (1 + k % 2))
     g.wait_ge(sem.sent, sent[0])

import math
from concourse.mybir import dt, AluOpType as A, AxisListType, ActivationFunctionType as F
from concourse.bass import DstId, RemoteDMATransfer

N, TS = 4, 5
WAKE, CALL, SHIP, LOAD, ROW, RATE = 135.0, 1000.0, 2800.0, 1800.0, 40.0, 20.0
CY, PE, FV, FS, GA, SCA = 0.85, 0.46, 47.0, 75.0, 1.75, 3.8
ROUNDS, SKEWS, SWAPS, HEAT = 0, (), 15000, 50.0
MARK, NEAR, HOLDS, WIDE = 0.2, 40, (100.0, 150.0, 220.0), 30
AGAIN = 6
PERIODS, START, STRETCH, LAST = ((12000.0, 6000.0), (13000.0, 6500.0), (14000.0, 7000.0)), 19000.0, 1.5, 8000.0
HALF, LATE = 0, 500.0
PLAN = {"SC0": 0, "FF0": .35, "SE0": .6, "KQ0": .84, "KL0": 1.05, "GM0": 1.16, "LS0": 1.7, "A20": 3.06, "ZS0": 3.28, "K80": 4.26, "UU0": 4.36, "TT0": 4.47, "TT1": 4.74,
        "LC0": 5.19, "SX0": 5.2, "NL0": 5.82, "PP0": 6.47, "PP1": 6.63, "X0": 6.8, "NL1": 9.2, "TR0": 9.4, "KK0": 7.73, "OFF0": 8.9, "NC0": 8.65,
        "MX0": 1.81, "MX1": 2.3, "MX2": 2.79, "MX3": 3.77, "MX4": 5.32, "MX5": 5.98, "MX6": 7.9, "MX7": 8.2,
        "DL0": 0, "PK0": 1.98, "AW0": 2.68, "XO0": 5.41, "HX0": 6.0, "JK0": 5.2, "AI0": 7.4,
        "WW0": .6, "WW1": 1.3, "WW2": 2.24, "WW3": 2.89, "WW4": 3.66, "WW5": 4.44, "WW6": 5.87, "WW7": 6.64}
ORDER = {}
ON = {"k8": "v", "a192": "v", "avg": "s", "mod": "p", "u": "v", "old": "v", "rows": "p"}
CH = ((1, 0, 2, "v"), (1, 2, 4, "s"), (1, 6, 4, "s"), (1, 10, 4, "s"), (0, 0, 4, "s"), (0, 4, 4, "s"), (0, 8, 4, "s"), (0, 12, 2, "s"))
MORE = {}
NB = sum(x[2] for x in CH if x[3] == "b")
BIG, M1_, MK_ = 2.0 ** 20, 1.5 * 2 ** 23, 1.5 * 2 ** 39
KAP = 0.0 if ON["mod"] == "v" else 1024 - 31 / 64
BOTH, G1, ALL = False, "T2", 16
XN = 2176
f32, b16, h16, i32, u16 = "float32", "bfloat16", "float16", "int32", "uint16"
SB_ = {
    "X": ([2 * XN], b16), "NM": ([256], i32), "PR": ([256], i32), "TH": ([16], i32), "CI": ([16], h16), "TB": ([448], h16), "ST": ([640], b16), "NIL": ([128], f32), "C3": ([512], b16), "PK": ([256], b16),
    "ME": ([8, 2, 14], b16), "MZ": ([8, 2, 14], b16),
    "ONE": ([128], f32), "If": ([8, 16], f32), "BOa": ([128], f32), "BO": ([8, 16], f32), "LT": ([128], b16), "PERM": ([128], b16),
    "PI": ([16], i32), "PI2": ([16], i32), "DJ": ([128], i32), "M1": ([128], b16), "COL": ([16], f32), "KC": ([32], f32),
    "Ib": ([128], b16), "nI": ([128], b16), "I2": ([128], b16), "I14": ([128], b16), "Im": ([128], b16), "Ih": ([128], b16), "I8": ([128], b16),
    "BO2": ([128], f32), "Zb": ([2, 144], b16), "A12": ([256], f32), "SEL": ([256], b16), "D12": ([256], b16), "MV2": ([8, 2], f32), "MVb": ([8, 2], b16),
    "PIf": ([112], f32), "LXY": ([224], b16), "WP": ([256], b16), "CAB": ([128], b16), "CF": ([128], b16), "CH": ([128], b16), "N128": ([272], b16),
    "PMf": ([4, 128], f32), "PMa": ([4, 128], b16), "PMb": ([4, 128], b16),
    "RX": ([3, 8, 2], b16), "RY": ([16], b16), "CK": ([8, 2, 14], b16), "CKi": ([8, 2, 14], f32), "OB": ([128], b16), "D0": ([224], f32), "RLi": ([8], i32), "RL": ([8], u16),
    "JI": ([8], i32), "JC": ([24], b16), "RK": ([448], b16), "QQ": ([448], i32), "UU": ([16], f32), "J8": ([32], b16), "IN2": ([16], b16), "MV": ([64], i32), "OH": ([64], b16),
    "MK": ([768], b16), "P16": ([256], b16), "NQ": ([256], h16), "AA": ([512], b16), "W1": ([256], b16), "W2": ([256], f32),
    "R1": ([4096], b16), "R2": ([4096], f32), "OC": ([8, 32], f32), "TR": ([8, 32], h16), "RF": ([256], b16),
    "NL": ([2560], h16), "NO": ([2048], h16), "KL": ([80], u16), "LR": ([64], u16), "ZL": ([2560], b16), "ZS": ([1280], b16),
    "PP": ([512], f32), "KK": ([448], b16), "DL": ([512], f32), "TT": ([512], f32),
    "OFF": ([448], u16), "WW": ([7168], b16), "MX": ([7168], b16),
    "SC": ([448], f32), "FF": ([16], f32), "SE": ([16], i32), "KQ": ([16], i32), "GM": ([256], b16), "LS": ([16], u16), "JK": ([16], f32), "ES": ([2], f32),
    "AW": ([256], b16), "A2": ([256], b16), "K8": ([16], b16), "LC": ([36], u16), "SX": ([256], f32), "HX": ([544], b16), "XO": ([544], b16),
    "Df": ([2, 128], f32), "Db": ([2, 128], b16), "D8": ([2, 128], b16),
    "NC": ([16], f32), "AI": ([16], b16), "AT": ([16], f32), "YE": ([16], f32), "YP": ([256], f32), "YF": ([256], f32), "ZO": ([256], b16),
}
SCRATCH = {k: ("sbuf", [128] + v[0], v[1]) for k, v in SB_.items()}
PSUM = {"S0": [512], "S1": [512], "S2": [512], "KP": [512], "HP": [32, 16], "SP": [32, 16], "T1": [32, 16], "T2": [32, 16]}
SCRATCH.update({k: ("psum", [128] + v, f32) for k, v in PSUM.items()})
SEMAPHORES = ["v", "p", "s", "gq", "sent", "out", "tw0", "tw1"] + ["l%d" % k for k in range(12)] + ["a%d%d" % (i, k) for i in range(2 * TS - 2) for k in range(3)]


def arrange(nodes, edges):
    n = len(nodes)
    dur = [x["dur"] for x in nodes]
    pre, suc = [[] for _ in nodes], [[] for _ in nodes]
    for (p, k), lag in edges.items():
        pre[k].append((p, lag))
        suc[p].append((k, lag + dur[k] - dur[p]))

    def sweep(pre_, suc_, prio):
        left, at, busy = [len(x) for x in pre_], [0.0] * n, {}
        ready = sorted((prio[k], k) for k in range(n) if not left[k])
        while ready:
            k = ready.pop(0)[1]
            t = max([0.0] + [at[p] + lag for p, lag in pre_[k]])
            row = busy.setdefault(nodes[k]["q"], [])
            j = len(row)
            while j and row[j - 1][1] > t:
                j -= 1
            while j < len(row) and row[j][0] < t + dur[k]:
                t = max(t, row[j][1])
                j += 1
            row.insert(j, (t, t + dur[k]))
            at[k] = t
            for m, _ in suc_[k]:
                left[m] -= 1
                if not left[m]:
                    ready.append((prio[m], m))
                    ready.sort()
        return at, max(at[k] + dur[k] + nodes[k]["lat"] for k in range(n))

    def deal(due, hold):
        at, todo, late = [None] * n, {}, 0.0
        for k in sorted(range(n), key=lambda k: due[k]):
            todo.setdefault(nodes[k]["q"], []).append(k)
        free, look = {q: 0.0 for q in todo}, {q: 0.0 for q in todo}
        while look:
            q = min(look, key=lambda q: look[q])
            t, memo = look[q], {}

            def soon(k):
                if k not in memo:
                    memo[k] = max([0.0] + [(at[p] if at[p] is not None else max(soon(p), free[nodes[p]["q"]], t)) + lag for p, lag in pre[k]])
                return memo[k]
            some, limit, pick = todo[q][:WIDE], 1e12, None
            for k in some:
                if soon(k) <= t + 1 and all(at[p] is not None for p, _ in pre[k]):
                    if t + dur[k] <= limit:
                        pick = k
                        break
                else:
                    limit = min(limit, max(soon(k) + hold, due[k] + late))
            if pick is None:
                look[q] = max(t + 20, min(soon(k) for k in some))
                continue
            at[pick], free[q] = t, t + dur[pick]
            look[q] = free[q]
            if nodes[pick]["tag"] == ("choose", 0):
                late = t - due[pick]
            todo[q].remove(pick)
            if not todo[q]:
                del look[q]
        return at, max(at[k] + dur[k] + nodes[k]["lat"] for k in range(n))

    tail = [0.0] * n
    for k in range(n - 1, -1, -1):
        tail[k] = max([dur[k] + nodes[k]["lat"]] + [tail[m] + lag - dur[m] + dur[k] for m, lag in suc[k]])
    best = None
    for skew in SKEWS:
        prio = [-tail[k] + skew * nodes[k]["h"] for k in range(n)]
        for r in range(ROUNDS):
            at, end = sweep(pre, suc, prio)
            if best is None or end < best[0]:
                best = (end, at)
            back, _ = sweep(suc, pre, [-(at[k] + dur[k] + nodes[k]["lat"]) for k in range(n)])
            prio = [-(back[k] + dur[k]) for k in range(n)]
    seed = [1]

    def rnd():
        seed[0] = (seed[0] * 1103515245 + 12345) % 2147483648
        return seed[0] / 2147483648

    twins = {}
    for k, x in enumerate(nodes):
        twins.setdefault(x["tag"], []).append(k)
    for period, skew in PERIODS:
        due, after = [0.0] * n, {}
        for k in range(n - 1, -1, -1):
            x = nodes[k]
            due[k] = min([START + 4 * period + skew + LAST - x["lat"] - dur[k]] + [due[m] - (lag - dur[m] + dur[k]) for m, lag in suc[k]])
            if x["tag"] == ("choose", 0):
                due[k] = min(due[k], START + x["i"] // 2 * period + x["h"] * skew)
            if x["tag"][0] == "look" and x["q"] != "p":
                due[k] = min(due[k], after.get((x["i"], x["q"]), 1e9) - STRETCH * dur[k])
                after[(x["i"], x["q"])] = due[k]
        for hold in HOLDS:
            at, end = deal(due, hold)
            for r in range(AGAIN + 1):
                if best is None or end < best[0]:
                    best = (end, at)
                if r < AGAIN:
                    back, _ = sweep(suc, pre, [-(at[k] + dur[k] + nodes[k]["lat"]) for k in range(n)])
                    at, end = sweep(pre, suc, [-(back[k] + dur[k]) for k in range(n)])
    line = sorted(range(n), key=lambda k: (best[1][k], k))
    if HALF:
        scan = {nodes[k]["i"]: best[1][k] for k in twins[("choose", 0)]}
        when = list(best[1])
        for k, x in enumerate(nodes):
            if x["i"] >= 0:
                t0 = scan[0] + x["i"] * HALF
                if x["key"] in PLAN and x["q"] != "sy" and "'" not in x["tag"][0]:
                    when[k] = t0 + 1000 * PLAN[x["key"]] - HALF * (x["tag"][0] in ("look", "ahead"))
                elif x["q"] in "vs":
                    when[k] += t0 - scan[x["i"]]
                else:
                    when[k] = max([t0 - HALF] + [when[p] + lag for p, lag in pre[k]])
        left, line = [len(x) for x in pre], []
        ready = [k for k in range(n) if not left[k]]
        while ready:
            k = min(ready, key=lambda k: when[k])
            ready.remove(k)
            line.append(k)
            for m, _ in suc[k]:
                left[m] -= 1
                if not left[m]:
                    ready.append(m)
        pre2, suc2, tail_ = [list(x) for x in pre], [list(x) for x in suc], {}
        for k in line:
            q = nodes[k]["q"]
            if (q in "vs" or "KP0" in PLAN) and q in tail_:
                pre2[k].append((tail_[q], dur[tail_[q]]))
                suc2[tail_[q]].append((k, 0.0))
            tail_[q] = k
        at = sweep(pre2, suc2, [when[k] + LATE * (x["key"][:2] == "KP") for k, x in enumerate(nodes)])[0]
        line = sorted(range(n), key=lambda k: (at[k], k))
    before, last, rest = [None] * n, {}, [dur[k] + nodes[k]["lat"] for k in range(n)]
    for k in line:
        before[k], last[nodes[k]["q"]] = last.get(nodes[k]["q"]), k
    direct = [{p for p, _ in x} for x in pre]

    def times(line, before, at, why, lo):
        for k in line[lo:]:
            t, w, b = 0.0, None, before[k]
            for p, lag in pre[k]:
                if at[p] + lag > t:
                    t, w = at[p] + lag, p
            if b is not None and at[b] + dur[b] >= t:
                t, w = at[b] + dur[b], b
            at[k], why[k] = t, w
        return max(range(n), key=lambda k: at[k] + rest[k])

    at, why = [0.0] * n, [None] * n
    k = times(line, before, at, why, 0)
    marks = twins[("choose", 0)]
    cost = lambda at, k: at[k] + rest[k] + MARK * sum(at[x] for x in marks)
    now = cost(at, k)
    best = (at[k] + rest[k], [at[x] + 1e-4 * j for j, x in sorted(enumerate(line), key=lambda y: y[1])])
    for r in range(SWAPS):
        pairs = []
        if rnd() < 0.7:
            k = marks[int(rnd() * len(marks))]
        while why[k] is not None:
            if why[k] == before[k] and why[k] not in direct[k]:
                pairs.append((why[k], k))
            k = why[k]
        u, v = pairs[int(rnd() * min(len(pairs), NEAR))]
        line2, before2, at2, why2, first = line, list(before), list(at), list(why), n
        up, far = rnd() < 0.5, 1 + int(6 * rnd() ** 2)
        mover = v if up else u
        some = [mover] if rnd() < 0.3 else [x for x in twins[nodes[mover]["tag"]] if rnd() < 0.5 or nodes[x]["h"] == nodes[mover]["h"]]
        for x0 in [x for x in some for _ in range(far)]:
            if up:
                u, v = before2[x0], x0
            else:
                u, v = x0, before2.index(x0) if x0 in before2 else None
            if u is None or v is None:
                continue
            lo, hi = line2.index(u), line2.index(v)
            down, stay, move = {u}, [], []
            for x in line2[lo + 1:hi]:
                if before2[x] in down or direct[x] & down:
                    down.add(x)
                    move.append(x)
                else:
                    stay.append(x)
            if not direct[v] & down:
                for x in line2[hi + 1:]:
                    if before2[x] == v:
                        before2[x] = u
                        break
                line2, first = line2[:lo] + stay + [v, u] + move + line2[hi + 1:], min(first, lo)
                before2[v], before2[u] = before2[u], v
        if first < n:
            k2 = times(line2, before2, at2, why2, first)
            end, new = at2[k2] + rest[k2], cost(at2, k2)
            if new < now - HEAT * (1 - r / SWAPS) * math.log(1e-9 + rnd()):
                line, before, at, why, now = line2, before2, at2, why2, new
                if end < best[0]:
                    best = (end, [at[x] + 1e-4 * j for j, x in sorted(enumerate(line), key=lambda y: y[1])])
        k = max(range(n), key=lambda k: at[k] + rest[k])
    return best


def rank_program(g, core, T, topo):
    rank = T.rank_of(core)
    if rank is None:
        return
    sem = T.sem
    Q = {"v": g.vector, "p": g.tensor, "s": g.scalar, "gq": g, "sy": g.sync}
    nodes, edges, hist, stream, part, seen_ = [], {}, {}, [0], ["", -1, 0], {}

    def add(q, fns, rd, wr, dur, lat=0.0, s=None, inc=1, free=False, moving=0.0):
        k, me = len(nodes), (q if inc == 1 else s)
        nodes.append({"q": q, "fns": fns, "dur": dur, "lat": lat, "s": s or q, "inc": inc, "h": stream[0], "wait": set(), "i": part[1], "tag": (part[0], part[2] if inc > 0 else s[-1])})
        part[2] += inc > 0
        name = (q, part[1], (wr or rd)[0][0])
        seen_[name] = seen_.get(name, -1) + 1
        nodes[k]["key"] = name[2] + str(seen_[name])

        def edge(p, wait):
            e = nodes[p]
            edges[(p, k)] = max(edges.get((p, k), 0.0), e["dur"] + (e["lat"] + WAKE if wait else 0.0))
            if wait:
                nodes[k]["wait"].add(p)
        for b in {r[0] for r in rd + wr if r[0] in PSUM}:
            old = hist.get(b, [])
            for e in old:
                if not (free and e[2]):
                    edge(e[0], e[1] != q)
            hist[b] = (old if free else []) + [(k, q, free)]
        for regs, w in ((rd, False), (wr, True)):
            for (b, lo, hi) in regs:
                if b in PSUM:
                    continue
                for e in hist.get(b, ()):
                    if e[0] < k and e[2] < hi and lo < e[3] and (w or e[4]):
                        edge(e[0], (e[4] or e[1] != me) and b != "GQ")
                hist[b] = [e for e in hist.get(b, ()) if not (w and lo <= e[2] and e[3] <= hi)] + [(k + (moving > 0), me, lo, hi, w)]
        if moving:
            nodes.append(dict(nodes[k], q="e", dur=moving, lat=0.3 * lat, wait=set(), tag=nodes[k]["tag"] + ("e",), key="-"))
            nodes[k]["lat"], edges[(k, k + 1)] = 0.0, dur + 0.7 * lat

    def c(b, lo=0, hi=None, st=1):
        hi = T[b].shape[1] if hi is None else hi
        return (T[b][:, lo:hi:st], (b, lo, hi))

    def a(b, ap=None, lo=0, hi=1 << 20):
        return (T[b][:] if ap is None else ap, (b, lo, hi))

    def ind(w, o):
        return (w[0].indirect(o[0]), w[1], o[1])

    def size(x):
        return math.prod(int(k) for k in list(x[0].shape)[1:])

    def op(q, fn, out, *ins, dur):
        add(q, [fn], [r for x in ins for r in x[1:]] + list(out[2:]), [out[1]], dur)

    def narrow(*xs):
        return all(SCRATCH[x[1][0]][2] in (b16, h16, u16) for x in xs)

    def span(out, i, f, fix=FV):
        if len(out) > 2:
            return fix + SCA * CY * size(i)
        if len(i) > 2:
            return fix + max(f, GA) * CY * size(out)
        return fix + CY * max(64, f * size(out))

    def tt(out, x, y, o):
        op("v", lambda e: e.tensor_tensor(out[0], x[0], y[0], o), out, x, y, dur=span(out, x, 1 if x[1][0] in PSUM or y[1][0] in PSUM else 2))

    def ts(out, x, s1, s2, o0, o1=None):
        y = [s for s in (s1, s2) if isinstance(s, tuple)]
        f1, f2 = [s[0] if isinstance(s, tuple) else s for s in (s1, s2)]
        more = () if o1 is None else (o1,)
        op("v", lambda e: e.tensor_scalar(out[0], x[0], f1, f2, o0, *more), out, x, *y, dur=span(out, x, 0.5 if narrow(out, x) else 1))

    def cp(out, x):
        op("v", lambda e: e.tensor_copy(out[0], x[0]), out, x, dur=span(out, x, 0.5 if narrow(out, x) else 1))

    def ms(out, k):
        op("v", lambda e: e.memset(out[0], k), out, dur=span(out, out, 0.5 if narrow(out) else 1))

    def turn(out, x):
        op("v", lambda e: e.transpose(out[0], x[0]), out, x, dur=span(out, x, 0.5 if narrow(out, x) else 1))

    def act(out, x, f, bias=0.0, scale=1.0):
        y = [s for s in (bias, scale) if isinstance(s, tuple)]
        bb, sc = [s[0] if isinstance(s, tuple) else s for s in (bias, scale)]
        op("s", lambda e: e.activation(out[0], x[0], f, bias=bb, scale=sc), out, x, *y, dur=span(out, x, 1, FS))

    def lin(q, out, x, scale, bias):
        if q == "v":
            ts(out, x, scale, bias, A.mult, A.add)
        else:
            act(out, x, F.Copy, bias=bias, scale=scale)

    def mms(terms, free=False):
        def call(out, l, r, first, last):
            def fn(e):
                if isinstance(last, list):
                    last[0] -= 1
                    return e.matmul(out[0], l[0], r[0], first, last[0] == 0)
                return e.matmul(out[0], l[0], r[0], first, last)
            return fn
        d = sum(max(min(64, size(l)), size(r)) * PE * (4 if SCRATCH[l[1][0]][2] == f32 else 1) for _, l, r, _, _ in terms)
        add("p", [call(*x) for x in terms], [y[1] for x in terms for y in x[1:3]], [x[0][1] for x in terms], d, free=free)

    def group(out, *terms, more=False, done=True):
        return [(out, l, r, n == 0 and not more, done and n == len(terms) - 1) for n, (l, r) in enumerate(terms)]

    def dmas(q, pairs, rd, wr, s, n):
        add(q, [lambda e, o=o, x=x: e.dma_start(o, x) for o, x in pairs], rd, wr, 60.0 * len(pairs), LOAD, s, 16, moving=sum(int(o.shape[0]) for o, _ in pairs) * (ROW + n / RATE) / 16)

    def gi(out, pat, base, cm):
        k = {} if SCRATCH[out[1][0]][2] == i32 else {"allow_small_or_imprecise_dtypes": True}
        add("gq", [lambda e: e.iota(out[0], pat, base, cm, **k)], [], [out[1], ("GQ", 0, 1)], 130 + 2 * CY * size(out))

    def gs(out, x, pat, cmp_, base, cm, fill=0.0):
        add("gq", [lambda e: e.affine_select(out[0], x[0], pat, cmp_, fill, base, cm)], [x[1]], [out[1], ("GQ", 0, 1)], 170 + 2 * CY * size(out))

    nxt, prv = T.cores[(rank + 1) % N], T.cores[(rank - 1) % N]
    ein, eout = len(topo.engines(prv, core)[:ALL]), topo.engines(core, nxt)[:ALL]
    sent = [0]

    def send(i, k):
        rid, pid = topo.addr(nxt, core)
        s = "a%d%d" % (i, k)
        sent[0] += len(eout)
        src, dst = ((half("NL", i, 256), [half("NO", i, 256)]), (half("ZS", i), [half("ZL", i + 2)]), (half("KL", i, 8), [half("LR", i, 8)]))[k]
        tr = [RemoteDMATransfer(dst_ids=[DstId(rid=rid, pnc=pid)] * len(dst), dma_engine_mask=sum(1 << x for x in eout), remote_sem=sem[s], srcs=[src[0]], dsts=[x[0] for x in dst])]
        add("gq", [lambda e: e.remote_dma_fused(tr, local_sem=sem.sent)], [src[1]], [x[1] for x in dst], CALL, SHIP, s, -ein * len(dst), moving=16 * (ROW + (512, 256, 16)[k] / 10))

    half = lambda b, h, n=128: c(b, h * n, h * n + n)
    col = lambda j: c("COL", j, j + 1)
    names = lambda b, i: half("N" + b, 2 * i)
    rows = lambda b, i: half("N" + b, 2 * i + 1)
    Ib, nI, IND, u0, ONE = c("Ib"), c("nI"), a("BO", T.BO[:, :, 0]), c("PI2", 0, 1), c("ONE")
    CS = lambda b, s: a(b, T[b][:, 0, 15 - s:143 - s])
    DS = lambda b, s: a(b, T[b][:, 1, 15 - s:143 - s])
    P64 = lambda k: slice(64 * k, 64 * k + 64)
    C128 = lambda k: slice(128 * k, 128 * k + 128)
    four = lambda b, h, lo=0, hi=32: a(b, T[b][:, 4 * h:4 * h + 4, lo:hi], h, h + 1)
    ps = lambda b, r, n=8: a(b, T[b][:, r:r + n, :]) if len(PSUM[b]) > 1 else c(b, 16 * r, 16 * (r + n))
    XW = lambda h: c("X", XN * h, XN * h + XN)
    xs = lambda h, k, lo, n: T.X[P64(k), XN * h + lo:XN * h + lo + n]

    def loads():
        for h in range(2):
            for n, (b, src) in enumerate((("PR", T.pr), ("NM", T.nm))):
                dmas("sy" if h else "s", [(T[b][P64(k), C128(h)], src[P64(h), C128(k)]) for k in range(2)], [], [half(b, h)[1]], "l%d" % (2 * h + n), 512)
        dmas("sy", [(T.TH[P64(k), 8 * h:8 * h + 5], T.th[P64(h), :]) for k in range(2) for h in range(2)], [], [c("TH")[1]], "l4", 20)
        dmas("sy", [(T.ZL[P64(k), C128(h)], T.z0[P64(h), C128(k)]) for k in range(2) for h in range(2)], [], [c("ZL", 0, 256)[1]], "l5", 256)
        for h in range(2):
            dmas("sy", [(xs(h, k, lo, n), T.xt[P64(h), src:src + n]) for k in range(2) for lo, src, n in ((0, 1024, 1024), (1024, 0, 1024), (2048, 1024, 128))],
                 [], [XW(h)[1]], "l%d" % (6 + h), 1450)
        for k in range(4, len(nodes) - 2):
            edges[(k, k + 2)] = nodes[k]["dur"]

    def consts():
        fill = lambda x, k: gi(x, [[0, size(x)]], k, 0)
        If = a("If")
        ms(ONE, 1.0)
        gi(c("PI"), [[0, 16]], 0, 1)
        gs(c("BOa"), ONE, [[-16, 8], [0, 16]], A.is_ge, 0, 1)
        gs(a("BO"), c("BOa"), [[16, 8], [0, 16]], A.is_ge, 15, -1)
        gs(c("LT"), a("BO"), [[1, 128]], A.is_gt, 0, -1)
        gs(If, ONE, [[-1, 128]], A.is_equal, 0, 1)
        gi(c("KC", 16, 32), [[-16, 16]], 0, 0)
        gi(c("KC", 0, 16), [[-1, 16]], 0, 0)
        gi(a("CAB", T.CAB[0:64, :]), [[0, 8], [64, 16]], -992, 0)
        for i in range(4):
            gs(a("PMf", T.PMf[:, i], i, i + 1), ONE, [[-32, 4], [1000, 2], [-1, 16]], A.is_equal, -16 * (i // 2) - 1000 * (i % 2), 1)
        gs(c("PERM"), ONE, [[-2, 64], [1, 2]], A.is_equal, -1, 1)
        one = c("ONE", 0, 112)
        gs(c("PIf"), one, [[-1, 14], [-16, 8]], A.is_equal, 0, 1)
        ms(c("NIL"), 0.0)
        for q, (pat, base, k, l) in enumerate((([[-2, 7], [1, 2], [-16, 8]], -1, 2400.0, 3232.0), ([[0, 14], [-16, 8]], -14, 3232.0, 2400.0))):
            gs(half("LXY", q, 112), c("NIL", 0, 112), pat, A.not_equal, base, 1, k)
            gs(half("LXY", q, 112), half("LXY", q, 112), [[-1, 14], [-16, 8]], A.not_equal, 0, 1, l)
        ts(c("PI2"), c("PI"), 15, None, A.bitwise_and)
        ts(col(1), u0, 16, None, A.mult)
        ts(col(0), u0, 1, None, A.mult)
        ts(col(2), u0, 16 - 2.0 ** -16, -240 + 0.5 + 15 * 2.0 ** -16, A.mult, A.add)
        ms(a("Zb"), 0.0)
        for j, o, k in ((0, 15, 1), (1, 15, 1), (1, 14, -1)):
            ts(a("Zb", T.Zb[:, j, o:o + 128:16]), IND, k, None, A.mult)
        for b, k in (("Ib", 1.0), ("I2", 2.0), ("I14", 14.0), ("Im", 2.0 ** -12), ("nI", -1.0), ("Ih", 0.5), ("I8", -8.0)):
            act(c(b), If, F.Copy, scale=k)
        ms(c("OB"), 1.0)
        for b in ("MV2", "MVb"):
            for q in range(2):
                act(a(b, T[b][:, :, q], q, q + 1), IND, F.Copy, scale=4096.0 * (2 * q - 1))
        ms(a("CAB", T.CAB[64:128, :]), -15 / 2048)
        for q in range(2):
            ts(col(3 + q), u0, 14 + q, None, A.is_equal)
            act(half("SEL", q), a("BO"), F.Copy, scale=col(3 + q))
        ms(c("NC", 0, 2), KAP)
        ts(c("ZL", 0, 256), c("ZL", 0, 256), 192, None, A.add)
        for j, k in enumerate((-1.0, 2.0, 1.0)[:2 + (NB > 0)]):
            for q, w in enumerate((512 * BIG, -512.0)):
                act(a("RX", T.RX[:, j, :, q], j, j + 1), IND, F.Copy, scale=k * w)
        for q, w in enumerate((512 * BIG, -1024 * BIG)):
            act(half("RY", q, 8), IND, F.Copy, scale=w)
        ms(c("C3"), -3.0)
        ms(c("D0"), 1.0)
        gs(a("ME"), c("D0"), [[-16, 8], [-1000, 2], [0, 14]], A.is_ge, 0, 1)
        gs(a("ME"), a("ME"), [[16, 8], [0, 28]], A.is_ge, 15, -1)
        for t in range(TS):
            gs((T.ST[0:5, C128(t)], half("ST", t)[1]), (T.NIL[0:5, 0:128], c("NIL")[1]), [[0, 128]], A.not_equal, -t, 1, -32 * BIG)
        if NB:
            ms(a("MZ"), 0.0)
            for q, w in enumerate((512 * BIG, -512.0)):
                ts(a("MZ", T.MZ[:, :, q, 0:NB]), a("BO", T.BO[:, :, 0:NB]), w, None, A.mult)
        for b, w in (("PMa", 512 * BIG), ("PMb", 512.0)):
            act(a(b), a("PMf"), F.Copy, scale=w)
        gi(a("CKi"), [[0, 8], [-210, 2], [1, 14]], 241, 0)
        for q, (w, k, l) in enumerate(((BIG, -16 * 6144 * BIG, 0.0), (1.0, 16 * 5088.0, 16.0))):
            act(a("CK", T.CK[0:64, :, q, :], q, q + 1), a("CKi", T.CKi[0:64, :, q, :]), F.Copy, scale=w / 64)
            ms(a("CK", T.CK[64:96, :, q, :], 2 + q, 3 + q), k)
            ms(a("CK", T.CK[96:128, :, q, :], 4 + q, 5 + q), l)
        gs(c("D0"), c("D0"), [[0, 8], [1, 28]], A.is_gt, 0, 0)
        for q in range(2):
            gs(half("D12", q), half("SEL", q), [[-1, 128]], A.not_equal, 0, 1, -1.0)
        gi(c("RLi"), [[1, 8]], 0, 0)
        gi(c("JI"), [[16, 8]], 0, 0)
        gi(c("DJ"), [[0, 8], [1, 16]], 0, 0)
        fill(c("MV"), 16)
        gi(c("MV", 1, 15), [[2, 7], [-1, 2]], 1, 0)
        gi(c("MV", 15, 29), [[1, 14]], 0, 0)
        gi(c("MV", 47, 61), [[2, 7], [-1, 2]], 1, 0)
        gi(c("CF"), [[0, 8], [512, 16]], -7680, 0)
        cp(c("RL"), c("RLi"))
        ts(c("M1"), c("DJ"), col(0), None, A.is_equal)
        ts(c("JC", 0, 8), c("JI"), col(0), -128, A.add, A.add)
        ms(c("JC", 8, 16), -14.5)
        ms(c("JC", 16, 17), 65.5)
        for k in range(2):
            ms(a("COL", T.COL[P64(k), 8:9], 8, 9), 2048 - 1024 * k)
            ms(a("CH", T.CH[P64(k), :], k, k + 1), (3.0, -0.25 / 64)[k])
        ts(c("J8", 0, 8), c("JC", 0, 8), 8, col(8), A.mult, A.add)
        if BOTH:
            ms(c("JC", 17, 18), 16.0)
            for o, n, k in ((8, 8, 1024), (16, 8, 2048), (24, 1, 1024)):
                ts(c("J8", o, o + n), c("JC", 0, n), 8, k, A.mult, A.add)
            for k in range(2):
                gs(a("Df", T.Df[:, k], k, k + 1), ONE, [[0, 2], [-1, 64]], A.is_equal, -64 * k, 1)
            for b, w in (("Db", 1.0), ("D8", -8.0)):
                act(a(b), a("Df"), F.Copy, scale=w)
        ms(c("N128"), -128.0)
        ts(c("OH"), c("MV"), col(0), None, A.is_equal)
        for q, w in enumerate((128.0, 1.0)):
            act(half("IN2", q, 8), IND, F.Copy, scale=w)
        for k in range(2):
            for q in range(2):
                act(a("BO2", T.BO2[P64(k), P64(q)], 2 * k + q, 2 * k + q + 1), a("BO", T.BO[P64(k), 4 * k:4 * k + 4, :]), F.Copy, scale=0.5)
        act(c("BOa"), a("BO"), F.Copy, scale=-1.0)
        for q in range(2):
            gs(half("A12", q), c("BOa"), [[0, 8], [1, 16]], A.is_equal, -14 - q, 0)
            gs(half("A12", q), half("A12", q), [[-1, 128]], A.not_equal, 0, 1, 1.0)
        ts(col(6), u0, 14, -16, A.is_lt, A.mult)
        ts(col(7), col(6), -1, -272, A.mult, A.add)
        act(half("WP", 0), c("PERM"), F.Copy, scale=col(6))
        act(half("WP", 1), If, F.Copy, scale=col(7))

    def thresholds():
        for h in range(2):
            ts(c("CI", 8 * h, 8 * h + 5), c("TH", 8 * h, 8 * h + 5), 1, None, A.add)
        mms(sum([group((T.KP[0:5, 224 * h:224 * h + 224], ("KP", 0, 1)), (c("CI", 8 * h, 8 * h + 5), a("ME"))) for h in range(2)], []))
        cp((T.TB[0:5, :], c("TB")[1]), (T.KP[0:5, 0:448], ("KP", 0, 1)))

    def cuts(w, R, h, step, on_v):
        for s in range(1, 16):
            r = c(R, 256 * s + 128 * h, 256 * s + 128 * h + size(w))
            if on_v(s):
                ts(r, w, -step * s, 0, A.add, A.max)
            else:
                act(r, w, F.Relu, bias=c("KC", s + (16 if step > 1 else 0), s + (17 if step > 1 else 1)))

    def standing_sums(b, w, R, h, mv, base):
        mms([(ps(b, 0), c("OB"), base, True, False), (a(b, T[b][:, 0:8, 0]), w, a(mv, T[mv][:, :, 1]), False, False)])
        n_ = [15]
        for s in range(1, 16):
            mms([(a(b, T[b][:, 0:8, s - 1:s + 1]), half(R, 2 * s + h), a(mv), False, n_)], True)

    def exchange(out, pm, src, flags=None):
        return [(out(x), a(pm, T[pm][:, 2 * x + y], 2 * x + y, 2 * x + y + 1), src(y)) + (flags or (y == 0, y == 1)) for x in range(2) for y in range(2)]

    code, odd = a("SP", T.SP[:, 16:24, :]), lambda x: a("SP", T.SP[:, 16 + x:24:2, :])

    def split(i):
        ts(names("L", i), code, M1_, -M1_, A.add, A.add)
        tt(rows("L", i), code, names("L", i), A.subtract)

    def slots():
        pr, mk, aa, p2 = c("P16"), lambda q: half("MK", q, 256), lambda q: half("AA", q, 256), c("S2", 0, 256)
        ts(pr, c("PR"), 16, None, A.mult)
        for q, o in enumerate((A.is_gt, A.is_equal)):
            ts(mk(q), c("PR"), col(0), None, o)
            mms(group(c("S%d" % q, 0, 256), (c("LT"), mk(q))))
            tt(aa(q), c("S%d" % q, 0, 256), mk(q), A.mult)
        for x in group(p2, (Ib, c("P16")), (c("I14"), mk(1)), (c("I2"), aa(0)), (Ib, aa(1))):
            mms([x])
        cp(c("W1"), p2)
        ts(mk(2), pr, col(1), None, A.is_lt)
        ts(c("NQ"), c("NM"), -2048, None, A.add)
        cuts(c("W1"), "R1", 0, 16, lambda s: s % 3 != 2)

    def first(h):
        b, p3 = ("T2", "T1")[h], c(("KP", "S0")[h], 0, 128)
        mms([(p3, l, r, n == 0, False) for n, (l, r) in enumerate(((CS("Zb", 0), half("W1", h)), (c("I2"), half("AA", h)), (Ib, half("MK", 4 + h)), (c("Im"), half("NQ", h))))])
        n_ = [15]
        for s in range(1, 16):
            mms([(p3, DS("Zb", s), half("R1", 2 * s + h), False, n_)], True)
        ts(half("W2", h), p3, col(2), None, A.add)
        cuts(half("W2", h), "R2", h, 1, lambda s: s % 7 % 2 == 0 or s == 15)
        standing_sums(b, half("W2", h), "R2", h, "MV2", c("CAB"))
        turn(four("OC", h), ps(b, 0))
        mms(exchange(odd, "PMf", lambda y: four("OC", h, 16 * y, 16 * y + 16)))
        split(h)

    last = lambda i: i >= 2 * TS - 2
    zz = lambda i: half("ZL", i)
    rec = lambda h, x, s, n: c("WW", 3584 * h + 128 * (s + 14 * x), 3584 * h + 128 * (s + n + 14 * x))
    tmp = lambda b, h, s, n: c(b, 1792 * h + 128 * s, 1792 * h + 128 * (s + n))
    offs = lambda h, y, s, n: c("OFF", 224 * h + 112 * y + 8 * s, 224 * h + 112 * y + 8 * (s + n))
    KP = lambda s, both: c("KP", s, 224, 14 if both else 28)
    chunks = lambda ns: [(sum(ns[:j]), n) for j, n in enumerate(ns)]
    bank = [0]

    def columns(i):
        h, nm_ = i % 2, names("L", i)
        total = lambda b, r, done: [(ps(b, r, 14), nm_, c("LXY"), True, False)] + [(ps(b, r + 7 * q, 7), half("PP", 2 * h + q), c("PIf"), False, done and q == 1) for q in range(2)]
        mms(group(ps("HP", 0), (c("PERM"), nm_)) + group(ps("HP", 8), (half("SEL", 0), nm_)))
        for q in range(2):
            tt(half("PP", 2 * h + q), ps("HP", 8 * q), nm_, A.mult)
        for x in total(G1, 16, True):
            mms([x])
        if ON["mod"] == "v":
            ts(half("QQ", h, 224), ps(G1, 16, 14), 32768, None, A.add)
            ts(half("QQ", h, 224), half("QQ", h, 224), 5, 2047, A.arith_shift_right, A.bitwise_and)
            ts(half("OFF", h, 224), half("QQ", h, 224), c("NC", i, i + 1), None, A.add)
        else:
            ts(half("KK", h, 224), ps(G1, 16, 14), MK_, -MK_, A.add, A.add)
            b = "T2" if NB else "S0"
            mms(total(b, 0, False))
            mms(group(ps(b, 0, 14), (nI, half("KK", h, 224)), more=True))
            ts(half("OFF", h, 224), ps(b, 0, 14), 1 / 32, c("NC", i, i + 1), A.mult, A.add)
        turn(four("TR", h), rows("L", i))
        if ON["rows"] == "s":
            mms(sum([exchange(lambda x: a("HP", T.HP[:, 2 * x + q:16:4, 0:14]), pm, lambda y: four("TR", h, 16 * y, 16 * y + 14)) for q, pm in enumerate(("PMa", "PMb"))], []))
            act(half("RK", h, 224), a("HP", T.HP[:, 0:16, 0:14]), F.Copy)

    def look(i):
        t, h, n_ = i // 2, i % 2, [(1 if ON["rows"] == "s" else 32) + (NB > 0) + 4 * 14 - NB]
        kp, w = c("KP", 0, 224), lambda x, j: a("RX", T.RX[:, j], j, j + 1) if x else half("RY", j, 8)
        mms([(kp, c("OB"), a("CK"), True, False), (kp, (T.ST[0:5, C128(t)], half("ST", t)[1]), (T.TB[0:5, 224 * h:224 * h + 224], half("TB", h, 224)[1]), False, False)])
        for l, r in [(Ib, half("RK", h, 224))][ON["rows"] != "s":] + [(zz(i), a("MZ"))][NB == 0:]:
            mms([(kp, l, r, False, n_)], True)
        for j in range(4 * (ON["rows"] != "s")):
            mms(sum([exchange(lambda x: c("KP", 56 * j + 28 * x + 14 * q, 56 * j + 28 * x + 14 * q + 14), pm,
                              lambda y: a("TR", T.TR[:, 4 * h + j, 16 * y:16 * y + 14], h, h + 1), (False, n_)) for q, pm in enumerate(("PMa", "PMb"))], []), True)
        if NB < 14:
            mms([(half("S1", k), Ib, zz(i), True, True) for k in range(4)])
        mms([(c("S2"), c("OB"), c("C3"), True, False)] + [(half("S2", k), Ib, zz(i), False, k == 3) for k in range(4)])
        for j, (x, s, n, q) in enumerate(CH):
            q = "v" if j in MORE.get(i, ()) else q
            raw, top = rec(h, x, s, n), c("MX", 3584 * h + 128 * (s + 14 * x), 3584 * h + 128 * (s + n + 14 * x))
            one = lambda b, k: c(b, 3584 * h + 128 * (k + 14 * x), 3584 * h + 128 * (k + 1 + 14 * x))
            if q == "v":
                ts(raw, ind(XW(h), offs(h, 1 - x, s, n)), 384 * x - 192, None, A.add)
            else:
                act(raw, ind(XW(h), offs(h, 1 - x, s, n)), F.Copy, bias=384.0 * x - 192)
            if q == "b":
                b = "S%d" % (s // 4 % 2 if NB == 14 else 0)
                mms([(c(b, 0, 128 * n), Ib, raw, True, False)] + [(half(b, k), nI, zz(i), False, k == n - 1) for k in range(n)])
                act(top, c(b, 0, 128 * n), F.Abs)
                mms([(KP(k, x), one("MX", k), w(x, 2), False, n_) for k in range(s, s + n)], True)
            else:
                mms([(KP(k, x), one("WW", k), w(x, 0), False, n_) for k in range(s, s + n)], True)
                tt(top, raw, c("S1" if x else "S2", 0, 128 * n), A.max)
                mms([(KP(k, x), one("MX", k), w(x, 1), False, n_) for k in range(s, s + n)], True)

    def choose(i):
        h = i % 2
        sc, sm = half("SC", h, 224), lambda b: half(b, h, 8)
        op("v", lambda e: e.tensor_tensor_scan(sc[0], T.D0[:, :], T.KP[:, 0:224], 0.0, A.mult, A.max), sc, a("D0"), a("KP"), dur=FV + CY * 224)
        w = c("SC", 224 * h + 27, 224 * h + 224, 28)
        ts(sm("FF"), w, BIG, 1 / BIG, A.is_lt, A.max)
        tt(sm("SE"), w, sm("FF"), A.mult)
        ts(half("KQ", h, 8), sm("SE"), 31, None, A.bitwise_and)
        cp(half("KL", i, 8), half("KQ", h, 8))
        if not last(i):
            send(i, 2)
        tt(half("GM", h), ind(half("KQ", h, 8), c("RL")), c("M1"), A.mult)
        mms(group(a("T1", T.T1[:, 0, :]), (Ib, c("JC", 0, 16)), (half("GM", h), c("IN2"))))
        cp(half("LS", h, 8), a("T1", T.T1[:, 0, 0:8]))

    def count(i):
        t, h = i // 2, i % 2
        p, terms = a("T1", T.T1[:, 1, 0:1]), [(a("If"), c("NC", i, i + 1)), (c("OB"), c("JC", 16, 17)), (c("BO2"), c("ES", h, h + 1))]
        mms(group(p, *terms))
        act(c("AI", i, i + 1), p, F.Copy, bias=-63 / 128 - KAP / 64, scale=1 / 64)
        ts(c("NC", i + 2, i + 3), c("AI", i, i + 1), -64, p, A.mult, A.add)
        if last(i):
            ye, at = c("YE", 8 * h, 8 * h + 5), c("AT", 8 * h, 8 * h + 5)
            ts(at, c("AI", h, 10, 2), -129, 64, A.add, A.mult)
            tt(ye, c("NC", h + 2, 12, 2), c("NC", h, 10, 2), A.subtract)
            tt(ye, ye, at, A.add)
            dmas("sy", [(T.ye[P64(h), :], T.YE[0:64, 8 * h:8 * h + 5])], [ye[1]], [], "out", 20)

    def table(i):
        h = i % 2
        zn, p, u = half("ZS", i), a("T2", T.T2[:, 0:8, :]), a("T2", T.T2[:, 8, 0:8])
        act(half("PK", h), ind(half("WW", h, 3584), half("LS", h, 8)), F.Copy)
        mms(group(ps("T2", 16), (nI, zz(i)), (Ib, half("PK", h))))
        act(half("AW", h), ps("T2", 16), F.Abs)
        mms(group(p, (c("OB"), c("CH")), (c("Ih"), zz(i)), (c("Ih"), half("PK", h))))
        lin(ON["a192"], half("A2", h), half("AW", h), 1.0, 192.0)
        tt(zn, p, half("A2", h), A.min)
        if not last(i):
            send(i, 1)
        sums = [(CS("Zb", k), c("ZS", 128 * i + k, 128 * i + 128, 16)) for k in range(16)]
        mms(group(a("T1", T.T1[:, 2, 0:8]), *sums))
        lin(ON["k8"], half("K8", h, 8), a("T1", T.T1[:, 2, 0:8]), 1 / 8, -255.4375)
        lin(ON["u"], half("UU", h, 8), a("T1", T.T1[:, 2, 0:8]), 1.0, 0.0)
        jk, es = half("JK", h, 8), c("ES", h, h + 1)
        add("s", [lambda e: e.activation(jk[0], T.T1[:, 0, 8:16], F.Sign, accum_out=es[0])], [("T1", 0, 1)], [jk[1], es[1]], FS + 75.0)
        if BOTH and not last(i):
            dup = lambda b, k: a(b, T[b][:, k], k, k + 1)
            u, val, lc = a("T2", T.T2[:, 8:25, 0]), ps("T2", 8, 17), c("LC", 18 * h, 18 * h + 17)
            parts = ((1, 0, 8), (0, 8, 8), (1, 16, 1))
            mms([(u, Ib, c("J8", 8, 25), True, False), (a("T2", T.T2[:, 24:25, 0]), c("OB"), c("JC", 17, 18), False, False)] + [(a("T2", T.T2[:, 8 + o:8 + o + n, 0]), dup(b, k), c(x, 8 * h, 8 * h + n), False, o == 16 and b == "D8")
                                                         for k, o, n in parts for b, x in (("Df", "UU"), ("D8", "K8"))])
            ts(lc, u, -2040, None, A.add)
            act(half("XO", h, 272), ind(XW(h), lc), F.Copy)
            mms([(val, Ib, half("XO", h, 272), True, False)] + [(ps("T2", 8 + o, n), dup("Db", k), c("ZS", 128 * i, 128 * i + 16 * n), False, o == 16) for k, o, n in parts])
            lin(ON["avg"], half("HX", h, 272), val, 0.5, 32 - 0.1875)
            tt(ind(XW(h), lc), half("HX", h, 272), c("N128"), A.add)
            return
        mms(group(u, (Ib, c("J8", 0, 8)), (c("I8"), half("K8", h, 8)), (a("If"), half("UU", h, 8))))
        xw, lc, hx = c("X", XN * h, XN * h + 2048), c("LC", 18 * h, 18 * h + 8), c("HX", 272 * h, 272 * h + 128)
        ts(lc, u, -2040, None, A.add)
        tt(half("SX", h), ind(xw, lc), zn, A.add)
        lin(ON["avg"], hx, half("SX", h), 0.5, 32 - 0.1875)
        tt(ind(xw, lc), hx, c("N128", 0, 128), A.add)
        if last(i):
            for k in range(2):
                dmas(("s", "sy")[k], [(T.yx[P64(h), 1024 * k:1024 * k + 1024], xs(h, k, 1024 - 1024 * k, 1024))], [xw[1]], [], "out", 2048)
            ts(half("ZO", h), zn, -192, None, A.add)
            dmas("sy", [(T.yz[P64(h), C128(k)], T.ZO[P64(k), C128(h)]) for k in range(2)], [half("ZO", h)[1]], [], "out", 256)
        else:
            dmas("sy", [(xs(h, 1 - k, 1024 - 1024 * k, 1024), xs(h, k, 1024 - 1024 * k, 1024)) for k in range(2)] + [(xs(h, k, 2048, 64), xs(h, 1, 0, 64)) for k in range(2)],
                 [], [XW(h)[1]], "tw%d" % h, 1088)

    def state(i):
        h = i % 2
        old, lst = ((rows("L", i),), half("KL", i, 8)) if last(i) else ((names("O", i), rows("O", i)), half("LR", i, 8))
        mms(sum([group(a("SP", T.SP[:, 8 * q:8 * q + 8, :]), *[(half("D12", q), x) for x in old]) for q in range(2)], []))
        act(half("DL", h, 256), a("SP", T.SP[:, 0:16, :]), F.Copy)
        mms(group(code, *[(Ib, x) for x in old], done=False))
        for q in range(2):
            tt(half("TT", 2 * h + q), ind(half("OH", q, 32), lst), half("DL", 2 * h + q), A.mult)
            mms(group(code, (half("A12", q), half("TT", 2 * h + q)), more=True, done=q == 1))
        if last(i):
            act(half("RF", h), code, F.Copy)
        else:
            split(i + 2)

    def finish(h):
        r, y = half("RF", h), (T.YF[0:8, C128(h)], half("YF", h)[1])
        mms(group(ps("HP", 0), (half("WP", 0), r), (half("WP", 1), r)))
        ts(half("W1", h), ps("HP", 0), 127.5, None, A.add)
        mms([(a("SP", T.SP[0:8, 0:8, k]), c("RF", 128 * h + k, 128 * h + 128, 16), c("Ib", 14, 128, 16), True, True) for k in range(16)])
        act(y, a("SP", T.SP[0:8, 0:8, :]), F.Copy, scale=-16.0, bias=7.5)
        dmas("sy", [(T.yf[4 * h:4 * h + 4, C128(k)], T.YF[4 * k:4 * k + 4, C128(h)]) for k in range(2)], [y[1]], [], "out", 512)
        cuts(half("W1", h), "R1", h, 16, lambda s: s % 3 != 2)
        standing_sums("HP", half("W1", h), "R1", h, "MVb", c("CF"))
        turn(four("OC", h), ps("HP", 0))
        mms(exchange(lambda x: a("HP", T.HP[:, 16 + x:24:2, :]), "PMf", lambda y: four("OC", h, 16 * y, 16 * y + 16)))
        act(half("YP", h), ps("HP", 16), F.Copy, scale=1 / 4096)
        dmas("sy", [(T.yp[P64(h), C128(k)], T.YP[P64(k), C128(h)]) for k in range(2)], [half("YP", h)[1]], [], "out", 512)

    loads()
    consts()
    slots()
    for h in range(2):
        stream[0] = h
        first(h)
    for h in range(2):
        stream[0] = h
        columns(h)
    thresholds()
    ahead = lambda i: send(i, 0)
    for i in range(2 * TS):
        stream[0] = i % 2
        for name, f in [("ahead", ahead)][last(i):] + [("look", look), ("choose", choose), ("table", table), ("count", count), ("state", state),
                                                       ("next", (lambda i: finish(i % 2)) if last(i) else (lambda i: columns(i + 2)))]:
            part[:] = [name + ("'" if last(i) and name in ("state", "next") else ""), i, 0]
            f(i)

    if not ORDER:
        end, at = arrange(nodes, edges)
        ORDER.update({"end": end, "at": at})
    needed = {p for x in nodes for p in x["wait"]}
    cnt, know, seen = {}, {q: {} for q in Q}, {}
    for k in sorted(range(len(nodes)), key=lambda k: (ORDER["at"][k], k)):
        x = nodes[k]
        q, s = x["q"], x["s"]
        if q == "e":
            seen[k] = seen[k - 1]
            continue
        for p in sorted(x["wait"], key=lambda p: -ORDER["at"][p]):
            ps, pn, snap = seen[p]
            if know[q].get(ps, 0) < pn:
                Q[q].wait_ge(sem[ps], pn)
                for y, n in list(snap.items()) + [(ps, pn)]:
                    know[q][y] = max(know[q].get(y, 0), n)
        calls = [fn(Q[q]) for fn in x["fns"]]
        if x["inc"] < 0:
            cnt[s] = -x["inc"]
            seen[k] = (s, cnt[s], {})
            continue
        for call in (calls if x["inc"] == 16 else calls[-1:] if k in needed else []):
            call.then_inc(sem[s], x["inc"])
            cnt[s] = cnt.get(s, 0) + x["inc"]
        seen[k] = (s, cnt.get(s, 0), dict(know[q]))
    for s in cnt:
        g.wait_ge(sem[s], cnt[s])
    g.wait_ge(sem.sent, sent[0])
